import numpy as np, ml_dtypes
CORES = [40,64,80,88,96,104,120,144]
N = 8
BF = ml_dtypes.bfloat16
def gentries(a):
    return np.ascontiguousarray(a.reshape(8, 16, -1).transpose(0, 2, 1)).reshape(8, -1)
def gtable(e):
    e = np.asarray(e); return np.ascontiguousarray(e.reshape(8, -1, 16).transpose(0, 2, 1)).reshape(128, -1).astype(np.int32)
A, H, S, ST, RO, R = 1024, 2048, 256, 5, 2, 10
def atoms(rng, reach):
    off = np.concatenate([np.arange(-reach, 0), np.arange(1, reach + 1)])
    ch = off[np.argsort(rng.random((8, A, 2 * reach)), axis=-1)[..., :16]]
    ch = ch * (rng.random((8, A, 1)) >= 0.03125)
    pos = (np.arange(A)[None, :, None] + ch) % A
    nb = np.zeros((8, 16, A), np.int64)
    for g in range(8):
        o = rng.permutation(A); nb[g][:, o] = o[pos[g]].T
    return nb
def parts(rng, reach=R):
    nb = atoms(rng, reach); e = rng.integers(0, 256, (N, 8, 16, H)); s0 = rng.integers(0, A, (N, 8, RO, S))
    return nb, e, s0, rng.integers(0, 256, (N, 8, 16, S)), rng.integers(70 * ST, 210 * ST, (N, 8, 16))
def layers(rng):
    m = (A - 1) // (2 * ST - 1); lay = rng.permutation(A - 1)[:m * (2 * ST - 1)].reshape(2 * ST - 1, m); nb = rng.integers(0, A, (16, A))
    nb[:8, lay[0]] = rng.choice(lay[1], (8, m)); nb[8:, lay[0]] = rng.choice(lay[ST], (8, m))
    for i in range(1, 2 * ST - 1):
        nb[:, lay[i]] = A - 1 if i in (ST - 1, 2 * ST - 2) else rng.choice(lay[i + 1], (16, m))
    return nb, lay[0]
def owned(rng):
    n = 2 * ST; free = np.ones(A, bool); taken = np.zeros(H, bool); c = np.zeros((S, n), np.int64)
    for j in range(S):
        for m in range(n):
            x = rng.permutation(np.flatnonzero(free)); hs = []
            if m >= 2: hs.append(place(c[j, m - 2], c[j, m - 1], x))
            if m == n - 1: hs += [place(c[j, m - 1], x, c[j, 0]), place(x, c[j, 0], c[j, 1])]
            good = np.ones(x.shape, bool)
            for a in range(len(hs)):
                good &= ~taken[hs[a]]
                for b in range(a): good &= hs[a] != hs[b]
            i = int(np.argmax(good)); c[j, m] = x[i]; free[x[i]] = False
            for h in hs: taken[h[i]] = True
    nb = rng.integers(0, A, (16, A)); nb[:8, c[:, 0]] = c[:, 1]; nb[8:, c[:, 0]] = c[:, n - 1]
    for m in range(1, ST):
        nb[:, c[:, m]] = c[:, m + 1]; nb[:, c[:, n - m]] = c[:, n - m - 1]
    return nb, c[:, 0]
def pack(nb, e, s0, q, th):
    return {"nb": np.repeat(nb.reshape(1, 128, A), N, axis=0).astype(np.int32), "ang": e.reshape(N, 128, H).astype(np.float32).astype(BF),
            "st": np.stack([gtable(a.reshape(8, -1)) for a in s0]), "q": q.reshape(N, 128, S).astype(np.float32).astype(BF), "th": th.reshape(N, 128, 1).astype(np.int32)}
def setup_inputs(rng):
    return pack(*parts(rng))
def setup_inputs_ties(rng):
    nb, e, s0, q, th = parts(rng); v = np.arange(A)[None, :]
    nb[0] = 8 * (v >> 3) + rng.integers(0, 8, (16, A)); e[:, 0] = rng.choice(np.array([0, 192, 255, 255, 255]), (N, 1, H)); q[:, 0] = 0
    e[:, 1] = 10 * rng.integers(0, 2, (N, 16, H)); q[:, 1] = 10 * rng.integers(0, 2, (N, 16, S)); th[:, 1] = 10 * rng.integers(1, ST + 1, (N, 16))
    e[:, 2] = rng.choice(np.array([0, 3, 4, 255]), (N, 1, H)); q[:, 2] = 4; th[:, 2] = rng.integers(255, 520, (N, 1))
    e[:, 3] = 7; q[:, 3] = rng.integers(0, 256, (N, 16, S)); th[:, 3] = 7 * rng.integers(3, 2 * ST, (N, 16))
    e[:, 4] = rng.choice(np.array([100, 156]), (N, 16, H)); q[:, 4] = 128
    e[:, 5] = e[:, 5] * rng.integers(0, 2, (N, 16, H))
    for r in range(N):
        for g, n in ((5, 9), (6, 8), (7, 16)): th[r, g] = np.where(rng.permutation(16) < n, 0, 4095)
    return pack(nb, e, s0, q, th)
def setup_inputs_repeats(rng):
    nb, e, s0, q, th = parts(rng, 8)
    s0[:, ::2] = rng.choice(np.array([0, A - 1, A // 2, 5]), (N, 4, RO, S))
    e[:, 1::2] = e[:1, 1::2].copy(); q[:, 2::4] = q[:, 2::4, :, :1].copy()
    return pack(nb, e, s0, q, th >> 1)
def setup_inputs_stuck(rng):
    nb, e, s0, q, th = parts(rng); v = np.arange(A)[None, :]; k = np.arange(16)[:, None]
    nb[0] = 4 * (v >> 2) + rng.integers(0, 4, (16, A))
    nb[1, :8] = v; nb[2, 8:] = v
    nb[3] = v ^ rng.integers(0, 2, (16, A)); nb[3, ::8] = v ^ 1; nb[4] = v
    nb[5] = nb[5][rng.integers(0, 4, (16, A)), np.repeat(v, 16, axis=0)]
    nb[6] = 8 * (v >> 3) + rng.integers(0, 8, (16, A))
    x = v & 127; nb[7] = np.where(x == 0, v + 16 + k, np.where((x < 16) | (x >= 16 * (ST - 2)), v - x, v + 16))
    for g in (0, 3, 4, 6): th[:, g] = rng.integers(0, 800, (N, 16))
    s0[:, :, :, 0] = 0; s0[:, :, :, S - 1] = A - 1
    s0[:, 7] = 128 * rng.integers(0, A >> 7, (N, RO, S)) + rng.integers(1, 16, (N, RO, S))
    s0[0, 3] = rng.integers(256, A, (RO, 1)); th[0, 3] = 0
    return pack(nb, e, s0, q, th)
def setup_inputs_far(rng):
    nb, e, s0, q, th = parts(rng)
    for g in range(8):
        nb[g], a = layers(rng); s0[:, g] = rng.choice(a, (N, RO, S))
    if 2 * ST * S <= A:
        nb[1], a = owned(rng); s0[:, 1] = a[np.argsort(rng.random((N, RO, S)), axis=-1)]
    th = rng.integers(200 * ST, 300 * ST, (N, 8, 16)); th[2:, 5] = 4095; th[2:, 6] = 0; th[:2] = 0
    e[:, 2] = rng.integers(224, 256, (N, 16, H)); th[:, 2] = rng.integers(min(2048, 448 * ST), 448 * ST + 1, (N, 16))
    e[:, 3] = 255; th[:, 3] = 510 * ST; th[2:, 3, :8] = 510 * ST + 1
    return pack(nb, e, s0, q, th)
def setup_inputs_spread(rng):
    nb, e, s0, q, th = parts(rng); v = np.arange(A)[None, :]; k = np.arange(16)[:, None]
    e = (np.exp2(8 * rng.random((N, 8, 1, H))) * rng.random((N, 8, 16, H))).astype(np.int64)
    q = (np.exp2(8 * rng.random((N, 8, 1, S))) * rng.random((N, 8, 16, S))).astype(np.int64)
    th = np.minimum(np.exp2(12 * rng.random((N, 8, 16))).astype(np.int64), 4095)
    s0 = np.minimum((A * rng.random((N, 8, RO, S)) ** 3).astype(np.int64), A - 1)
    c = v & 3; nb[0] = 4 * rng.integers(0, A >> 2, (16, A)) + np.where(c >= 2, c, np.where(k < 8, 2, 3))
    s0[:, 0] = 4 * (s0[:, 0] >> 2) + rng.integers(0, 2, (N, RO, S))
    nb[2:4] = rng.integers(0, A, (2, 16, A))
    return pack(nb, e, s0, q, th)
def check_inputs(d):
    bad = []
    for k, lo, hi in (("nb", 0, A - 1), ("ang", 0, 255), ("st", 0, A - 1), ("q", 0, 255), ("th", 0, 4095)):
        v = np.asarray(d[k]).astype(np.float64)
        if not np.all((v >= lo) & (v <= hi)): bad.append("range of " + k)
        elif not np.all(v == np.floor(v)): bad.append(k + " holds numbers that aren't whole")
    if np.any(d["nb"] != d["nb"][:1]): bad.append("nb isn't alike on all ranks")
    return bad
def place(p, v, n):
    return ((((2 * p + 1) * (2 * n + 1)) >> 4) + 37 * v) & (H - 1)
def walk(e, v0, w, rows, nbr):
    path = [v0]; kk = np.arange(16)[None, :, None]
    for i in range(ST):
        v = path[i]; p = path[max(i - 1, 0)]
        n = np.take_along_axis(nbr, v[:, None, :], 2)
        h = place(p[:, None, :], v[:, None, :], n)
        x = np.take_along_axis(e, h.reshape(8, 1, 16 * S), 2).reshape(8, 16, 16, S)
        sc = np.add.reduce(np.abs(x - w[:, :, None, :]), axis=1)
        bar = np.any(np.stack(path)[:, :, None, :] == n[None], axis=0)
        if i == 0: bar = bar | (kk < rows) | (kk >= rows + 8)
        sc = np.where(bar, 2 ** 20, sc); k = np.argmin(sc, axis=1)[:, None, :]
        ok = np.take_along_axis(sc, k, 1)[:, 0] < 2 ** 20
        path.append(np.where(ok, np.take_along_axis(n, k, 1)[:, 0], v))
    return np.stack(path)
def reference(nb, ang, st, q, th):
    e = np.asarray(ang, np.float32).astype(np.int32).reshape(N, 8, 16, H); w = np.asarray(q, np.float32).astype(np.int32).reshape(N, 8, 16, S)
    lim = th.astype(np.int64).reshape(N, 8, 16, 1); nbr = nb.astype(np.int64).reshape(N, 8, 16, A)
    sl = np.stack([gentries(a) for a in st]).astype(np.int64).reshape(N, 8, RO, S)
    rings = np.zeros((N, 8, 16, RO, S), np.int64); m = np.arange(16)[None, :, None]
    for t in range(RO):
        new = []
        for r in range(N):
            s = (r + 1 + t % (N - 1)) % N
            pa = walk(e[r], sl[r, :, t], w[r], 0, nbr[r]); pb = walk(e[s], sl[r, :, t], w[r], 8, nbr[s])
            eq = pa[1:, None] == pb[None, 1:]; eq[0, 0] = False
            eq = eq.reshape(ST * ST, 8, S); found = np.any(eq, axis=0); f = np.argmax(eq, axis=0)
            i = f // ST + 1; j = f - (i - 1) * ST + 1; ln = np.where(found, i + j, 0)[:, None, :]; i = i[:, None, :]
            ca = np.take_along_axis(pa.transpose(1, 0, 2), np.minimum(m, i), 1); cb = np.take_along_axis(pb.transpose(1, 0, 2), np.clip(ln - m, 0, ST), 1)
            c = np.where(m <= i, ca, cb); live = m < ln
            before = np.take_along_axis(c, np.clip(np.where(m == 0, ln - 1, m - 1), 0, 15), 1)
            after = np.take_along_axis(c, np.clip(np.where(m == ln - 1, 0, m + 1), 0, 15), 1)
            h = place(before, c, after)
            x = np.take_along_axis(e[r], h.reshape(8, 1, 16 * S), 2).reshape(8, 16, 16, S)
            tot = np.add.reduce(np.where(live[:, None], x, 0), axis=2)
            heavy = found & (np.add.reduce((tot >= lim[r]).astype(np.int64), axis=1) >= 9)
            use = live & heavy[:, None, :]; gg = np.broadcast_to(np.arange(8)[:, None, None], h.shape)
            mark = np.zeros((8, H), bool); mark[gg[use], h[use]] = True
            new.append(np.where(mark[:, None, :], e[r] - (e[r] >> 2), e[r])); rings[r, :, :, t] = np.where(live, c, -1)
        e = np.stack(new)
    return {"ye": e.reshape(N, 128, H).astype(np.float32).astype(BF), "yr": rings.reshape(N, 128, RO * S).astype(np.float32)}

@@ -1,0 +1,786 @@
+from concourse.mybir import dt, AluOpType, ActivationFunctionType
+import comms_topo
+
+OP = AluOpType
+FN = ActivationFunctionType
+BIG = float(2 ** 26)
+REST = float(2041 * 8192)
+F32, B16, H16, I32 = "float32", "bfloat16", "float16", "int32"
+SCRATCH = {}
+for _n, _p, _w, _t in (
+        ("NB", 128, 1024, I32), ("XI", 128, 1024, I32), ("TO", 128, 2064, B16), ("TO1", 128, 2064, B16), ("TO2", 128, 2048, B16),
+        ("TP0", 128, 2048, B16), ("TPn", 128, 2048, B16), ("TP1", 128, 2048, B16), ("EL0", 128, 2048, B16), ("ELn", 128, 2048, B16),
+        ("EL1", 128, 2048, B16), ("TMP", 128, 2048, H16), ("ST", 128, 32, I32), ("SU", 128, 32, "uint16"), ("TH", 128, 1, I32),
+        ("THF", 128, 1, F32), ("Q", 128, 256, B16), ("QR", 128, 4096, B16), ("ON", 128, 2048, B16), ("CB", 128, 2384, B16),
+        ("CT", 128, 464, B16), ("CH", 128, 2512, H16), ("C2", 128, 512, H16), ("CF", 9, 1024, B16), ("CW", 9, 1408, H16),
+        ("VS", 8, 2048, B16), ("VH", 8, 2048, H16), ("SELL", 128, 2048, B16), ("CBIG", 128, 256, B16), ("S8", 128, 8, B16),
+        ("NEGI", 128, 128, B16), ("CR", 33, 512, B16), ("I128", 128, 128, B16), ("RT", 97, 1280, B16), ("MT0", 128, 128, B16),
+        ("WT", 128, 384, B16), ("NT", 9, 3072, H16), ("X0B", 128, 256, H16), ("PT0", 128, 176, H16), ("PT1", 128, 176, H16),
+        ("NPK0", 128, 128, F32), ("NPK1", 128, 128, F32), ("U", 128, 176, F32), ("PR", 128, 144, F32), ("V5", 128, 144, F32),
+        ("TT", 128, 160, I32), ("HH", 128, 160, I32), ("EQ", 128, 384, B16), ("EW", 128, 384, B16), ("E1", 128, 192, B16),
+        ("E2", 128, 96, B16), ("E3", 128, 64, B16), ("JS", 128, 128, F32), ("JR", 128, 16, I32), ("IL", 128, 32, H16),
+        ("VV", 128, 176, F32), ("MI", 128, 160, F32), ("JP", 128, 240, H16), ("UJ", 128, 48, F32), ("WW", 128, 160, I32),
+        ("TB", 128, 160, I32), ("TBP", 128, 160, F32), ("TV", 128, 160, H16), ("TVL", 80, 256, B16), ("HS", 128, 160, F32),
+        ("HV", 128, 160, H16), ("WS", 128, 320, F32), ("HT", 80, 256, H16), ("OFR", 128, 256, "uint16"), ("XR", 128, 2560, B16),
+        ("CMP", 128, 256, B16), ("HVY", 80, 256, B16), ("TM", 97, 256, B16), ("OH", 128, 20480, B16), ("TL", 128, 2560, B16),
+        ("CS", 128, 132, F32), ("DD", 128, 128, F32), ("MK", 128, 128, B16), ("MKT", 128, 128, B16), ("MKP", 128, 128, B16),
+        ("YN", 128, 256, H16), ("YM", 128, 256, H16), ("YP", 128, 256, H16), ("YK", 128, 1024, H16), ("YB", 128, 1536, H16),
+        ("YR", 128, 512, F32)):
+    SCRATCH[_n] = ("sbuf", [_p, _w], _t)
+for _c in "01":
+    for _n, _w, _t in (("NN", 256, H16), ("M", 256, F32), ("T", 256, I32), ("B", 256, I32), ("OF", 256, "uint16"), ("DV", 2560, B16),
+                       ("AB", 4096, B16), ("XG", 2048, B16), ("BQ", 1280, B16), ("SB", 128, F32), ("L1", 128, F32), ("L2", 64, F32),
+                       ("K", 32, I32), ("KD", 64, F32), ("SH", 32, I32), ("R", 32, I32), ("VL", 16, "uint16")):
+        SCRATCH[_n + _c] = ("sbuf", [128, _w], _t)
+BANKS = ("kA", "kB", "wA", "wB", "xA", "xB", "dA", "dB")
+for _b in BANKS:
+    SCRATCH[_b] = ("psum", [128, 512], F32)
+NITEM = 7
+NDMA = 14
+SEMAPHORES = ["v", "s", "t", "gc", "aTP0", "aTPn", "aMK"] + ["d%d" % i for i in range(NDMA)]
+SEMAPHORES += ["ri%d" % i for i in range(NITEM)] + ["lo%d" % i for i in range(NITEM)]
+
+CY = 0.00104
+TCY = 0.00075
+LEAD = 6.0
+SHOT = (1, 2, 3, 4)
+HINT = {"vM1": -2.0, "vOF0": -5.0, "vBQ1": 1.0, "vNN0": -0.5, "t#kA": -0.5, "t#xB": 0.5, "sab0": -28.5, "vCSz": 13.0, "vYP": -8.0,
+        "vOH": -7.0, "vhF": -20.0, "vWWe": -3.5, "vVL0": -2.5, "vMJ": -2.5, "vTVb": -2.0, "sXG0": -8.5, "vwP": -4.0, "sXG1": -0.5,
+        "vMK": 7.0, "vcPa": 2.0, "vSH1": 16.0, "vWSb": -5.0, "vcE": 10.5, "vhPS": -6.0, "vD20": 1.0, "vPTu": -4.0, "vWWa": 1.5,
+        "vNT": 1.5, "t#dA": 0.5, "vTHF": -0.5, "vJR": 1.0, "vJP": -2.0, "vTMz": 8.5, "vR1": 5.0, "vDD": 0.5}
+ORDERS = {}
+
+
+def items(x, T, topo):
+    me = T.cores[x]
+    n = len(T.cores)
+
+    def via(dst, other):
+        if not other and topo.may_write(me, dst):
+            return None
+        for c in topo.cores_of(me):
+            if c != me and topo.may_write(c, dst) and (topo.die(c) != topo.die(me)) == bool(other):
+                return c
+        for c in topo.cores_of(me):
+            if c != me and topo.may_write(c, dst):
+                return c
+        return None
+    out = []
+    d0, d1 = T.cores[(x - 1) % n], T.cores[(x - 2) % n]
+    for h, c0 in ((0, 0), (1, 1024), (0, 512), (1, 1536)):
+        out.append(("TO", c0, c0 + 512, "TP0", "aTP0", d0, via(d0, h)))
+    for h in (0, 1):
+        out.append(("TO", h * 1024, h * 1024 + 1024, "TPn", "aTPn", d1, via(d1, h)))
+    out.append(("MKT", 0, 128, "MKP", "aMK", d1, via(d1, 0)))
+    return out
+
+
+def remote(g, T, topo, core, dst, out, src, rsem, lsem):
+    rid, pid = topo.addr(dst, core)
+    g.remote_dma(out, src, T.sem[rsem], T.sem[lsem], pid, rid, topo.mask(core, dst))
+
+
+def hand_on(g, core, T, topo):
+    todo = []
+    for x in range(len(T.cores)):
+        for k, it in enumerate(items(x, T, topo)):
+            if it[6] == core:
+                todo.append((k, it, len(topo.engines(T.cores[x], core))))
+    for k, it, ne in todo:
+        g.wait_ge(T.sem["ri%d" % k], ne)
+        ap = T[it[3]][:, it[1]:it[2]]
+        remote(g, T, topo, core, it[5], ap, ap, it[4], "lo%d" % k)
+    for k, it, ne in todo:
+        g.wait_ge(T.sem["lo%d" % k], len(topo.engines(core, it[5])))
+
+
+def build(g, core, T, topo):
+    ops = []
+    lastw, reads, bank = {}, {}, {}
+    bon = [0.0]
+
+    def hint(q, W):
+        if not W or q is None:
+            return 0.0
+        w = W[0].split(".")[0]
+        for name in (w, w[:3], "".join(c for c in w if not c.isdigit())):
+            if q + name in HINT:
+                return HINT[q + name]
+        return 0.0
+
+    def op(q, fn, R, W, cost, kind="c", sem=None, val=1, lat=0.0):
+        n = len(ops)
+        deps, order = set(), set()
+        for k in list(R) + list(W):
+            if k[0] == "#":
+                b = bank.setdefault(k, {})
+                for e in b:
+                    if e == q:
+                        order.add(b[e][-1])
+                    elif e != "last":
+                        deps.update(b[e])
+                b[q] = b[q] + [n] if b.get("last") == [q] else [n]
+                b["last"] = [q]
+        for k in R:
+            if k[0] != "#":
+                if k in lastw:
+                    deps.add(lastw[k])
+                reads.setdefault(k, []).append(n)
+        for k in W:
+            if k[0] != "#":
+                if k in lastw:
+                    deps.add(lastw[k])
+                deps.update(reads.get(k, []))
+                lastw[k] = n
+                reads[k] = []
+        deps.discard(n)
+        order.discard(n)
+        ops.append(dict(q=q, fn=fn, deps=deps, order=(order - deps if q == "t" else set()), cost=cost, lat=lat, kind=kind, sem=sem, val=val, bon=bon[0] + hint(q, W)))
+
+    def V(fn, R, W, n):
+        op("v", lambda: fn(g.vector), R, W, max(64, n) * CY + 0.03)
+
+    def TS(out, a, s1, o0, R, W, n, s2=None, o1=None):
+        if o1 is None:
+            V(lambda e: e.tensor_scalar(out, a, s1, None, o0), R, W, n)
+        else:
+            V(lambda e: e.tensor_scalar(out, a, s1, s2, o0, o1), R, W, n)
+
+    def TTo(out, a, b, o, R, W, n):
+        V(lambda e: e.tensor_tensor(out, a, b, o), R, W, n)
+
+    def CP(out, a, R, W, n):
+        V(lambda e: e.tensor_copy(out, a), R, W, n)
+
+    def fill(ap, c, R, W, n):
+        V(lambda e: e.memset(ap, c), R, W, n)
+
+    def S(out, a, f, R, W, n, **kw):
+        op("s", lambda: g.scalar.activation(out, a, f, **kw), R, W, max(64, n) * CY + 0.05)
+
+    def MM(out, l, r, st, sp, R, W, m, n):
+        op("t", lambda: g.tensor.matmul(out, l, r, st, sp), R, W, max(min(64, m), n) * TCY + 0.01)
+
+    def GC(fn, R, W, n):
+        op("g", fn, R, W, 0.18 + 2 * n * CY)
+
+    def iota(out, pat, base, R, W, n):
+        GC(lambda: g.iota(out, pat, base, 0, allow_small_or_imprecise_dtypes=True), R, W, n)
+
+    nd = [0]
+
+    def DMA(q, out, a, R, W):
+        s = "d%d" % nd[0]
+        nd[0] += 1
+        eng = g.sync if q == "y" else g.scalar
+        op(q, lambda: eng.dma_start(out, a), R, W, 0.06, "d", s, 16, 2.5)
+
+    PS = {b: T[b] for b in BANKS}
+
+    DMA("y", T.ST[:, :], T.st[:, :], [], ["ST"])
+    DMA("s", T.TO[:, 0:2048], T.ang[:, :], [], ["TO"])
+    DMA("y", T.NB[:, :], T.nb[:, :], [], ["NB"])
+    DMA("s", T.Q[:, :], T.q[:, :], [], ["Q"])
+    DMA("y", T.TH[:, :], T.th[:, :], [], ["TH"])
+
+    fill(T.ON[:, :], 1.0, [], ["ON"], 1024)
+    fill(T.TO[:, 2048:2064], 0.0, [], ["TOz"], 64)
+    fill(T.TO1[:, 2048:2064], 0.0, [], ["TO1z"], 64)
+
+    def aff(out, src, pat, cmp, fv, base, cm, R, W):
+        n = 1
+        for p in pat:
+            n *= p[1]
+        GC(lambda: g.affine_select(out, src, pat, cmp, fv, base, cm), R, W, n)
+
+    def eqs(b, c0, pat, base, key, rows=128, cm=1):
+        n = 1
+        for p in pat:
+            n *= p[1]
+        aff(b[0:rows, c0:c0 + n], T.ON[0:rows, 0:n], pat, OP.is_equal, 0.0, base, cm, ["ON"], [key])
+
+    GC(lambda: g.iota(T.XI[:, 0:256], [[1, 256]], 0, 0), [], ["XI0"], 256)
+    for z in range(1, 4):
+        TS(T.XI[:, z * 256:z * 256 + 256], T.XI[:, 0:256], float(z * 256), OP.add, ["XI0"], ["XI%d" % z], 256)
+    CB, CH, CF, CW, CT = T.CB, T.CH, T.CF, T.CW, T.CT
+    hi = [[0, 8], [1, 2], [0, 8]]
+    eqs(CB, 128, [[-1, 8], [-8, 2], [-16, 8]], 0, "cPM")
+    eqs(CB, 0, [[-1, 128]], 0, "cI")
+    iota(CT[:, 208:336], hi, 0, [], ["cHi"], 128)
+    eqs(CB, 256, [[-1, 8], [-16, 8]], 0, "cA1")
+    eqs(CB, 320, [[-1, 8], [-16, 8]], -8, "cB1")
+    eqs(CF, 384, [[-1, 8], [0, 16]], 0, "cE0", 9)
+    aff(CF[0:9, 0:128], CF[0:9, 384:512], [[0, 128]], OP.not_equal, 0.5, -8, 1, ["cE0"], ["cF0"])
+    for z, kz in ((0, "cF"), (384, "cE")):
+        TTo(CF[0:9, z + 256:z + 384], CF[0:9, z:z + 128], CT[0:9, 208:336], OP.mult, [kz + "0", "cHi"], [kz + "2"], 256)
+        TTo(CF[0:9, z + 128:z + 256], CF[0:9, z:z + 128], CF[0:9, z + 256:z + 384], OP.subtract, [kz + "0", kz + "2"], [kz + "1"], 256)
+    fill(T.CR[:, :], 0.0, [], ["CR"], 256)
+    fill(T.CR[0:1, :], -16711680.0, ["CR"], ["CR"], 256)
+    iota(T.CR[32:33, 0:256], [[0, 2], [1024, 8], [0, 16]], 0, ["CR"], ["CR"], 256)
+    for z in (256, 384):
+        iota(T.CR[32:33, z:z + 64], [[1024, 8], [0, 8]], 0, ["CR"], ["CR"], 64)
+    aff(CT[:, 0:128], T.ON[:, 0:128], [[-16, 8], [0, 16]], OP.is_ge, 0.0, 0, 1, ["ON"], ["cT0"])
+    aff(CB[:, 896:1024], CT[:, 0:128], [[16, 8], [0, 16]], OP.is_ge, 0.0, 15, -1, ["cT0"], ["cEB"])
+    eqs(T.VS, 0, [[1, 16], [-16, 8], [-1, 16]], 0, "VS", 8, 16)
+    iota(T.I128[:, :], [[1, 128]], -128, [], ["I128"], 128)
+    eqs(T.RT, 0, [[-1, 80], [0, 16]], 0, "RT", 97)
+    iota(T.RT[96:97, :], [[0, 80], [-1, 16]], -2, ["RT"], ["RT"], 1280)
+    iota(T.MT0[:, :], [[0, 8], [1, 16]], 0, [], ["MT0"], 128)
+    aff(CT[:, 128:208], T.ON[:, 0:80], [[0, 10], [-16, 8]], OP.is_ge, 0.0, 0, 1, ["ON"], ["cT1"])
+    aff(CB[:, 1024:1104], CT[:, 128:208], [[0, 10], [16, 8]], OP.is_ge, 0.0, 15, -1, ["cT1"], ["cRC"])
+    eqs(CB, 1104, [[-1, 8], [1000, 2], [-8, 8]], 0, "cPR", 80)
+    eqs(CB, 1232, [[-1, 8], [1000, 2], [-8, 8]], -1000, "cPS", 80)
+    for z in range(8):
+        eqs(CB, 1360 + z * 128, [[-1, 8], [1000, 8], [-8, 2]], -64 - 1000 * z, "cPT%d" % z, 80)
+    iota(CF[0:9, 768:896], [[0, 8], [-1, 16]], 0, [], ["cM0"], 128)
+    aff(CF[0:9, 896:1024], CF[0:9, 768:896], [[0, 128]], OP.is_equal, 0.0, -8, 1, ["cM0"], ["cM1"])
+    eqs(CT, 336, [[-1, 128]], -1, "cSF")
+    eqs(T.SELL, 0, [[-1, 16], [-16, 8], [0, 16]], 0, "SELL")
+
+    I16, IB = CH[:, 0:128], CB[:, 0:128]
+    CP(T.SU[:, :], T.ST[:, :], ["ST"], ["SU"], 64)
+    CP(CH[:, 128:256], CB[:, 128:256], ["cPM"], ["hPM"], 64)
+    CP(CH[:, 0:128], IB, ["cI"], ["hI"], 64)
+    fill(CB[:, 512:520], 0.0, [], ["cP1a"], 64)
+    fill(CB[:, 760:768], 0.0, [], ["cP2a"], 64)
+    TTo(CB[:, 768:896], IB, CT[:, 208:336], OP.mult, ["cI", "cHi"], ["cP3"], 256)
+    TTo(CB[:, 384:512], IB, CB[:, 768:896], OP.subtract, ["cI", "cP3"], ["cP0"], 256)
+    CP(CB[:, 520:640], CB[:, 384:504], ["cP0"], ["cP1"], 64)
+    CP(CB[:, 640:760], CB[:, 776:896], ["cP3"], ["cP2"], 64)
+    CP(CH[:, 384:896], CB[:, 384:896], ["cP0", "cP1", "cP1a", "cP2", "cP2a", "cP3"], ["hP4"], 256)
+    CP(CH[:, 256:384], CB[:, 256:384], ["cA1", "cB1"], ["hF1"], 64)
+    FK, EK = ["cF0", "cF1", "cF2"], ["cE0", "cE1", "cE2"]
+    TS(CW[:, 0:384], CF[:, 0:384], 4.0, OP.mult, FK, ["wP"], 192)
+    TS(CW[:, 384:768], CF[:, 0:384], 2.0, OP.mult, FK, ["wQ"], 192)
+    TS(CW[:, 768:1152], CF[:, 384:768], 592.0, OP.mult, EK, ["wV"], 192)
+    CP(CW[:, 1152:1280], CF[:, 384:512], EK, ["wE"], 64)
+    for a in (0, 1, 2, 3, 6, 7, 8, 10, 11):
+        CP(T.NT[:, a * 256:a * 256 + 256], T.ON[0:9, 0:256], ["ON"], ["NT%d" % a], 128)
+    TS(T.CBIG[:, :], CB[:, 128:384], BIG, OP.mult, ["cPM", "cA1", "cB1"], ["CBIG"], 128)
+    TS(T.S8[:, :], CB[:, 896:1024:16], 8192.0, OP.mult, ["cEB"], ["S8"], 64)
+    TS(T.NEGI[:, :], IB, -1.0, OP.mult, ["cI"], ["NEGI"], 64)
+    QE, QO = ["QR%d" % k for k in range(0, 16, 2)], ["QR%d" % k for k in range(1, 16, 2)]
+    for k in list(range(0, 16, 2)) + list(range(1, 16, 2)):
+        if k % 4 < 2:
+            CP(T.QR[:, k::16], T.Q[:, :], ["Q"], ["QR%d" % k], 128)
+        else:
+            S(T.QR[:, k::16], T.Q[:, :], FN.Copy, ["Q"], ["QR%d" % k], 256)
+    QA = QE + QO
+    CP(T.VH[:, :], T.VS[:, :], ["VS"], ["VH"], 1024)
+
+    def late_constants():
+        CP(CH[0:80, 1104:1232], CB[0:80, 1104:1232], ["cPR"], ["hPR"], 64)
+        CP(CH[0:80, 1360:2512], CB[0:80, 1232:2384], ["cPS"] + ["cPT%d" % z for z in range(8)], ["hPS"], 576)
+        TTo(CW[:, 1280:1408], CF[:, 384:512], CF[:, 896:1024], OP.add, EK + ["cM1"], ["wM"], 256)
+        TS(T.MT0[:, :], T.MT0[:, :], 1.0, OP.min, ["MT0"], ["MT0"], 64)
+        CP(T.THF[:, :], T.TH[:, :], ["TH"], ["THF"], 64)
+        fill(T.VV[:, 0:16], 0.0, [], ["VV0"], 64)
+        fill(T.VV[:, 160:176], 0.0, [], ["VV10"], 64)
+        TTo(CH[:, 1232:1360], IB, CT[:, 336:464], OP.subtract, ["cI", "cSF"], ["hDM"], 256)
+        fill(T.TM[:, :], 0.0, [], ["TMz"], 64)
+        fill(T.TM[96:97, :], 1.0, ["TMz"], ["TMz"], 64)
+        fill(T.CS[:, 128:132], 0.0, [], ["CSz"], 64)
+        fill(T.CS[:, 129:130], 100.0, ["CSz"], ["CSz"], 64)
+        x = 0
+        for L in range(3, 11):
+            for i in range(max(1, L - 5), min(5, L - 1) + 1):
+                fill(T.WT[:, x:x + 16], float(25 - (i - 1) * 5 - (L - i - 1)), [], ["WT%d" % x], 64)
+                x += 16
+
+    n = len(T.cores)
+    r = T.rank_of(core)
+    its = items(r, T, topo)
+
+    def send(k):
+        buf, c0, c1, land, asem, dst, rel = its[k]
+
+        def fn():
+            if rel is None:
+                remote(g, T, topo, core, dst, T[land][:, c0:c1], T[buf][:, c0:c1], asem, "lo%d" % k)
+            else:
+                remote(g, T, topo, core, rel, T[land][:, c0:c1], T[buf][:, c0:c1], "ri%d" % k, "lo%d" % k)
+        op("g", fn, [buf], [], 0.5, "r", "lo%d" % k, len(topo.engines(core, dst if rel is None else rel)))
+
+    def arrive(land, asem, giver, lat, after):
+        tot = 0
+        for it in items(giver, T, topo):
+            if it[4] == asem:
+                tot += len(topo.engines(T.cores[giver] if it[6] is None else it[6], core))
+        op(None, None, after, [land], 0.0, "x", asem, tot, lat)
+    for k in range(6):
+        send(k)
+    arrive("TP0", "aTP0", (r + 1) % n, 14.0, ["TO"])
+    arrive("TPn", "aTPn", (r + 2) % n, 25.0, ["TO"])
+
+    NB = T.NB[:, 0:1024]
+
+    def nt(c, a):
+        return 0 if a == 0 else (a if c == 0 else 5 + a)
+
+    def NTs(s, rows=9):
+        return T.NT[0:rows, s * 256:s * 256 + 256]
+
+    def start(t):
+        P = "PT%d" % t
+        vl = T.SU[:, t * 16:t * 16 + 16]
+        V(lambda e: e.tensor_copy(T.X0B[:, :], T.XI[:, 0:1024].indirect(vl)), ["XI0", "XI1", "XI2", "XI3", "SU"], ["X0B"], 384)
+        X = PS["xA"]
+        MM(X[0:8, 0:256], CH[:, 128:136], T.X0B[:, :], True, True, ["hPM", "X0B"], ["#xA"], 8, 256)
+        for b in (0, 1):
+            MM(X[:, 256 + b * 8:264 + b * 8], T.X0B[:, b * 128:b * 128 + 128], CH[:, 128:136], True, True, ["hPM", "X0B"], ["#xA"], 128, 8)
+        CP(T.NT[0:8, 0:256], X[0:8, 0:256], ["#xA"], ["NT0"], 256)
+        for b in (0, 1):
+            CP(T[P][:, 80 + b:96:2], X[:, 256 + b * 8:264 + b * 8], ["#xA"], [P + "s5"], 64)
+        V(lambda e: e.tensor_copy(T.NN0[:, :], NB.indirect(vl)), ["NB", "SU"], ["NN0"], 384)
+
+    def step(t, c, a, tab, tkey):
+        C = str(c)
+        P = "PT%d" % t
+        bon[0] = LEAD * (1 - c)
+        kb, wb, xb, db = ("kA", "wA", "xA", "dA") if c == 0 else ("kB", "wB", "xB", "dB")
+        K, W, X, D = PS[kb], PS[wb], PS[xb], PS[db]
+        KB, WB, XB, DB = "#" + kb, "#" + wb, "#" + xb, "#" + db
+        nn, nnk = (T.NN0, "NN0") if a == 0 else (T["NN" + C], "NN" + C)
+
+        def sl(i):
+            return 5 + i if c == 0 else 5 - i
+        if a == 0:
+            w = 128
+            p0 = 384 + 256 * c
+            MM(X[:, 0:128], CH[:, p0:p0 + 128], nn[:, 0::2], True, False, ["hP4", nnk], [XB], 128, 128)
+            MM(X[:, 0:128], CH[:, p0 + 128:p0 + 256], nn[:, 1::2], False, True, ["hP4", nnk], [XB], 128, 128)
+            E, O = T.NT[:, 0:256:2], T.NT[:, 1:256:2]
+            MM(W[:, 0:128], CW[:, 128:256], E, True, False, ["wP", "NT0"], [WB], 128, 128)
+            MM(W[:, 0:128], CW[:, 256:384], O, False, True, ["wP", "NT0"], [WB], 128, 128)
+            for z, (q0, src) in enumerate(((512, E), (640, O), (896, E), (1024, O))):
+                MM(W[:, 256:384], CW[:, q0:q0 + 128], src, z == 0, z == 3, ["wQ", "wV", "NT0"], [WB], 128, 128)
+            S(T["NPK" + C][:, :], X[:, 0:128], FN.Copy, [XB], ["NPK" + C], 128)
+            src, sk = T["NPK" + C][:, :], "NPK" + C
+            parts = ((1024, 512, "s"), (1536, 512, "s"), (0, 512, "v"), (512, 512, "v"))
+        else:
+            w = 256
+            V(lambda e: e.tensor_copy(nn[:, :], NB.indirect(T["VL" + C][:, 0:16])), ["NB", "VL" + C], [nnk], 384)
+            s0, s1 = nt(c, a - 1), nt(c, a)
+            MM(W[:, 0:256], CW[:, 0:128], NTs(s0), True, True, ["wP", "NT%d" % s0], [WB], 128, 256)
+            MM(W[:, 256:512], CW[:, 384:512], NTs(s0), True, False, ["wQ", "NT%d" % s0], [WB], 128, 256)
+            MM(W[:, 256:512], CW[0:8, 768:896], NTs(s1, 8), False, True, ["wV", "NT%d" % s1], [WB], 128, 256)
+            src, sk = nn[:, :], nnk
+            parts = tuple((z, 512, "s") for z in (2560, 3072, 3584)) + tuple((z, 512, "v") for z in range(0, 2560, 512))
+        TTo(T["M" + C][:, 0:w], src, W[:, 0:w], OP.mult, [sk, WB], ["M" + C], w)
+        TTo(T["T" + C][:, 0:w], T["M" + C][:, 0:w], W[:, 256:256 + w], OP.add, ["M" + C, WB], ["T" + C], w)
+        TS(T["B" + C][:, 0:w], T["T" + C][:, 0:w], 4, OP.arith_shift_right, ["T" + C], ["B" + C], w, 2047, OP.bitwise_and)
+        CP(T["OF" + C][:, 0:w], T["B" + C][:, 0:w], ["B" + C], ["OF" + C], w)
+        win = tab[:, 0:2048]
+        dv, ab, xg = T["DV" + C], T["AB" + C], T["XG" + C]
+
+        def keys(nm, p, ln):
+            return ["%s%s.%d" % (nm, C, z) for z in range(p // 512, (p + ln) // 512)]
+
+        def qv(p, ln):
+            return T.QR[:, 2 * p:2 * p + 2 * ln:2] if a == 0 else T.QR[:, p:p + ln]
+        QK = QE if a == 0 else QA
+        for p, ln, e in parts:
+            off = T["OF" + C][:, p // 16:(p + ln) // 16]
+            if e == "v":
+                V(lambda en, p=p, ln=ln, off=off: en.tensor_tensor(dv[:, p:p + ln], win.indirect(off), qv(p, ln), OP.subtract),
+                  ["OF" + C, tkey] + QK, keys("dv", p, ln), ln * 1.5)
+            else:
+                op("s", lambda p=p, ln=ln, off=off: g.scalar.activation(xg[:, p % 2048:p % 2048 + ln], win.indirect(off), FN.Copy),
+                   ["OF" + C, tkey], keys("XG", p % 2048, ln), ln * 1.5 * CY + 0.07)
+        MM(K[:, 0:256], T.ON[0:33, 0:128], T.CR[:, 256 * (a == 0):256 * (a == 0) + 256], True, False, ["ON", "CR"], [KB], 128, 256)
+        pc, pw, bc = (256 + 64 * c, 64, 128 + 64 * c) if a == 0 else (128, 128, 0)
+        for b in (0, 1):
+            MM(K[:, b * 128:b * 128 + pw], nn[:, b * 128:b * 128 + 128], CH[:, pc:pc + pw], False, False, [nnk, "hPM", "hF1"], [KB], 128, pw)
+        for p, ln, e in parts:
+            if e == "v":
+                S(ab[:, p:p + ln], dv[:, p:p + ln], FN.Abs, keys("dv", p, ln), keys("ab", p, ln), ln)
+            else:
+                MM(D[:, :], IB, xg[:, p % 2048:p % 2048 + 512], True, False, ["cI"] + keys("XG", p % 2048, 512), [DB], 128, 512)
+                MM(D[:, :], T.NEGI[:, :], qv(p, 512), False, True, ["NEGI"] + QK, [DB], 128, 512)
+                S(ab[:, p:p + 512], D[:, :], FN.Abs, [DB], keys("ab", p, 512), 512)
+
+        def score(b, last):
+            stp = 8 if a == 0 else 16
+            base = b * 128 * stp
+            for k in range(stp):
+                col = b * 128 + (k * 8 if a == 0 else (k % 8) * 16 + (k // 8) * 8)
+                MM(K[:, col:col + 8], ab[:, base + k:base + 128 * stp:stp], T.S8[:, :], False, last and k == stp - 1,
+                   keys("ab", base, 128 * stp) + ["S8"], [KB], 128, 8)
+        score(0, False)
+        BQ = T["BQ" + C]
+        for j in range(a + 1):
+            s = nt(c, j)
+            x0, j0 = (j % 2) * 256, j * 256
+            MM(X[:, x0:x0 + 256], CW[0:8, 1152:1280], NTs(s, 8), True, True, ["wE", "NT%d" % s], [XB], 128, 256)
+            bk = "BQ%s%d" % (C, j)
+            TTo(BQ[:, j0:j0 + 256], nn[:, :], X[:, x0:x0 + 256], OP.is_equal, [nnk, XB], [bk], 256)
+            for b in (0, 1):
+                MM(K[:, b * 128:b * 128 + pw], BQ[:, j0 + b * 128:j0 + b * 128 + 128], T.CBIG[:, bc:bc + pw], False, False, [bk, "CBIG"], [KB], 128, pw)
+        score(1, True)
+        KD = T["KD" + C]
+        TS(KD[:, 0:16], T[P][:, sl(a) * 16:sl(a) * 16 + 16], REST, OP.add, [P + "s%d" % sl(a)], ["KR" + C], 64)
+        h = 32 if a == 0 else 64
+        SBt, L1, L2, Kt, Rt, SHt = T["SB" + C], T["L1" + C], T["L2" + C], T["K" + C], T["R" + C], T["SH" + C]
+        for b in (0, 1):
+            S(SBt[:, b * 64:b * 64 + h], K[:, b * 128 + h:b * 128 + 2 * h], FN.Copy, [KB], ["SB%s%d" % (C, b)], h)
+        for b in (0, 1):
+            TTo(L1[:, b:2 * h:2], K[:, b * 128:b * 128 + h], SBt[:, b * 64:b * 64 + h], OP.min, [KB, "SB%s%d" % (C, b)], ["L1%s%d" % (C, b)], h)
+        TTo(L2[:, 0:h], L1[:, 0:h], L1[:, h:2 * h], OP.min, ["L1%s0" % C, "L1%s1" % C], ["L2" + C], 2 * h)
+        TTo(Kt[:, 0:h // 2], L2[:, 0:h // 2], L2[:, h // 2:h], OP.min, ["L2" + C], ["K" + C], h)
+        TTo(Kt[:, 0:16], Kt[:, 0:16], KD[:, 0:16], OP.min, ["K" + C, "KR" + C], ["K" + C], 64)
+        ns = sl(a + 1)
+        out, ok = T[P][:, ns * 16:ns * 16 + 16], P + "s%d" % ns
+        if a == 0:
+            TS(Rt[:, 0:16], Kt[:, 0:16], 1023, OP.bitwise_and, ["K" + C], ["R" + C], 64)
+            CP(out, Rt[:, 0:16], ["R" + C], [ok], 64)
+        else:
+            TS(SHt[:, :], Kt[:, :], 13, OP.arith_shift_right, ["K" + C], ["SH" + C], 64)
+            TS(Rt[:, :], Kt[:, :], 1023, OP.bitwise_and, ["K" + C], ["R" + C], 64)
+            TTo(KD[:, 16:32], SHt[:, 0:16], SHt[:, 16:32], OP.is_gt, ["SH" + C], ["SL" + C], 64)
+            TTo(KD[:, 32:48], Rt[:, 16:32], Rt[:, 0:16], OP.subtract, ["R" + C], ["DF" + C], 64)
+            TTo(KD[:, 48:64], KD[:, 32:48], KD[:, 16:32], OP.mult, ["DF" + C, "SL" + C], ["D2" + C], 64)
+            TTo(out, Rt[:, 0:16], KD[:, 48:64], OP.add, ["R" + C, "D2" + C], [ok], 64)
+        if a < 4:
+            s = nt(c, a + 1)
+            for b in (0, 1):
+                MM(X[0:8, b * 128:b * 128 + 128], T[P][:, ns * 16 + b:ns * 16 + 16:2], I16, True, True, [ok, "hI"], [XB], 8, 128)
+            CP(NTs(s, 8), X[0:8, 0:256], [XB], ["NT%d" % s], 256)
+            for i in range(16):
+                MM(X[:, 256:272], T.VH[:, i * 128:i * 128 + 128], T.NT[0:8, s * 256 + i:s * 256 + 256:16], i == 0, i == 15, ["VH", "NT%d" % s], [XB], 128, 16)
+            CP(T["VL" + C][:, :], X[:, 256:272], [XB], ["VL" + C], 64)
+        bon[0] = 0.0
+
+    def lesser(el, tab, tk):
+        TS(T.TMP[:, :], tab[:, 0:2048], 0.75, OP.mult, [tk], ["TMP"], 1024, 1024.375, OP.add)
+        TS(T[el][:, :], T.TMP[:, :], -1024.0, OP.add, ["TMP"], [el], 1024)
+
+    def lessen(tab, tk, mk, el, out, okey, banks):
+        for qd in range(4):
+            b = banks[qd % len(banks)]
+            B = PS[b]
+            MM(B[:, :], IB, tab[:, qd * 512:qd * 512 + 512], True, False, ["cI", tk], ["#" + b], 128, 512)
+            for z in range(4):
+                tt = (qd * 4 + z) * 128
+                MM(B[:, z * 128:z * 128 + 128], T.SELL[:, tt:tt + 128], T[mk][:, :], False, z == 3, ["SELL", mk], ["#" + b], 128, 128)
+            TTo(out[:, qd * 512:qd * 512 + 512], B[:, :], T[el][:, qd * 512:qd * 512 + 512], OP.max, ["#" + b, el], ["%s%d" % (okey, qd)], 512)
+
+    def hot(c0, c1, kz, hk):
+        TS(T.WW[:, c0:c1], T.HH[:, c0:c1], 127, OP.bitwise_and, hk, ["WW" + kz], c1 - c0)
+        TS(T.WS[:, c0:c1], T.WW[:, c0:c1], -128.0, OP.add, ["WW" + kz], ["WS" + kz], c1 - c0)
+        if kz == "e":
+            S(T.WS[:, 160 + c0:160 + c1], T.WS[:, c0:c1], FN.Copy, ["WSe"], ["WB"], c1 - c0, bias=100.0, scale=200.0)
+        for col in sorted(range(c0, c1), key=lambda z: (z % 2, z % 16, z)):
+            o = T.OH[:, col * 128:col * 128 + 128]
+            if col // 16 in SHOT:
+                S(o, T.I128[:, :], FN.Sigmoid, ["I128", "WB"], ["OH%d" % col], 128, bias=T.WS[:, 160 + col:161 + col], scale=-200.0)
+            else:
+                TS(o, T.I128[:, :], T.WS[:, col:col + 1], OP.is_equal, ["I128", "WS" + kz], ["OH%d" % col], 64)
+
+    def rings(t, tab, tk):
+        P = "PT%d" % t
+        pt, JS = T[P], T.JS
+        pk = [P + "s%d" % i for i in range(11)]
+        uk, hw = [P + "u%d" % i for i in range(3)], ["HHe", "HHx", "HHy"]
+        for z, (c0, c1, kk) in enumerate(((16, 160, pk[1:10]), (0, 16, pk[0:1]), (160, 176, pk[10:11]))):
+            TS(T.U[:, c0:c1], pt[:, c0:c1], 2.0, OP.mult, kk, [uk[z]], c1 - c0, 1.0, OP.add)
+        for z, (c0, c1, kk, ku) in enumerate(((16, 128, pk[1:10], uk[0:1]), (0, 16, pk[0:3], uk[0:2]), (128, 144, pk[8:11], [uk[0], uk[2]]))):
+            TTo(T.PR[:, c0:c1], T.U[:, c0:c1], T.U[:, c0 + 32:c1 + 32], OP.mult, ku, ["PR%d" % z], 2 * (c1 - c0))
+            TS(T.V5[:, c0:c1], pt[:, c0 + 16:c1 + 16], 592.0, OP.mult, kk, ["V5%d" % z], c1 - c0)
+            TTo(T.TT[:, c0:c1], T.PR[:, c0:c1], T.V5[:, c0:c1], OP.add, ["PR%d" % z, "V5%d" % z], ["TT%d" % z], 2 * (c1 - c0))
+            TS(T.HH[:, c0:c1], T.TT[:, c0:c1], 4, OP.arith_shift_right, ["TT%d" % z], [hw[z]], c1 - c0, 2047, OP.bitwise_and)
+        hot(16, 128, "e", ["HHe"])
+        x = 0
+        ek = []
+        for L in range(3, 11):
+            i0 = max(1, L - 5)
+            m = (min(5, L - 1) - i0 + 1) * 16
+            a0, b0 = (5 + i0) * 16, (5 + i0 - L) * 16
+            TTo(T.EQ[:, x:x + m], pt[:, a0:a0 + m], pt[:, b0:b0 + m], OP.is_equal, pk, ["EQ%d" % L], 2 * m)
+            ek.append("EQ%d" % L)
+            x += m
+        TTo(T.EW[:, :], T.EQ[:, :], T.WT[:, :], OP.mult, ek + ["WT%d" % z for z in range(0, 384, 16)], ["EW"], 768)
+        TTo(T.E1[:, :], T.EW[:, 0:192], T.EW[:, 192:384], OP.max, ["EW"], ["E1"], 384)
+        TTo(T.E2[:, :], T.E1[:, 0:96], T.E1[:, 96:192], OP.max, ["E1"], ["E2"], 192)
+        TTo(T.E3[:, 0:48], T.E2[:, 0:48], T.E2[:, 48:96], OP.max, ["E2"], ["E3"], 96)
+        TTo(T.E3[:, 48:64], T.E3[:, 0:16], T.E3[:, 16:32], OP.max, ["E3"], ["E4"], 64)
+        JW, JF, JI, JU, JL, JJ, VJ, PJ = [JS[:, z * 16:z * 16 + 16] for z in range(8)]
+        TTo(JW, T.E3[:, 48:64], T.E3[:, 32:48], OP.max, ["E3", "E4"], ["JW"], 64)
+        TS(JF, JW, 0.5, OP.is_ge, ["JW"], ["JF"], 64)
+        TS(T.JR[:, :], JW, -0.2, OP.mult, ["JW"], ["JR"], 64, 5.6, OP.add)
+        TTo(JI, T.JR[:, :], JF, OP.mult, ["JR", "JF"], ["JI"], 64)
+        TS(JU, T.JR[:, :], -4.0, OP.mult, ["JR"], ["JU"], 64, 31.0, OP.add)
+        TTo(JL, JU, JW, OP.subtract, ["JU", "JW"], ["JL"], 64)
+        TTo(T.IL[:, 16:32], JL, JF, OP.mult, ["JL", "JF"], ["ILl"], 64)
+        TTo(JJ, T.IL[:, 16:32], JI, OP.subtract, ["ILl", "JI"], ["JJ"], 64)
+        for m in range(0, 5):
+            z = (5 + m) * 16
+            TS(T.VV[:, z:z + 16], JI, m + 0.5, OP.is_ge, ["JI"], ["VV%d" % (5 + m)], 64)
+            if m:
+                z = (5 - m) * 16
+                TS(T.VV[:, z:z + 16], JJ, m + 0.5, OP.is_ge, ["JJ"], ["VV%d" % (5 - m)], 64)
+        vk = ["VV%d" % i for i in range(11)]
+        MI, MJ = T.MI[:, 0:80], T.MI[:, 80:160]
+        TTo(MI, T.VV[:, 80:160], T.VV[:, 96:176], OP.subtract, vk, ["MI"], 160)
+        TTo(MJ, T.VV[:, 16:96], T.VV[:, 0:80], OP.subtract, vk, ["MJ"], 160)
+        TTo(T.JP[:, 0:80], MI, pt[:, 80:160], OP.mult, ["MI"] + pk, ["JP0"], 160)
+        TTo(T.JP[:, 80:160], MI, pt[:, 96:176], OP.mult, ["MI"] + pk, ["JP1"], 160)
+        TTo(T.JP[:, 160:240], MJ, pt[:, 16:96], OP.mult, ["MJ"] + pk, ["JP2"], 160)
+        J = PS["kA"]
+        for z in range(3):
+            for k in range(5):
+                MM(J[:, z * 16:z * 16 + 16], I16, T.JP[:, z * 80 + k * 16:z * 80 + k * 16 + 16], k == 0, k == 4, ["hI", "JP%d" % z], ["#kA"], 128, 16)
+        TS(T.UJ[:, :], J[:, 0:48], 2.0, OP.mult, ["#kA"], ["UJ"], 64, 1.0, OP.add)
+        TS(VJ, J[:, 16:32], 592.0, OP.mult, ["#kA"], ["VJ"], 64)
+        TTo(PJ, T.UJ[:, 0:16], T.UJ[:, 32:48], OP.mult, ["UJ"], ["PJ"], 64)
+        TTo(T.TT[:, 144:160], PJ, VJ, OP.add, ["PJ", "VJ"], ["TTb"], 64)
+        TS(T.HH[:, 144:160], T.TT[:, 144:160], 4, OP.arith_shift_right, ["TTb"], ["HHb"], 64, 2047, OP.bitwise_and)
+        hk = hw + ["HHb"]
+        TS(T.HS[:, :], T.HH[:, :], -2048.0, OP.add, hk, ["HS"], 160)
+        TTo(T.HV[:, 0:144], T.HS[:, 0:144], T.VV[:, 16:160], OP.mult, ["HS"] + vk, ["HVa"], 288)
+        TTo(T.HV[:, 144:160], T.HS[:, 144:160], T.VV[:, 80:96], OP.mult, ["HS"] + vk, ["HVb"], 64)
+        TS(T.TB[:, :], T.HH[:, :], 7, OP.arith_shift_right, hk, ["TB"], 160)
+        TS(T.TBP[:, :], T.TB[:, :], 2.0, OP.add, ["TB"], ["TBP"], 160)
+        TTo(T.TV[:, 0:144], T.TBP[:, 0:144], T.VV[:, 16:160], OP.mult, ["TBP"] + vk, ["TVa"], 288)
+        TTo(T.TV[:, 144:160], T.TBP[:, 144:160], T.VV[:, 80:96], OP.mult, ["TBP"] + vk, ["TVb"], 64)
+        X, X2 = PS["xA"], PS["xB"]
+        for b in (0, 1):
+            MM(X[0:80, b * 128:b * 128 + 128], T.HV[:, b::2], I16, True, True, ["HVa", "HVb", "hI"], ["#xA"], 80, 128)
+        CP(T.HT[:, :], X[0:80, 0:256], ["#xA"], ["HT"], 256)
+        MM(X2[:, 0:128], CH[0:80, 1104:1232], T.HT[:, 0::2], True, False, ["hPR", "HT"], ["#xB"], 128, 128)
+        MM(X2[:, 0:128], CH[0:80, 1360:1488], T.HT[:, 1::2], False, True, ["hPS", "HT"], ["#xB"], 128, 128)
+        for z in range(8):
+            MM(X2[:, 128:160], CH[64:80, 1488 + z * 128:1616 + z * 128], T.HT[64:80, z::8], z == 0, z == 7, ["hPS", "HT"], ["#xB"], 128, 32)
+        TS(T.OFR[:, 0:160], X2[:, 0:160], 2048.0, OP.add, ["#xB"], ["OFR"], 160)
+        win = tab[:, 0:2064]
+        for b in (1, 0):
+            for x0, ln in ((b * 1024, 1024), (2048 + b * 256, 256)):
+                xo, fo = T.XR[:, x0:x0 + ln], T.OFR[:, x0 // 16:(x0 + ln) // 16]
+                if b:
+                    op("s", lambda xo=xo, fo=fo: g.scalar.activation(xo, win.indirect(fo), FN.Copy), ["OFR", tk, tk + "z"], ["XR%d.%d" % (b, ln)], ln * 1.5 * CY + 0.07)
+                else:
+                    V(lambda e, xo=xo, fo=fo: e.tensor_copy(xo, win.indirect(fo)), ["OFR", tk, tk + "z"], ["XR%d.%d" % (b, ln)], ln * 1.5)
+        for b in (0, 1):
+            MM(X[0:80, b * 128:b * 128 + 128], T.TV[:, b::2], I16, True, True, ["TVa", "TVb", "hI"], ["#xA"], 80, 128)
+        S(T.TVL[:, :], X[0:80, 0:256], FN.Copy, ["#xA"], ["TVL"], 256)
+        hot(0, 16, "a", hk)
+        hot(128, 160, "b", hk)
+        B, W = PS["kB"], PS["wA"]
+        for b in (0, 1):
+            for m in range(10):
+                xs = T.XR[:, b * 1024 + m:(b + 1) * 1024:8] if m < 8 else T.XR[:, 2040 + b * 256 + m:2304 + b * 256:2]
+                MM(B[:, b * 128:b * 128 + 128], IB, xs, m == 0, m == 9, ["cI", "XR%d.%d" % (b, 1024 if m < 8 else 256)], ["#kB"], 128, 128)
+        for b in (0, 1):
+            TS(T.CMP[:, b * 128:b * 128 + 128], B[:, b * 128:b * 128 + 128], T.THF[:, 0:1], OP.is_ge, ["#kB", "THF"], ["CMP%d" % b], 128)
+        MM(W[0:80, 0:256], CB[:, 1024:1104], T.CMP[:, :], True, True, ["CMP0", "CMP1", "cRC"], ["#wA"], 80, 256)
+        TS(T.HVY[:, :], W[0:80, 0:256], 8.5, OP.is_ge, ["#wA"], ["HVY"], 256)
+        TTo(T.TM[0:80, :], T.TVL[:, :], T.HVY[:, :], OP.mult, ["TVL", "HVY", "TMz"], ["TM"], 512)
+        C = PS["wB"]
+        z = 0
+        for b in (0, 1):
+            for c0 in range(0, 1280, 512):
+                c1 = min(1280, c0 + 512)
+                bn = ("xA", "wA", "dA")[z % 3]
+                z += 1
+                MM(PS[bn][:, 0:c1 - c0], T.TM[:, b * 128:b * 128 + 128], T.RT[:, c0:c1], True, True, ["TM", "TMz", "RT"], ["#" + bn], 128, c1 - c0)
+                S(T.TL[:, b * 1280 + c0:b * 1280 + c1], PS[bn][:, 0:c1 - c0], FN.Sigmoid, ["#" + bn, "CSz"], ["TL%d.%d" % (b, c0 // 512)], c1 - c0,
+                  bias=T.CS[:, 129:130], scale=200.0)
+        for b in (0, 1):
+            for th in (0, 1):
+                for gr in range(8):
+                    ms = [m for m in range(10) if (m in SHOT) == bool(th)]
+                    y = th * 256 + b * 128 + gr * 16
+                    for m in ms:
+                        col = m * 16 + gr * 2 + b
+                        l0 = (m * 8 + gr) * 16
+                        MM(C[:, y:y + 16], T.OH[:, col * 128:col * 128 + 128], T.TL[:, b * 1280 + l0:b * 1280 + l0 + 16], m == ms[0], m == ms[-1],
+                           ["OH%d" % col, "TL%d.%d" % (b, l0 // 512)], ["#wB"], 128, 16)
+        CP(T.C2[:, :], C[:, :], ["#wB"], ["C2"], 512)
+        C = PS["xB"]
+        for z in range(4):
+            MM(C[:, 0:128], CH[:, 1232:1360] if z > 1 else I16, T.C2[:, z * 128:z * 128 + 128], z == 0, z == 3, ["hDM", "hI", "C2"], ["#xB"], 128, 128)
+        TTo(T.CS[:, 0:128], C[:, 0:128], T.MT0[:, :], OP.mult, ["#xB", "MT0"], ["CS"], 128)
+        TTo(T.DD[:, :], C[:, 0:128], T.CS[:, 1:129], OP.subtract, ["#xB", "CS", "CSz"], ["DD"], 128)
+        TS(T.MK[:, :], T.DD[:, :], 1.0, OP.min, ["DD"], ["MK"], 128, -512.0, OP.mult)
+        MM(X[:, 0:128], T.MK[:, :], IB, True, True, ["MK", "cI"], ["#xA"], 128, 128)
+        S(T.MKT[:, :], X[:, 0:128], FN.Copy, ["#xA"], ["MKT"], 128)
+
+    def show(t):
+        P = "PT%d" % t
+        pt = T[P]
+        D, E = PS["dA"], PS["dB"]
+        TTo(T.IL[:, 0:16], T.JS[:, 32:48], T.JS[:, 16:32], OP.add, ["JI", "JF"], ["ILi"], 64)
+        for b in (0, 1):
+            MM(D[0:8, b * 128:b * 128 + 128], pt[:, 160 + b:176:2], I16, True, True, [P + "s10", "hI"], ["#dA"], 8, 128)
+        for b in (0, 1):
+            MM(D[0:8, 256 + b * 128:384 + b * 128], T.IL[:, b:16:2], I16, True, True, ["ILi", "hI"], ["#dA"], 8, 128)
+        for b in (0, 1):
+            MM(E[0:8, b * 128:b * 128 + 128], T.IL[:, 16 + b:32:2], I16, True, True, ["ILl", "hI"], ["#dB"], 8, 128)
+        CP(NTs(5, 8), D[0:8, 0:256], ["#dA"], ["NT5"], 256)
+        CP(NTs(10, 8), D[0:8, 256:512], ["#dA"], ["NT10"], 256)
+        CP(NTs(11, 8), E[0:8, 0:256], ["#dB"], ["NT11"], 256)
+        for z in (0, 1):
+            MM(D[:, z * 256:z * 256 + 256], CW[:, 1280:1408], NTs(10 + z), True, True, ["wM", "NT%d" % (10 + z)], ["#dA"], 128, 256)
+        for i in range(6):
+            MM(E[:, 0:256], T.VH[:, i * 128:i * 128 + 128], NTs(i, 8), i == 0, i == 5, ["VH", "NT%d" % i], ["#dB"], 128, 256)
+        R1, R2 = D[:, 0:256], D[:, 256:512]
+        TS(T.YN[:, :], R1, 0.5, OP.is_le, ["#dA"], ["YN"], 256)
+        TS(T.YM[:, :], R1, 0.5, OP.is_ge, ["#dA"], ["YM"], 256)
+        TTo(T.YP[:, :], T.YN[:, :], R2, OP.mult, ["#dA", "YN"], ["YP"], 256)
+        TS(T.YB[:, 256:512], R2, 0.5, OP.is_le, ["#dA"], ["YB1"], 256, -1.0, OP.mult)
+        TTo(T.YB[:, 0:256], T.YM[:, :], E[:, 0:256], OP.mult, ["#dB", "YM"], ["YB0"], 256)
+        for j in range(1, 5):
+            k0 = (j - 1) * 256
+            MM(E[:, 256:512], CW[0:8, 1152:1280], NTs(5 + j, 8), True, True, ["wE", "NT%d" % (5 + j)], ["#dB"], 128, 256)
+            TS(T.YK[:, k0:k0 + 256], T.YP[:, :], float(j), OP.is_equal, ["YP"], ["YK%d" % j], 128)
+            TTo(T.YB[:, 256 + j * 256:512 + j * 256], T.YK[:, k0:k0 + 256], E[:, 256:512], OP.mult, ["YK%d" % j, "#dB"], ["YB%d" % (j + 1)], 256)
+        for z in range(6):
+            MM(D[:, 0:256], I16, T.YB[:, z * 256:z * 256 + 256], z == 0, z == 5, ["hI", "YB%d" % z], ["#dA"], 128, 256)
+        S(T.YR[:, t * 256:t * 256 + 256], D[:, 0:256], FN.Copy, ["#dA"], ["YR%d" % t], 256)
+        DMA("y", T.yr[:, t * 256:t * 256 + 256], T.YR[:, t * 256:t * 256 + 256], ["YR%d" % t], [])
+
+    start(0)
+    for a in range(5):
+        step(0, 0, a, T.TO, "TO")
+        step(0, 1, a, T.TP0, "TP0")
+    late_constants()
+    lesser("EL0", T.TO, "TO")
+    lesser("ELn", T.TPn, "TPn")
+    rings(0, T.TO, "TO")
+    send(6)
+    arrive("MKP", "aMK", (r + 2) % n, 7.0, ["MKT"])
+    show(0)
+    lessen(T.TO, "TO", "MKT", "EL0", T.TO1, "T1q", ("kA", "kB", "xB", "wA"))
+    op(None, None, ["T1q%d" % q for q in range(4)], ["TO1"], 0.0, "n")
+    start(1)
+    lessen(T.TPn, "TPn", "MKP", "ELn", T.TP1, "P1q", ("dB",))
+    op(None, None, ["P1q%d" % q for q in range(4)], ["TP1"], 0.0, "n")
+    for a in range(5):
+        step(1, 0, a, T.TO1, "TO1")
+        step(1, 1, a, T.TP1, "TP1")
+    lesser("EL1", T.TO1, "TO1")
+    rings(1, T.TO1, "TO1")
+    show(1)
+    lessen(T.TO1, "TO1", "MKT", "EL1", T.TO2, "T2q", ("kA", "kB", "xB", "wA"))
+    for qd in range(4):
+        DMA("y" if qd % 2 == 0 else "s", T.ye[:, qd * 512:qd * 512 + 512], T.TO2[:, qd * 512:qd * 512 + 512], ["T2q%d" % qd], [])
+    for o in ops:
+        more = set()
+        for d in o["deps"]:
+            if ops[d]["kind"] == "n":
+                more |= ops[d]["deps"]
+            else:
+                more.add(d)
+        o["deps"] = more
+    return ops
+
+
+def schedule(ops):
+    n = len(ops)
+    wake, same = 0.12, 0.04
+    succ = [[] for _ in range(n)]
+    need = [0] * n
+    for i, o in enumerate(ops):
+        for d in o["deps"]:
+            succ[d].append((i, False))
+            need[i] += 1
+        for d in o["order"]:
+            succ[d].append((i, True))
+            need[i] += 1
+    prio = [0.0] * n
+    for i in range(n - 1, -1, -1):
+        best = 0.0
+        for j, od in succ[i]:
+            best = max(best, prio[j] + (0.0 if od else (wake if ops[j]["q"] != ops[i]["q"] else same)))
+        prio[i] = best + ops[i]["cost"] + ops[i]["lat"]
+    prio = [prio[i] + ops[i]["bon"] for i in range(n)]
+    ready, free, order = {}, {}, []
+    tready, fin = [0.0] * n, [0.0] * n
+    for i in range(n):
+        if need[i] == 0:
+            ready.setdefault(ops[i]["q"], []).append(i)
+    while len(order) < n:
+        bq, bt = None, 1e18
+        for q in ready:
+            for i in ready[q]:
+                s = max(free.get(q, 0.0), tready[i])
+                if s < bt:
+                    bt, bq = s, q
+        lst = ready[bq]
+        pick, pp = None, -1e9
+        for i in lst:
+            if max(free.get(bq, 0.0), tready[i]) <= bt + 0.1 and prio[i] > pp:
+                pick, pp = i, prio[i]
+        lst.remove(pick)
+        if not lst:
+            del ready[bq]
+        o = ops[pick]
+        s = max(free.get(bq, 0.0), tready[pick])
+        if bq is not None:
+            free[bq] = s + o["cost"]
+        fin[pick] = s + o["cost"] + o["lat"]
+        order.append(pick)
+        for j, od in succ[pick]:
+            tj = s if od else fin[pick] + (wake if ops[j]["q"] != o["q"] else same)
+            tready[j] = max(tready[j], tj)
+            need[j] -= 1
+            if need[j] == 0:
+                ready.setdefault(ops[j]["q"], []).append(j)
+    return order
+
+
+def emit(g, T, ops, order):
+    eng = {"v": g.vector, "s": g.scalar, "t": g.tensor, "g": g, "y": g.sync}
+    csem = {"v": "v", "s": "s", "t": "t", "g": "gc"}
+    count, final = {}, {}
+    know = {q: {} for q in eng}
+    mark = [None] * len(ops)
+    after = [None] * len(ops)
+    for i in order:
+        o = ops[i]
+        q = o["q"]
+        if o["kind"] == "n":
+            continue
+        if o["kind"] == "x":
+            mark[i] = (o["sem"], o["val"])
+            after[i] = {o["sem"]: o["val"]}
+            final[o["sem"]] = o["val"]
+            continue
+        K = know[q]
+        for d in sorted(o["deps"], key=lambda d: -sum(after[d].values())):
+            s, v = mark[d]
+            if K.get(s, 0) >= v:
+                continue
+            eng[q].wait_ge(T.sem[s], v)
+            for s2, v2 in after[d].items():
+                if K.get(s2, 0) < v2:
+                    K[s2] = v2
+        if q == "g" and o["kind"] == "c" and K.get("gc", 0) < count.get("gc", 0):
+            g.wait_ge(T.sem["gc"], count["gc"])
+            K["gc"] = count["gc"]
+        ins = o["fn"]()
+        if o["kind"] == "c":
+            s = csem[q]
+            count[s] = count.get(s, 0) + 1
+            ins.then_inc(T.sem[s], 1)
+            mark[i] = (s, count[s])
+        elif o["kind"] == "d":
+            ins.then_inc(T.sem[o["sem"]], 16)
+            mark[i] = (o["sem"], 16)
+        else:
+            mark[i] = (o["sem"], o["val"])
+        final[mark[i][0]] = mark[i][1]
+        after[i] = dict(K)
+        after[i][mark[i][0]] = mark[i][1]
+    for s in final:
+        if know["g"].get(s, 0) < final[s]:
+            g.wait_ge(T.sem[s], final[s])
+
+
+def rank_program(g, core, T, topo):
+    if T.rank_of(core) is None:
+        hand_on(g, core, T, topo)
+        return
+    ops = build(g, core, T, topo)
+    if "order" not in ORDERS:
+        ORDERS["order"] = schedule(ops)
+    emit(g, T, ops, ORDERS["order"])

@@ -1,36 +1,35 @@
-from concourse.mybir import dt, AluOpType, ActivationFunctionType
+from concourse.mybir import dt, AluOpType, AxisListType, ActivationFunctionType
 import comms_topo
 
 OP = AluOpType
 FN = ActivationFunctionType
 BIG = float(2 ** 26)
-REST = float(2041 * 8192)
-F32, B16, H16, I32 = "float32", "bfloat16", "float16", "int32"
+REST = 2041 * 8192
+F32, B16, H16, I32, U16 = "float32", "bfloat16", "float16", "int32", "uint16"
+NV = [1024, 2048, 2048, 2048, 1536]
+SHOT = [0, 1, 2, 8]
 SCRATCH = {}
 for _n, _p, _w, _t in (
-        ("NB", 128, 1024, I32), ("XI", 128, 1024, I32), ("TO", 128, 2064, B16), ("TO1", 128, 2064, B16), ("TO2", 128, 2048, B16),
+        ("NB", 128, 1024, I32), ("XI", 128, 176, I32), ("XJ", 128, 176, I32), ("TO", 128, 2064, B16), ("TO1", 128, 2064, B16), ("TO2", 128, 2048, B16),
         ("TP0", 128, 2048, B16), ("TPn", 128, 2048, B16), ("TP1", 128, 2048, B16), ("EL0", 128, 2048, B16), ("ELn", 128, 2048, B16),
-        ("EL1", 128, 2048, B16), ("TMP", 128, 2048, H16), ("ST", 128, 32, I32), ("SU", 128, 32, "uint16"), ("TH", 128, 1, I32),
-        ("THF", 128, 1, F32), ("Q", 128, 256, B16), ("QR", 128, 4096, B16), ("ON", 128, 2048, B16), ("CB", 128, 2384, B16),
-        ("CT", 128, 464, B16), ("CH", 128, 2512, H16), ("C2", 128, 512, H16), ("CF", 9, 1024, B16), ("CW", 9, 1408, H16),
-        ("VS", 8, 2048, B16), ("VH", 8, 2048, H16), ("SELL", 128, 2048, B16), ("CBIG", 128, 256, B16), ("S8", 128, 8, B16),
-        ("NEGI", 128, 128, B16), ("CR", 33, 512, B16), ("I128", 128, 128, B16), ("RT", 97, 1280, B16), ("MT0", 128, 128, B16),
-        ("WT", 128, 384, B16), ("NT", 9, 3072, H16), ("X0B", 128, 256, H16), ("PT0", 128, 176, H16), ("PT1", 128, 176, H16),
-        ("NPK0", 128, 128, F32), ("NPK1", 128, 128, F32), ("U", 128, 176, F32), ("PR", 128, 144, F32), ("V5", 128, 144, F32),
-        ("TT", 128, 160, I32), ("HH", 128, 160, I32), ("EQ", 128, 384, B16), ("EW", 128, 384, B16), ("E1", 128, 192, B16),
-        ("E2", 128, 96, B16), ("E3", 128, 64, B16), ("JS", 128, 128, F32), ("JR", 128, 16, I32), ("IL", 128, 32, H16),
-        ("VV", 128, 176, F32), ("MI", 128, 160, F32), ("JP", 128, 240, H16), ("UJ", 128, 48, F32), ("WW", 128, 160, I32),
-        ("TB", 128, 160, I32), ("TBP", 128, 160, F32), ("TV", 128, 160, H16), ("TVL", 80, 256, B16), ("HS", 128, 160, F32),
-        ("HV", 128, 160, H16), ("WS", 128, 320, F32), ("HT", 80, 256, H16), ("OFR", 128, 256, "uint16"), ("XR", 128, 2560, B16),
-        ("CMP", 128, 256, B16), ("HVY", 80, 256, B16), ("TM", 97, 256, B16), ("OH", 128, 20480, B16), ("TL", 128, 2560, B16),
-        ("CS", 128, 132, F32), ("DD", 128, 128, F32), ("MK", 128, 128, B16), ("MKT", 128, 128, B16), ("MKP", 128, 128, B16),
-        ("YN", 128, 256, H16), ("YM", 128, 256, H16), ("YP", 128, 256, H16), ("YK", 128, 1024, H16), ("YB", 128, 1536, H16),
-        ("YR", 128, 512, F32)):
+        ("TMP", 128, 2048, H16), ("ST", 128, 32, I32), ("SU", 128, 32, U16), ("STH", 128, 32, H16), ("TH", 128, 1, I32),
+        ("THF", 128, 1, F32), ("Q", 128, 256, B16), ("QR", 128, 4096, B16), ("QZ", 128, 2048, B16), ("ON", 128, 2048, B16), ("CB", 128, 1424, B16),
+        ("CH", 128, 2192, H16), ("SI", 128, 512, H16), ("CG", 128, 384, B16), ("CF", 17, 384, B16), ("CW", 17, 1408, H16), ("CC", 128, 32, F32),
+        ("VH", 16, 1024, H16), ("SELL", 128, 2048, B16), ("S8", 128, 8, B16), ("RC", 128, 160, B16), ("RS", 128, 16, F32),
+        ("CR", 33, 256, B16), ("IO", 128, 128, B16), ("RT", 97, 1280, B16), ("RH", 97, 1280, H16), ("IX", 1, 544, B16),
+        ("NT", 17, 1408, H16), ("NZ", 128, 256, H16), ("PT0", 128, 176, H16), ("PT1", 128, 176, H16), ("NP0", 128, 128, H16), ("NP1", 128, 128, H16),
+        ("DZ", 128, 128, F32), ("U", 128, 176, F32), ("PR", 128, 144, F32), ("V5", 128, 144, F32), ("PX", 128, 176, F32), ("DX", 128, 160, F32),
+        ("TT", 128, 160, I32), ("HH", 128, 160, I32), ("JA", 128, 400, B16), ("JD", 128, 400, B16), ("JC", 128, 400, B16),
+        ("JI", 128, 64, I32), ("JS", 128, 96, F32), ("IL", 128, 32, H16), ("NM", 128, 160, F32), ("JP", 128, 192, H16),
+        ("WW", 128, 160, I32), ("WS", 128, 160, F32), ("HV", 128, 160, H16), ("HT", 80, 256, H16), ("OFR", 128, 160, U16), ("XR", 128, 2560, B16),
+        ("CMP", 128, 256, B16), ("TM", 97, 256, H16), ("OH", 128, 20480, B16), ("TL", 128, 2560, B16), ("C2", 128, 272, H16),
+        ("MKT", 128, 128, B16), ("MKP", 128, 128, B16), ("AT", 96, 128, H16), ("LT", 16, 256, H16),
+        ("YM", 128, 256, H16), ("YP", 128, 256, H16), ("YK", 128, 512, H16), ("YB", 128, 1536, H16), ("YR", 128, 256, F32)):
     SCRATCH[_n] = ("sbuf", [_p, _w], _t)
 for _c in "01":
-    for _n, _w, _t in (("NN", 256, H16), ("M", 256, F32), ("T", 256, I32), ("B", 256, I32), ("OF", 256, "uint16"), ("DV", 2560, B16),
-                       ("AB", 4096, B16), ("XG", 2048, B16), ("BQ", 1280, B16), ("SB", 128, F32), ("L1", 128, F32), ("L2", 64, F32),
-                       ("K", 32, I32), ("KD", 64, F32), ("SH", 32, I32), ("R", 32, I32), ("VL", 16, "uint16")):
+    for _n, _w, _t in (("NN", 256, H16), ("M", 256, F32), ("T", 256, I32), ("B", 256, I32), ("OF", 256, U16), ("DV", 2560, B16),
+                       ("AB", 4096, B16), ("XG", 3072, B16), ("BQ", 1280, B16), ("D", 256, F32), ("SC", 256, F32),
+                       ("K", 32, I32), ("KD", 48, F32), ("SH", 32, I32), ("R", 32, I32), ("VL", 16, U16)):
         SCRATCH[_n + _c] = ("sbuf", [128, _w], _t)
 BANKS = ("kA", "kB", "wA", "wB", "xA", "xB", "dA", "dB")
 for _b in BANKS:
@@ -40,14 +39,8 @@ NDMA = 14
 SEMAPHORES = ["v", "s", "t", "gc", "aTP0", "aTPn", "aMK"] + ["d%d" % i for i in range(NDMA)]
 SEMAPHORES += ["ri%d" % i for i in range(NITEM)] + ["lo%d" % i for i in range(NITEM)]
 
-CY = 0.00104
-TCY = 0.00075
-LEAD = 6.0
-SHOT = (1, 2, 3, 4)
-HINT = {"vM1": -2.0, "vOF0": -5.0, "vBQ1": 1.0, "vNN0": -0.5, "t#kA": -0.5, "t#xB": 0.5, "sab0": -28.5, "vCSz": 13.0, "vYP": -8.0,
-        "vOH": -7.0, "vhF": -20.0, "vWWe": -3.5, "vVL0": -2.5, "vMJ": -2.5, "vTVb": -2.0, "sXG0": -8.5, "vwP": -4.0, "sXG1": -0.5,
-        "vMK": 7.0, "vcPa": 2.0, "vSH1": 16.0, "vWSb": -5.0, "vcE": 10.5, "vhPS": -6.0, "vD20": 1.0, "vPTu": -4.0, "vWWa": 1.5,
-        "vNT": 1.5, "t#dA": 0.5, "vTHF": -0.5, "vJR": 1.0, "vJP": -2.0, "vTMz": 8.5, "vR1": 5.0, "vDD": 0.5}
+PLAN = dict(cy=0.00100, tcy=0.00062, gat=1.5, wake=0.12, same=0.05, lead=6.0, tp0=12.0, mk=7.0, turns=3)
+HINT = {}
 ORDERS = {}
 
 
@@ -98,6 +91,7 @@ def build(g, core, T, topo):
     ops = []
     lastw, reads, bank = {}, {}, {}
     bon = [0.0]
+    CY, TCY, GAT = PLAN["cy"], PLAN["tcy"], PLAN["gat"]
 
     def hint(q, W):
         if not W or q is None:
@@ -158,14 +152,23 @@ def build(g, core, T, topo):
     def S(out, a, f, R, W, n, **kw):
         op("s", lambda: g.scalar.activation(out, a, f, **kw), R, W, max(64, n) * CY + 0.05)
 
+    def SG(out, a, R, W, n):
+        op("s", lambda: g.scalar.activation(out, a, FN.Copy), R, W, n * GAT * CY + 0.07)
+
     def MM(out, l, r, st, sp, R, W, m, n):
         op("t", lambda: g.tensor.matmul(out, l, r, st, sp), R, W, max(min(64, m), n) * TCY + 0.01)
 
     def GC(fn, R, W, n):
         op("g", fn, R, W, 0.18 + 2 * n * CY)
 
-    def iota(out, pat, base, R, W, n):
-        GC(lambda: g.iota(out, pat, base, 0, allow_small_or_imprecise_dtypes=True), R, W, n)
+    def iota(out, pat, base, cm, R, W, n):
+        GC(lambda: g.iota(out, pat, base, cm, allow_small_or_imprecise_dtypes=True), R, W, n)
+
+    def eqs(b, c0, pat, base, key, rows=128):
+        n = 1
+        for p in pat:
+            n *= p[1]
+        GC(lambda: g.affine_select(b[0:rows, c0:c0 + n], T.ON[0:rows, 0:n], pat, OP.is_equal, 0.0, base, 1), ["ON" if n <= 256 else "ONb"], [key], n)
 
     nd = [0]
 
@@ -183,115 +186,118 @@ def build(g, core, T, topo):
     DMA("s", T.Q[:, :], T.q[:, :], [], ["Q"])
     DMA("y", T.TH[:, :], T.th[:, :], [], ["TH"])
 
-    fill(T.ON[:, :], 1.0, [], ["ON"], 1024)
-    fill(T.TO[:, 2048:2064], 0.0, [], ["TOz"], 64)
-    fill(T.TO1[:, 2048:2064], 0.0, [], ["TO1z"], 64)
-
-    def aff(out, src, pat, cmp, fv, base, cm, R, W):
-        n = 1
-        for p in pat:
-            n *= p[1]
-        GC(lambda: g.affine_select(out, src, pat, cmp, fv, base, cm), R, W, n)
-
-    def eqs(b, c0, pat, base, key, rows=128, cm=1):
-        n = 1
-        for p in pat:
-            n *= p[1]
-        aff(b[0:rows, c0:c0 + n], T.ON[0:rows, 0:n], pat, OP.is_equal, 0.0, base, cm, ["ON"], [key])
-
-    GC(lambda: g.iota(T.XI[:, 0:256], [[1, 256]], 0, 0), [], ["XI0"], 256)
-    for z in range(1, 4):
-        TS(T.XI[:, z * 256:z * 256 + 256], T.XI[:, 0:256], float(z * 256), OP.add, ["XI0"], ["XI%d" % z], 256)
-    CB, CH, CF, CW, CT = T.CB, T.CH, T.CF, T.CW, T.CT
-    hi = [[0, 8], [1, 2], [0, 8]]
-    eqs(CB, 128, [[-1, 8], [-8, 2], [-16, 8]], 0, "cPM")
-    eqs(CB, 0, [[-1, 128]], 0, "cI")
-    iota(CT[:, 208:336], hi, 0, [], ["cHi"], 128)
-    eqs(CB, 256, [[-1, 8], [-16, 8]], 0, "cA1")
-    eqs(CB, 320, [[-1, 8], [-16, 8]], -8, "cB1")
-    eqs(CF, 384, [[-1, 8], [0, 16]], 0, "cE0", 9)
-    aff(CF[0:9, 0:128], CF[0:9, 384:512], [[0, 128]], OP.not_equal, 0.5, -8, 1, ["cE0"], ["cF0"])
-    for z, kz in ((0, "cF"), (384, "cE")):
-        TTo(CF[0:9, z + 256:z + 384], CF[0:9, z:z + 128], CT[0:9, 208:336], OP.mult, [kz + "0", "cHi"], [kz + "2"], 256)
-        TTo(CF[0:9, z + 128:z + 256], CF[0:9, z:z + 128], CF[0:9, z + 256:z + 384], OP.subtract, [kz + "0", kz + "2"], [kz + "1"], 256)
-    fill(T.CR[:, :], 0.0, [], ["CR"], 256)
-    fill(T.CR[0:1, :], -16711680.0, ["CR"], ["CR"], 256)
-    iota(T.CR[32:33, 0:256], [[0, 2], [1024, 8], [0, 16]], 0, ["CR"], ["CR"], 256)
-    for z in (256, 384):
-        iota(T.CR[32:33, z:z + 64], [[1024, 8], [0, 8]], 0, ["CR"], ["CR"], 64)
-    aff(CT[:, 0:128], T.ON[:, 0:128], [[-16, 8], [0, 16]], OP.is_ge, 0.0, 0, 1, ["ON"], ["cT0"])
-    aff(CB[:, 896:1024], CT[:, 0:128], [[16, 8], [0, 16]], OP.is_ge, 0.0, 15, -1, ["cT0"], ["cEB"])
-    eqs(T.VS, 0, [[1, 16], [-16, 8], [-1, 16]], 0, "VS", 8, 16)
-    iota(T.I128[:, :], [[1, 128]], -128, [], ["I128"], 128)
-    eqs(T.RT, 0, [[-1, 80], [0, 16]], 0, "RT", 97)
-    iota(T.RT[96:97, :], [[0, 80], [-1, 16]], -2, ["RT"], ["RT"], 1280)
-    iota(T.MT0[:, :], [[0, 8], [1, 16]], 0, [], ["MT0"], 128)
-    aff(CT[:, 128:208], T.ON[:, 0:80], [[0, 10], [-16, 8]], OP.is_ge, 0.0, 0, 1, ["ON"], ["cT1"])
-    aff(CB[:, 1024:1104], CT[:, 128:208], [[0, 10], [16, 8]], OP.is_ge, 0.0, 15, -1, ["cT1"], ["cRC"])
-    eqs(CB, 1104, [[-1, 8], [1000, 2], [-8, 8]], 0, "cPR", 80)
-    eqs(CB, 1232, [[-1, 8], [1000, 2], [-8, 8]], -1000, "cPS", 80)
-    for z in range(8):
-        eqs(CB, 1360 + z * 128, [[-1, 8], [1000, 8], [-8, 2]], -64 - 1000 * z, "cPT%d" % z, 80)
-    iota(CF[0:9, 768:896], [[0, 8], [-1, 16]], 0, [], ["cM0"], 128)
-    aff(CF[0:9, 896:1024], CF[0:9, 768:896], [[0, 128]], OP.is_equal, 0.0, -8, 1, ["cM0"], ["cM1"])
-    eqs(CT, 336, [[-1, 128]], -1, "cSF")
-    eqs(T.SELL, 0, [[-1, 16], [-16, 8], [0, 16]], 0, "SELL")
-
-    I16, IB = CH[:, 0:128], CB[:, 0:128]
+    CB, CH, CG, CF, CW, CC = T.CB, T.CH, T.CG, T.CF, T.CW, T.CC
+    IB, I16, NEGI, BIGI, BIGP = CB[:, 8:136], CH[:, 8:136], CG[:, 0:128], CG[:, 128:256], CG[:, 256:384]
+    PMV, PM0 = 144, 272
+    fill(T.ON[:, 0:256], 1.0, [], ["ON"], 128)
+    fill(T.NT[:, :], 1.0, [], ["NT%d" % s for s in range(11)], 704)
+    eqs(CB, 0, [[-1, 144]], 8, "cI")
+    eqs(CB, PMV, [[-2, 8], [-1, 2], [-16, 8]], 0, "cPV")
+    eqs(CB, PM0, [[-8, 2], [-16, 8], [-1, 8]], 0, "cP0")
+    eqs(CF, 0, [[-1, 8], [-8, 2], [0, 8]], 0, "cE0", 17)
+    eqs(CF, 128, [[-8, 2], [-1, 8], [0, 16]], 0, "cEB", 17)
+    GC(lambda: g.iota(T.XI[:, 0:8], [[-16, 8]], 0, 1), [], ["XI"], 8)
+    iota(T.CR[:, :], [[0, 32], [1024, 8]], 0, 0, [], ["CR"], 256)
+    iota(T.RS[:, :], [[2048, 16]], REST, 0, [], ["RS"], 16)
+    CP(T.STH[:, :], T.ST[:, :], ["ST"], ["STH"], 64)
     CP(T.SU[:, :], T.ST[:, :], ["ST"], ["SU"], 64)
-    CP(CH[:, 128:256], CB[:, 128:256], ["cPM"], ["hPM"], 64)
-    CP(CH[:, 0:128], IB, ["cI"], ["hI"], 64)
-    fill(CB[:, 512:520], 0.0, [], ["cP1a"], 64)
-    fill(CB[:, 760:768], 0.0, [], ["cP2a"], 64)
-    TTo(CB[:, 768:896], IB, CT[:, 208:336], OP.mult, ["cI", "cHi"], ["cP3"], 256)
-    TTo(CB[:, 384:512], IB, CB[:, 768:896], OP.subtract, ["cI", "cP3"], ["cP0"], 256)
-    CP(CB[:, 520:640], CB[:, 384:504], ["cP0"], ["cP1"], 64)
-    CP(CB[:, 640:760], CB[:, 776:896], ["cP3"], ["cP2"], 64)
-    CP(CH[:, 384:896], CB[:, 384:896], ["cP0", "cP1", "cP1a", "cP2", "cP2a", "cP3"], ["hP4"], 256)
-    CP(CH[:, 256:384], CB[:, 256:384], ["cA1", "cB1"], ["hF1"], 64)
-    FK, EK = ["cF0", "cF1", "cF2"], ["cE0", "cE1", "cE2"]
-    TS(CW[:, 0:384], CF[:, 0:384], 4.0, OP.mult, FK, ["wP"], 192)
-    TS(CW[:, 384:768], CF[:, 0:384], 2.0, OP.mult, FK, ["wQ"], 192)
-    TS(CW[:, 768:1152], CF[:, 384:768], 592.0, OP.mult, EK, ["wV"], 192)
-    CP(CW[:, 1152:1280], CF[:, 384:512], EK, ["wE"], 64)
-    for a in (0, 1, 2, 3, 6, 7, 8, 10, 11):
-        CP(T.NT[:, a * 256:a * 256 + 256], T.ON[0:9, 0:256], ["ON"], ["NT%d" % a], 128)
-    TS(T.CBIG[:, :], CB[:, 128:384], BIG, OP.mult, ["cPM", "cA1", "cB1"], ["CBIG"], 128)
-    TS(T.S8[:, :], CB[:, 896:1024:16], 8192.0, OP.mult, ["cEB"], ["S8"], 64)
-    TS(T.NEGI[:, :], IB, -1.0, OP.mult, ["cI"], ["NEGI"], 64)
-    QE, QO = ["QR%d" % k for k in range(0, 16, 2)], ["QR%d" % k for k in range(1, 16, 2)]
-    for k in list(range(0, 16, 2)) + list(range(1, 16, 2)):
-        if k % 4 < 2:
-            CP(T.QR[:, k::16], T.Q[:, :], ["Q"], ["QR%d" % k], 128)
+    CP(CH[:, 0:144], CB[:, 0:144], ["cI"], ["hI"], 72)
+    CP(CH[:, PMV:PMV + 128], CB[:, PMV:PMV + 128], ["cPV"], ["hPV"], 64)
+    CP(CH[:, PM0:PM0 + 128], CB[:, PM0:PM0 + 128], ["cP0"], ["hP0"], 64)
+    for z in (0, 1):
+        V(lambda e, z=z: e.tensor_reduce(CC[:, z:z + 1], CB[:, PM0 + 64 * z:PM0 + 64 * z + 64], AxisListType.X, OP.add), ["cP0"], ["cR%d" % z], 64)
+    for c in (0, 1):
+        for b in (0, 1):
+            x = 8 + 8 * (c - b)
+            TS(CH[:, 400 + (2 * c + b) * 128:528 + (2 * c + b) * 128], CH[:, x:x + 128], CC[:, c:c + 1], OP.mult, ["hI", "cR%d" % c], ["hP4%d%d" % (c, b)], 64)
+    TS(CC[0:17, 2:3], CB[0:17, 24:25], 0.5, OP.mult, ["cI"], ["cH"], 64)
+    TS(CC[0:17, 3:4], CB[0:17, 24:25], 1.0 / 594.0, OP.mult, ["cI"], ["cH2"], 64)
+    TS(CW[:, 0:128], CF[:, 0:128], CC[0:17, 2:3], OP.add, ["cE0", "cH"], ["w01"], 64, 4.0, OP.mult)
+    TS(CW[:, 128:256], CF[:, 0:128], CC[0:17, 3:4], OP.add, ["cE0", "cH2"], ["w02"], 64, 594.0, OP.mult)
+    CP(CW[:, 256:384], CF[:, 0:128], ["cE0"], ["w03"], 64)
+    TS(CW[:, 384:640], CF[:, 128:384], CC[0:17, 2:3], OP.add, ["cEB", "cH"], ["wP"], 128, 4.0, OP.mult)
+    TS(CW[:, 640:896], CF[:, 128:384], CC[0:17, 2:3], OP.add, ["cEB", "cH"], ["wQ"], 128, 2.0, OP.mult)
+    TS(CW[:, 896:1152], CF[:, 128:384], 592.0, OP.mult, ["cEB"], ["wV"], 128)
+    CP(CW[:, 1152:1408], CF[:, 128:384], ["cEB"], ["wE"], 128)
+    TS(T.XJ[:, 0:8], T.XI[:, 0:8], 4, OP.arith_shift_right, ["XI"], ["XJ"], 64)
+    TS(T.S8[:, :], T.XJ[:, 0:8], 0.0, OP.is_equal, ["XJ"], ["S8"], 64, 8192.0, OP.mult)
+    fill(T.CR[0:32, :], 0.0, ["CR"], ["CR"], 128)
+    fill(T.CR[0:1, :], -16711680.0, ["CR"], ["CR"], 128)
+    TS(NEGI, IB, -1.0, OP.mult, ["cI"], ["NEGI"], 64)
+    TS(BIGI, IB, BIG, OP.mult, ["cI"], ["BIGI"], 64)
+    TS(BIGP, CB[:, PM0:PM0 + 128], BIG, OP.mult, ["cP0"], ["BIGP"], 64)
+    fill(T.DZ[:, :], -BIG, [], ["DZ"], 128)
+    for c in "01":
+        fill(T["D" + c][:, :], -BIG, [], ["D" + c], 256)
+        TS(T["D" + c][:, 8::16], T.RS[:, :], 2047.0, OP.add, ["RS", "D" + c], ["D" + c], 64)
+    QZ, QA = ["QZ%d" % k for k in range(8)], ["QR%d" % k for k in range(32)]
+    for k in range(8):
+        if k % 2:
+            CP(T.QZ[:, k::8], T.Q[:, :], ["Q"], [QZ[k]], 128)
         else:
-            S(T.QR[:, k::16], T.Q[:, :], FN.Copy, ["Q"], ["QR%d" % k], 256)
-    QA = QE + QO
-    CP(T.VH[:, :], T.VS[:, :], ["VS"], ["VH"], 1024)
+            S(T.QZ[:, k::8], T.Q[:, :], FN.Copy, ["Q"], [QZ[k]], 256)
+    for b in (0, 1):
+        for k in range(16):
+            o, i = T.QR[:, b * 2048 + k:b * 2048 + 2048:16], T.Q[:, b::2]
+            if k % 3:
+                CP(o, i, ["Q"], [QA[b * 16 + k]], 64)
+            else:
+                S(o, i, FN.Copy, ["Q"], [QA[b * 16 + k]], 128)
+    for h, bn in ((0, "wB"), (1, "kB")):
+        for z in range(4):
+            x = PMV + (h * 4 + z) * 16
+            MM(PS[bn][0:16, z * 128:z * 128 + 128], CH[:, x:x + 16], I16, True, True, ["hPV", "hI"], ["#" + bn], 16, 128)
+        CP(T.VH[:, h * 512:h * 512 + 512], PS[bn][0:16, :], ["#" + bn], ["VH%d" % h], 512)
 
-    def late_constants():
-        CP(CH[0:80, 1104:1232], CB[0:80, 1104:1232], ["cPR"], ["hPR"], 64)
-        CP(CH[0:80, 1360:2512], CB[0:80, 1232:2384], ["cPS"] + ["cPT%d" % z for z in range(8)], ["hPS"], 576)
-        TTo(CW[:, 1280:1408], CF[:, 384:512], CF[:, 896:1024], OP.add, EK + ["cM1"], ["wM"], 256)
-        TS(T.MT0[:, :], T.MT0[:, :], 1.0, OP.min, ["MT0"], ["MT0"], 64)
+    PR1, PR2, PTZ, PAB, I2, I592, I4K, NI4K, DM, NDM = 912, 1040, 1168, 1680, 0, 128, 256, 384, 1936, 2064
+
+    def ring_constants():
+        fill(T.ON[:, 256:2048], 1.0, ["ON"], ["ONb"], 896)
+        fill(T.TO[:, 2048:2064], 0.0, [], ["TOz"], 64)
+        fill(T.TO1[:, 2048:2064], 0.0, [], ["TO1z"], 64)
+        iota(T.IO[:, :], [[1, 128]], 0, 0, [], ["IO"], 128)
+        eqs(CB, 400, [[-1, 8], [-16, 8], [-8, 2]], 0, "cR1", 80)
+        eqs(CB, 528, [[-1, 8], [-16, 8], [-8, 2]], 80, "cR2", 80)
+        for z in range(4):
+            eqs(CB, 656 + z * 128, [[-1, 8], [1000, 4], [-8, 4]], -48 - 1000 * z, "cZ%d" % z, 80)
+        eqs(CB, 1168, [[-8, 2], [-1, 8], [-16, 16]], 0, "cAB", 96)
+        CP(CH[0:80, PR1:PR1 + 768], CB[0:80, 400:1168], ["cR1", "cR2"] + ["cZ%d" % z for z in range(4)], ["hPR"], 384)
+        CP(CH[0:96, PAB:PAB + 256], CB[0:96, 1168:1424], ["cAB"], ["hAB"], 128)
+        TTo(CH[:, DM:DM + 128], CB[:, 8:136], CB[:, 7:135], OP.subtract, ["cI"], ["hDM"], 256)
+        TTo(CH[:, NDM:NDM + 128], CB[:, 7:135], CB[:, 8:136], OP.subtract, ["cI"], ["hND"], 256)
+        for b in (0, 1):
+            GC(lambda b=b: g.iota(T.XI[:, 16 + b * 80:96 + b * 80], [[0, 5], [1000, 2], [-16, 8]], -1000 * b, 1), [], ["XI%d" % b], 80)
+        TS(T.XJ[:, 16:176], T.XI[:, 16:176], 4, OP.arith_shift_right, ["XI0", "XI1"], ["XJb"], 160)
+        TS(T.RC[:, :], T.XJ[:, 16:176], 0.0, OP.is_equal, ["XJb"], ["RC"], 160, -4096.0, OP.mult)
+        eqs(T.RT, 0, [[-1, 80], [0, 16]], 0, "RT", 97)
+        iota(T.RT[96:97, :], [[0, 80], [-128, 16]], -128, 0, ["RT"], ["RT"], 1280)
+        CP(T.RH[:, :], T.RT[:, :], ["RT"], ["RH"], 640)
+        eqs(T.SELL, 0, [[-8, 16], [-1, 8], [0, 16]], 0, "SELL")
+        S(T.SELL[:, :], T.SELL[:, :], FN.Copy, ["SELL"], ["SELL"], 2048, scale=-512.0)
+        iota(T.IX[0:1, 0:400], [[0, 16], [8, 5], [1, 5]], 9, 0, [], ["IX"], 400)
+        fill(T.IX[0:1, 0:400:25], 64.0, ["IX"], ["IX"], 64)
+        fill(T.IX[0:1, 400:528], 34816.0, [], ["IXc"], 64)
+        fill(T.IX[0:1, 528:544], 1.0, [], ["IXd"], 64)
+        fill(T.JD[:, :], 0.0, [], ["JD"], 200)
+        fill(T.JD[:, 0::25], 64.0, ["JD"], ["JD"], 64)
+        for x, f in ((I2, 2.0), (I592, 592.0), (I4K, 4096.0), (NI4K, -4096.0)):
+            TS(T.SI[:, x:x + 128], I16, f, OP.mult, ["hI"], ["SI%d" % x], 64)
         CP(T.THF[:, :], T.TH[:, :], ["TH"], ["THF"], 64)
-        fill(T.VV[:, 0:16], 0.0, [], ["VV0"], 64)
-        fill(T.VV[:, 160:176], 0.0, [], ["VV10"], 64)
-        TTo(CH[:, 1232:1360], IB, CT[:, 336:464], OP.subtract, ["cI", "cSF"], ["hDM"], 256)
-        fill(T.TM[:, :], 0.0, [], ["TMz"], 64)
-        fill(T.TM[96:97, :], 1.0, ["TMz"], ["TMz"], 64)
-        fill(T.CS[:, 128:132], 0.0, [], ["CSz"], 64)
-        fill(T.CS[:, 129:130], 100.0, ["CSz"], ["CSz"], 64)
-        x = 0
-        for L in range(3, 11):
-            for i in range(max(1, L - 5), min(5, L - 1) + 1):
-                fill(T.WT[:, x:x + 16], float(25 - (i - 1) * 5 - (L - i - 1)), [], ["WT%d" % x], 64)
-                x += 16
+        fill(T.TM[:, :], 0.0, [], ["TMz"], 128)
+        fill(T.TM[96:97, :], 1.0, ["TMz"], ["TMz"], 128)
+        fill(T.C2[:, 0:8], 0.0, [], ["C2y"], 64)
+        fill(T.C2[:, 136:144], 0.0, [], ["C2z"], 64)
+        fill(CC[:, 4:5], -100.0, [], ["c100"], 64)
+        GC(lambda: g.iota(T.JI[:, 48:56], [[0, 8]], 0, 1), [], ["cm"], 8)
+        TS(T.JI[:, 56:64], T.JI[:, 48:56], 15, OP.bitwise_and, ["cm"], ["cm2"], 64)
+        for j in range(6):
+            TS(CC[:, 8 + j:9 + j], T.JI[:, 56:57], float(j) if j < 5 else 0.5, OP.add, ["cm2"], ["cM%d" % j], 64)
 
     n = len(T.cores)
     r = T.rank_of(core)
     its = items(r, T, topo)
 
-    def send(k):
+    def send(k, after=()):
         buf, c0, c1, land, asem, dst, rel = its[k]
 
         def fn():
@@ -299,7 +305,7 @@ def build(g, core, T, topo):
                 remote(g, T, topo, core, dst, T[land][:, c0:c1], T[buf][:, c0:c1], asem, "lo%d" % k)
             else:
                 remote(g, T, topo, core, rel, T[land][:, c0:c1], T[buf][:, c0:c1], "ri%d" % k, "lo%d" % k)
-        op("g", fn, [buf], [], 0.5, "r", "lo%d" % k, len(topo.engines(core, dst if rel is None else rel)))
+        op("g", fn, [buf] + list(after), ["sent%d" % k], 0.5 if k else 2.5, "r", "lo%d" % k, len(topo.engines(core, dst if rel is None else rel)))
 
     def arrive(land, asem, giver, lat, after):
         tot = 0
@@ -307,127 +313,135 @@ def build(g, core, T, topo):
             if it[4] == asem:
                 tot += len(topo.engines(T.cores[giver] if it[6] is None else it[6], core))
         op(None, None, after, [land], 0.0, "x", asem, tot, lat)
-    for k in range(6):
+    for k in range(4):
         send(k)
-    arrive("TP0", "aTP0", (r + 1) % n, 14.0, ["TO"])
-    arrive("TPn", "aTPn", (r + 2) % n, 25.0, ["TO"])
+    arrive("TP0", "aTP0", (r + 1) % n, PLAN["tp0"], ["sent%d" % k for k in range(4)])
 
     NB = T.NB[:, 0:1024]
 
-    def nt(c, a):
-        return 0 if a == 0 else (a if c == 0 else 5 + a)
+    def nt(t, c, a):
+        return t if a == 0 else (1 + a if c == 0 else 6 + a)
 
-    def NTs(s, rows=9):
-        return T.NT[0:rows, s * 256:s * 256 + 256]
+    def NTs(s, rows=17):
+        return T.NT[0:rows, s * 128:s * 128 + 128]
+
+    def offsets(C, w):
+        TS(T["B" + C][:, 0:w], T["T" + C][:, 0:w], 4, OP.arith_shift_right, ["T" + C], ["B" + C], w, 2047, OP.bitwise_and)
+        CP(T["OF" + C][:, 0:w], T["B" + C][:, 0:w], ["B" + C], ["OF" + C], w)
 
     def start(t):
         P = "PT%d" % t
-        vl = T.SU[:, t * 16:t * 16 + 16]
-        V(lambda e: e.tensor_copy(T.X0B[:, :], T.XI[:, 0:1024].indirect(vl)), ["XI0", "XI1", "XI2", "XI3", "SU"], ["X0B"], 384)
-        X = PS["xA"]
-        MM(X[0:8, 0:256], CH[:, 128:136], T.X0B[:, :], True, True, ["hPM", "X0B"], ["#xA"], 8, 256)
-        for b in (0, 1):
-            MM(X[:, 256 + b * 8:264 + b * 8], T.X0B[:, b * 128:b * 128 + 128], CH[:, 128:136], True, True, ["hPM", "X0B"], ["#xA"], 128, 8)
-        CP(T.NT[0:8, 0:256], X[0:8, 0:256], ["#xA"], ["NT0"], 256)
-        for b in (0, 1):
-            CP(T[P][:, 80 + b:96:2], X[:, 256 + b * 8:264 + b * 8], ["#xA"], [P + "s5"], 64)
-        V(lambda e: e.tensor_copy(T.NN0[:, :], NB.indirect(vl)), ["NB", "SU"], ["NN0"], 384)
+        X = PS["dA"]
+        for z in range(8):
+            MM(X[0:16, z:128:8], CH[:, PMV + z * 16:PMV + z * 16 + 16], T.STH[:, t * 16:t * 16 + 16], True, True, ["hPV", "STH"], ["#dA"], 16, 16)
+        CP(NTs(t, 16), X[0:16, 0:128], ["#dA"], ["NT%d" % t], 128)
+        MM(X[:, 128:144], NTs(t, 16), CH[0:16, 8:24], True, True, ["NT%d" % t, "hI"], ["#dA"], 128, 16)
+        CP(T[P][:, 80:96], X[:, 128:144], ["#dA"], [P + "s5"], 64)
+        TTo(T.DZ[:, 0::8], T[P][:, 80:96], T.RS[:, :], OP.add, [P + "s5", "RS", "DZ"], ["DZ"], 64)
+        V(lambda e: e.tensor_copy(T.NZ[:, :], NB.indirect(T.SU[:, t * 16:t * 16 + 16])), ["NB", "SU"], ["NZ"], 256 * GAT)
+        for c, bn in ((0, "dA"), (1, "dB")):
+            C, X = str(c), PS[bn]
+            bon[0] = PLAN["lead"] * (1 - c)
+            for b in (0, 1):
+                x = 400 + (2 * c + b) * 128
+                MM(X[:, 0:128], CH[:, x:x + 128], T.NZ[:, b::2], b == 0, b == 1, ["hP4%d%d" % (c, b), "NZ"], ["#" + bn], 128, 128)
+            for z in range(3):
+                MM(X[:, 128 + z * 128:256 + z * 128], CW[:, z * 128:z * 128 + 128], NTs(t), True, True, ["w0%d" % (z + 1), "NT%d" % t], ["#" + bn], 128, 128)
+            np_ = T["NP" + C][:, :]
+            CP(np_, X[:, 0:128], ["#" + bn], ["NP" + C], 128)
+            TTo(T["M" + C][:, 0:128], np_, X[:, 128:256], OP.mult, ["NP" + C, "#" + bn], ["M%s0" % C], 128)
+            TTo(T["T" + C][:, 0:128], T["M" + C][:, 0:128], X[:, 256:384], OP.add, ["M%s0" % C, "#" + bn], ["T" + C], 128)
+            TTo(T["BQ" + C][:, 0:128], np_, X[:, 384:512], OP.is_equal, ["NP" + C, "#" + bn], ["BQ%s0" % C], 128)
+            offsets(C, 128)
+        bon[0] = 0.0
 
     def step(t, c, a, tab, tkey):
         C = str(c)
         P = "PT%d" % t
-        bon[0] = LEAD * (1 - c)
+        bon[0] = PLAN["lead"] * (1 - c)
         kb, wb, xb, db = ("kA", "wA", "xA", "dA") if c == 0 else ("kB", "wB", "xB", "dB")
         K, W, X, D = PS[kb], PS[wb], PS[xb], PS[db]
         KB, WB, XB, DB = "#" + kb, "#" + wb, "#" + xb, "#" + db
-        nn, nnk = (T.NN0, "NN0") if a == 0 else (T["NN" + C], "NN" + C)
+        nn, nnk = T["NN" + C], "NN" + C
+        nv = NV[a]
+        tot, qr, QK = (2048, T.QZ, QZ) if a == 0 else (4096, T.QR, QA)
 
         def sl(i):
             return 5 + i if c == 0 else 5 - i
-        if a == 0:
-            w = 128
-            p0 = 384 + 256 * c
-            MM(X[:, 0:128], CH[:, p0:p0 + 128], nn[:, 0::2], True, False, ["hP4", nnk], [XB], 128, 128)
-            MM(X[:, 0:128], CH[:, p0 + 128:p0 + 256], nn[:, 1::2], False, True, ["hP4", nnk], [XB], 128, 128)
-            E, O = T.NT[:, 0:256:2], T.NT[:, 1:256:2]
-            MM(W[:, 0:128], CW[:, 128:256], E, True, False, ["wP", "NT0"], [WB], 128, 128)
-            MM(W[:, 0:128], CW[:, 256:384], O, False, True, ["wP", "NT0"], [WB], 128, 128)
-            for z, (q0, src) in enumerate(((512, E), (640, O), (896, E), (1024, O))):
-                MM(W[:, 256:384], CW[:, q0:q0 + 128], src, z == 0, z == 3, ["wQ", "wV", "NT0"], [WB], 128, 128)
-            S(T["NPK" + C][:, :], X[:, 0:128], FN.Copy, [XB], ["NPK" + C], 128)
-            src, sk = T["NPK" + C][:, :], "NPK" + C
-            parts = ((1024, 512, "s"), (1536, 512, "s"), (0, 512, "v"), (512, 512, "v"))
-        else:
-            w = 256
-            V(lambda e: e.tensor_copy(nn[:, :], NB.indirect(T["VL" + C][:, 0:16])), ["NB", "VL" + C], [nnk], 384)
-            s0, s1 = nt(c, a - 1), nt(c, a)
-            MM(W[:, 0:256], CW[:, 0:128], NTs(s0), True, True, ["wP", "NT%d" % s0], [WB], 128, 256)
-            MM(W[:, 256:512], CW[:, 384:512], NTs(s0), True, False, ["wQ", "NT%d" % s0], [WB], 128, 256)
-            MM(W[:, 256:512], CW[0:8, 768:896], NTs(s1, 8), False, True, ["wV", "NT%d" % s1], [WB], 128, 256)
-            src, sk = nn[:, :], nnk
-            parts = tuple((z, 512, "s") for z in (2560, 3072, 3584)) + tuple((z, 512, "v") for z in range(0, 2560, 512))
-        TTo(T["M" + C][:, 0:w], src, W[:, 0:w], OP.mult, [sk, WB], ["M" + C], w)
-        TTo(T["T" + C][:, 0:w], T["M" + C][:, 0:w], W[:, 256:256 + w], OP.add, ["M" + C, WB], ["T" + C], w)
-        TS(T["B" + C][:, 0:w], T["T" + C][:, 0:w], 4, OP.arith_shift_right, ["T" + C], ["B" + C], w, 2047, OP.bitwise_and)
-        CP(T["OF" + C][:, 0:w], T["B" + C][:, 0:w], ["B" + C], ["OF" + C], w)
+        if a:
+            V(lambda e: e.tensor_copy(nn[:, :], NB.indirect(T["VL" + C][:, 0:16])), ["NB", "VL" + C], [nnk], 256 * GAT)
+            s0, s1 = nt(t, c, a - 1), nt(t, c, a)
+            for b in (0, 1):
+                y = b * 128
+                MM(W[:, y:y + 128], CW[:, 384 + y:512 + y], NTs(s0), True, True, ["wP", "NT%d" % s0], [WB], 128, 128)
+            for b in (0, 1):
+                y = b * 128
+                MM(W[:, 256 + y:384 + y], CW[:, 640 + y:768 + y], NTs(s0), True, False, ["wQ", "NT%d" % s0], [WB], 128, 128)
+                MM(W[:, 256 + y:384 + y], CW[0:16, 896 + y:1024 + y], NTs(s1, 16), False, True, ["wV", "NT%d" % s1], [WB], 128, 128)
+            for b in (0, 1):
+                y = b * 128
+                TTo(T["M" + C][:, y:y + 128], nn[:, b::2], W[:, y:y + 128], OP.mult, [nnk, WB], ["M%s%d" % (C, b)], 128)
+            TTo(T["T" + C][:, :], T["M" + C][:, :], W[:, 256:512], OP.add, ["M%s0" % C, "M%s1" % C, WB], ["T" + C], 256)
+            offsets(C, 256)
         win = tab[:, 0:2048]
         dv, ab, xg = T["DV" + C], T["AB" + C], T["XG" + C]
+        parts, p = [], tot
+        while p > nv:
+            parts.insert(0, (max(nv, p - 512), p, "s"))
+            p = parts[0][0]
+        parts += [(z, min(nv, z + 512), "v") for z in range(0, nv, 512)]
 
-        def keys(nm, p, ln):
-            return ["%s%s.%d" % (nm, C, z) for z in range(p // 512, (p + ln) // 512)]
-
-        def qv(p, ln):
-            return T.QR[:, 2 * p:2 * p + 2 * ln:2] if a == 0 else T.QR[:, p:p + ln]
-        QK = QE if a == 0 else QA
-        for p, ln, e in parts:
-            off = T["OF" + C][:, p // 16:(p + ln) // 16]
+        def keys(nm, p0, p1):
+            return ["%s%s.%d" % (nm, C, z) for z in range(p0 // 128, (p1 + 127) // 128)]
+        for p0, p1, e in parts:
+            off = T["OF" + C][:, p0 // 16:p1 // 16]
             if e == "v":
-                V(lambda en, p=p, ln=ln, off=off: en.tensor_tensor(dv[:, p:p + ln], win.indirect(off), qv(p, ln), OP.subtract),
-                  ["OF" + C, tkey] + QK, keys("dv", p, ln), ln * 1.5)
+                V(lambda en, p0=p0, p1=p1, off=off: en.tensor_tensor(dv[:, p0:p1], win.indirect(off), qr[:, p0:p1], OP.subtract),
+                  ["OF" + C, tkey] + QK, keys("dv", p0, p1), (p1 - p0) * GAT)
             else:
-                op("s", lambda p=p, ln=ln, off=off: g.scalar.activation(xg[:, p % 2048:p % 2048 + ln], win.indirect(off), FN.Copy),
-                   ["OF" + C, tkey], keys("XG", p % 2048, ln), ln * 1.5 * CY + 0.07)
-        MM(K[:, 0:256], T.ON[0:33, 0:128], T.CR[:, 256 * (a == 0):256 * (a == 0) + 256], True, False, ["ON", "CR"], [KB], 128, 256)
-        pc, pw, bc = (256 + 64 * c, 64, 128 + 64 * c) if a == 0 else (128, 128, 0)
-        for b in (0, 1):
-            MM(K[:, b * 128:b * 128 + pw], nn[:, b * 128:b * 128 + 128], CH[:, pc:pc + pw], False, False, [nnk, "hPM", "hF1"], [KB], 128, pw)
-        for p, ln, e in parts:
+                SG(xg[:, p0 - nv:p1 - nv], win.indirect(off), ["OF" + C, tkey], keys("XG", p0 - nv, p1 - nv), p1 - p0)
+        kw = tot // 16
+        MM(K[:, 0:kw], T.ON[0:33, 0:128], T.CR[:, 0:kw], True, False, ["ON", "CR"], [KB], 128, kw)
+        BQ = T["BQ" + C]
+        if a == 0:
+            MM(K[:, 0:128], T["NP" + C][:, :], CH[:, PM0:PM0 + 128], False, False, ["NP" + C, "hP0"], [KB], 128, 128)
+            MM(K[:, 0:128], BQ[:, 0:128], BIGP, False, False, ["BQ%s0" % C, "BIGP"], [KB], 128, 128)
+        else:
+            for b in (0, 1):
+                MM(K[:, b * 128:b * 128 + 128], nn[:, b::2], I16, False, False, [nnk, "hI"], [KB], 128, 128)
+        for p0, p1, e in parts:
             if e == "v":
-                S(ab[:, p:p + ln], dv[:, p:p + ln], FN.Abs, keys("dv", p, ln), keys("ab", p, ln), ln)
+                S(ab[:, p0:p1], dv[:, p0:p1], FN.Abs, keys("dv", p0, p1), keys("ab", p0, p1), p1 - p0)
             else:
-                MM(D[:, :], IB, xg[:, p % 2048:p % 2048 + 512], True, False, ["cI"] + keys("XG", p % 2048, 512), [DB], 128, 512)
-                MM(D[:, :], T.NEGI[:, :], qv(p, 512), False, True, ["NEGI"] + QK, [DB], 128, 512)
-                S(ab[:, p:p + 512], D[:, :], FN.Abs, [DB], keys("ab", p, 512), 512)
+                w = p1 - p0
+                MM(D[:, 0:w], IB, xg[:, p0 - nv:p1 - nv], True, False, ["cI"] + keys("XG", p0 - nv, p1 - nv), [DB], 128, w)
+                MM(D[:, 0:w], NEGI, qr[:, p0:p1], False, True, ["NEGI"] + QK, [DB], 128, w)
+                S(ab[:, p0:p1], D[:, 0:w], FN.Abs, [DB], keys("ab", p0, p1), w)
 
         def score(b, last):
-            stp = 8 if a == 0 else 16
-            base = b * 128 * stp
-            for k in range(stp):
-                col = b * 128 + (k * 8 if a == 0 else (k % 8) * 16 + (k // 8) * 8)
-                MM(K[:, col:col + 8], ab[:, base + k:base + 128 * stp:stp], T.S8[:, :], False, last and k == stp - 1,
-                   keys("ab", base, 128 * stp) + ["S8"], [KB], 128, 8)
+            for k in range(8 if a == 0 else 16):
+                if a == 0:
+                    o, l, kk = K[:, b * 64 + k:b * 64 + 64:8], ab[:, b * 8 + k:2048:16], keys("ab", 0, 2048)
+                else:
+                    o, l, kk = K[:, b * 128 + k:b * 128 + 128:16], ab[:, b * 2048 + k:b * 2048 + 2048:16], keys("ab", b * 2048, b * 2048 + 2048)
+                MM(o, l, T.S8[:, :], False, last and k == (7 if a == 0 else 15), kk + ["S8"], [KB], 128, 8)
         score(0, False)
-        BQ = T["BQ" + C]
-        for j in range(a + 1):
-            s = nt(c, j)
+        for j in range(a + 1 if a else 0):
+            s = nt(t, c, j)
             x0, j0 = (j % 2) * 256, j * 256
-            MM(X[:, x0:x0 + 256], CW[0:8, 1152:1280], NTs(s, 8), True, True, ["wE", "NT%d" % s], [XB], 128, 256)
+            for b in (0, 1):
+                MM(X[:, x0 + b:x0 + 256:2], CW[0:16, 1152 + b * 128:1280 + b * 128], NTs(s, 16), True, True, ["wE", "NT%d" % s], [XB], 128, 128)
             bk = "BQ%s%d" % (C, j)
             TTo(BQ[:, j0:j0 + 256], nn[:, :], X[:, x0:x0 + 256], OP.is_equal, [nnk, XB], [bk], 256)
             for b in (0, 1):
-                MM(K[:, b * 128:b * 128 + pw], BQ[:, j0 + b * 128:j0 + b * 128 + 128], T.CBIG[:, bc:bc + pw], False, False, [bk, "CBIG"], [KB], 128, pw)
+                MM(K[:, b * 128:b * 128 + 128], BQ[:, j0 + b:j0 + 256:2], BIGI, False, False, [bk, "BIGI"], [KB], 128, 128)
         score(1, True)
-        KD = T["KD" + C]
-        TS(KD[:, 0:16], T[P][:, sl(a) * 16:sl(a) * 16 + 16], REST, OP.add, [P + "s%d" % sl(a)], ["KR" + C], 64)
-        h = 32 if a == 0 else 64
-        SBt, L1, L2, Kt, Rt, SHt = T["SB" + C], T["L1" + C], T["L2" + C], T["K" + C], T["R" + C], T["SH" + C]
-        for b in (0, 1):
-            S(SBt[:, b * 64:b * 64 + h], K[:, b * 128 + h:b * 128 + 2 * h], FN.Copy, [KB], ["SB%s%d" % (C, b)], h)
-        for b in (0, 1):
-            TTo(L1[:, b:2 * h:2], K[:, b * 128:b * 128 + h], SBt[:, b * 64:b * 64 + h], OP.min, [KB, "SB%s%d" % (C, b)], ["L1%s%d" % (C, b)], h)
-        TTo(L2[:, 0:h], L1[:, 0:h], L1[:, h:2 * h], OP.min, ["L1%s0" % C, "L1%s1" % C], ["L2" + C], 2 * h)
-        TTo(Kt[:, 0:h // 2], L2[:, 0:h // 2], L2[:, h // 2:h], OP.min, ["L2" + C], ["K" + C], h)
-        TTo(Kt[:, 0:16], Kt[:, 0:16], KD[:, 0:16], OP.min, ["K" + C, "KR" + C], ["K" + C], 64)
+        SC, KD, Kt, Rt, SHt = T["SC" + C], T["KD" + C], T["K" + C], T["R" + C], T["SH" + C]
+        dd, dk = (T.DZ, "DZ") if a == 0 else (T["D" + C], "D" + C)
+        if a:
+            TTo(dd[:, 0::16], T[P][:, sl(a) * 16:sl(a) * 16 + 16], T.RS[:, :], OP.add, [P + "s%d" % sl(a), "RS", dk], [dk], 64)
+        V(lambda e: e.tensor_tensor_scan(SC[:, 0:kw], dd[:, 0:kw], K[:, 0:kw], -BIG, OP.max, OP.min), [dk, KB], ["SC" + C], kw)
+        CP(Kt[:, 0:kw // 8], SC[:, 7:kw:8], ["SC" + C], ["K" + C], 64)
         ns = sl(a + 1)
         out, ok = T[P][:, ns * 16:ns * 16 + 16], P + "s%d" % ns
         if a == 0:
@@ -436,23 +450,25 @@ def build(g, core, T, topo):
         else:
             TS(SHt[:, :], Kt[:, :], 13, OP.arith_shift_right, ["K" + C], ["SH" + C], 64)
             TS(Rt[:, :], Kt[:, :], 1023, OP.bitwise_and, ["K" + C], ["R" + C], 64)
-            TTo(KD[:, 16:32], SHt[:, 0:16], SHt[:, 16:32], OP.is_gt, ["SH" + C], ["SL" + C], 64)
-            TTo(KD[:, 32:48], Rt[:, 16:32], Rt[:, 0:16], OP.subtract, ["R" + C], ["DF" + C], 64)
-            TTo(KD[:, 48:64], KD[:, 32:48], KD[:, 16:32], OP.mult, ["DF" + C, "SL" + C], ["D2" + C], 64)
-            TTo(out, Rt[:, 0:16], KD[:, 48:64], OP.add, ["R" + C, "D2" + C], [ok], 64)
+            TTo(KD[:, 0:16], SHt[:, 0::2], SHt[:, 1::2], OP.is_gt, ["SH" + C], ["SL" + C], 64)
+            TTo(KD[:, 16:32], Rt[:, 1::2], Rt[:, 0::2], OP.subtract, ["R" + C], ["DF" + C], 64)
+            TTo(KD[:, 32:48], KD[:, 16:32], KD[:, 0:16], OP.mult, ["DF" + C, "SL" + C], ["D2" + C], 64)
+            TTo(out, Rt[:, 0::2], KD[:, 32:48], OP.add, ["R" + C, "D2" + C], [ok], 64)
         if a < 4:
-            s = nt(c, a + 1)
-            for b in (0, 1):
-                MM(X[0:8, b * 128:b * 128 + 128], T[P][:, ns * 16 + b:ns * 16 + 16:2], I16, True, True, [ok, "hI"], [XB], 8, 128)
-            CP(NTs(s, 8), X[0:8, 0:256], [XB], ["NT%d" % s], 256)
-            for i in range(16):
-                MM(X[:, 256:272], T.VH[:, i * 128:i * 128 + 128], T.NT[0:8, s * 256 + i:s * 256 + 256:16], i == 0, i == 15, ["VH", "NT%d" % s], [XB], 128, 16)
+            s = nt(t, c, a + 1)
+            MM(X[0:16, 0:128], out, I16, True, True, [ok, "hI"], [XB], 16, 128)
+            CP(NTs(s, 16), X[0:16, 0:128], [XB], ["NT%d" % s], 128)
+            for i in range(8):
+                MM(X[:, 256:272], T.VH[:, i * 128:i * 128 + 128], T.NT[0:16, s * 128 + i:s * 128 + 128:8], i == 0, i == 7,
+                   ["VH%d" % (i // 4), "NT%d" % s], [XB], 128, 16)
             CP(T["VL" + C][:, :], X[:, 256:272], [XB], ["VL" + C], 64)
         bon[0] = 0.0
 
     def lesser(el, tab, tk):
-        TS(T.TMP[:, :], tab[:, 0:2048], 0.75, OP.mult, [tk], ["TMP"], 1024, 1024.375, OP.add)
-        TS(T[el][:, :], T.TMP[:, :], -1024.0, OP.add, ["TMP"], [el], 1024)
+        for h in (0, 1):
+            y = h * 1024
+            TS(T.TMP[:, y:y + 1024], tab[:, y:y + 1024], 0.75, OP.mult, [tk], ["TMP%d" % h], 512, 1024.375, OP.add)
+            TS(T[el][:, y:y + 1024], T.TMP[:, y:y + 1024], -1024.0, OP.add, ["TMP%d" % h], ["%s.%d" % (el, h)], 512)
 
     def lessen(tab, tk, mk, el, out, okey, banks):
         for qd in range(4):
@@ -462,205 +478,202 @@ def build(g, core, T, topo):
             for z in range(4):
                 tt = (qd * 4 + z) * 128
                 MM(B[:, z * 128:z * 128 + 128], T.SELL[:, tt:tt + 128], T[mk][:, :], False, z == 3, ["SELL", mk], ["#" + b], 128, 128)
-            TTo(out[:, qd * 512:qd * 512 + 512], B[:, :], T[el][:, qd * 512:qd * 512 + 512], OP.max, ["#" + b, el], ["%s%d" % (okey, qd)], 512)
+            TTo(out[:, qd * 512:qd * 512 + 512], B[:, :], T[el][:, qd * 512:qd * 512 + 512], OP.max, ["#" + b, "%s.%d" % (el, qd // 2)], ["%s%d" % (okey, qd)], 512)
 
     def hot(c0, c1, kz, hk):
         TS(T.WW[:, c0:c1], T.HH[:, c0:c1], 127, OP.bitwise_and, hk, ["WW" + kz], c1 - c0)
-        TS(T.WS[:, c0:c1], T.WW[:, c0:c1], -128.0, OP.add, ["WW" + kz], ["WS" + kz], c1 - c0)
-        if kz == "e":
-            S(T.WS[:, 160 + c0:160 + c1], T.WS[:, c0:c1], FN.Copy, ["WSe"], ["WB"], c1 - c0, bias=100.0, scale=200.0)
-        for col in sorted(range(c0, c1), key=lambda z: (z % 2, z % 16, z)):
-            o = T.OH[:, col * 128:col * 128 + 128]
-            if col // 16 in SHOT:
-                S(o, T.I128[:, :], FN.Sigmoid, ["I128", "WB"], ["OH%d" % col], 128, bias=T.WS[:, 160 + col:161 + col], scale=-200.0)
+        for m in range(c0 // 16, c1 // 16):
+            ws, ww = T.WS[:, m * 16:m * 16 + 16], T.WW[:, m * 16:m * 16 + 16]
+            if m in SHOT:
+                TS(ws, ww, -200.0, OP.mult, ["WW" + kz], ["WS%d" % m], 64, 100.0, OP.add)
             else:
-                TS(o, T.I128[:, :], T.WS[:, col:col + 1], OP.is_equal, ["I128", "WS" + kz], ["OH%d" % col], 64)
+                CP(ws, ww, ["WW" + kz], ["WS%d" % m], 64)
+        for col in sorted(range(c0, c1), key=lambda z: (z % 16, z)):
+            o, wk = T.OH[:, col * 128:col * 128 + 128], "WS%d" % (col // 16)
+            if col // 16 in SHOT:
+                S(o, T.IO[:, :], FN.Sigmoid, ["IO", wk], ["OH%d" % col], 128, bias=T.WS[:, col:col + 1], scale=200.0)
+            else:
+                TS(o, T.IO[:, :], T.WS[:, col:col + 1], OP.is_ge, ["IO", wk], ["OH%d" % col], 64)
 
     def rings(t, tab, tk):
         P = "PT%d" % t
-        pt, JS = T[P], T.JS
+        pt, JS, SI = T[P], T.JS, T.SI
         pk = [P + "s%d" % i for i in range(11)]
-        uk, hw = [P + "u%d" % i for i in range(3)], ["HHe", "HHx", "HHy"]
+        uk, hw = ["U%d" % i for i in range(3)], ["HHe", "HHx", "HHy"]
+
+        def slot(s):
+            return pt[:, s * 16:s * 16 + 16]
         for z, (c0, c1, kk) in enumerate(((16, 160, pk[1:10]), (0, 16, pk[0:1]), (160, 176, pk[10:11]))):
             TS(T.U[:, c0:c1], pt[:, c0:c1], 2.0, OP.mult, kk, [uk[z]], c1 - c0, 1.0, OP.add)
         for z, (c0, c1, kk, ku) in enumerate(((16, 128, pk[1:10], uk[0:1]), (0, 16, pk[0:3], uk[0:2]), (128, 144, pk[8:11], [uk[0], uk[2]]))):
             TTo(T.PR[:, c0:c1], T.U[:, c0:c1], T.U[:, c0 + 32:c1 + 32], OP.mult, ku, ["PR%d" % z], 2 * (c1 - c0))
-            TS(T.V5[:, c0:c1], pt[:, c0 + 16:c1 + 16], 592.0, OP.mult, kk, ["V5%d" % z], c1 - c0)
+            TS(T.V5[:, c0:c1], pt[:, c0 + 16:c1 + 16], 592.0, OP.mult, kk[1:2] if z else kk, ["V5%d" % z], c1 - c0)
             TTo(T.TT[:, c0:c1], T.PR[:, c0:c1], T.V5[:, c0:c1], OP.add, ["PR%d" % z, "V5%d" % z], ["TT%d" % z], 2 * (c1 - c0))
             TS(T.HH[:, c0:c1], T.TT[:, c0:c1], 4, OP.arith_shift_right, ["TT%d" % z], [hw[z]], c1 - c0, 2047, OP.bitwise_and)
+        TS(T.PX[:, 16:160], pt[:, 16:160], 1.0 / 2048, OP.mult, pk[1:10], ["PXa"], 144)
+        TS(T.PX[:, 160:176], slot(10), 1.0 / 2048, OP.mult, pk[10:11], ["PXb"], 64)
+        TTo(T.DX[:, 16:80], T.PX[:, 32:96], T.PX[:, 16:80], OP.subtract, ["PXa"], ["DXa"], 128)
+        TTo(T.DX[:, 80:144], T.PX[:, 80:144], T.PX[:, 96:160], OP.subtract, ["PXa"], ["DXb"], 128)
+        TTo(T.DX[:, 144:160], T.PX[:, 144:160], T.PX[:, 160:176], OP.subtract, ["PXa", "PXb"], ["DXc"], 64)
         hot(16, 128, "e", ["HHe"])
-        x = 0
-        ek = []
-        for L in range(3, 11):
-            i0 = max(1, L - 5)
-            m = (min(5, L - 1) - i0 + 1) * 16
-            a0, b0 = (5 + i0) * 16, (5 + i0 - L) * 16
-            TTo(T.EQ[:, x:x + m], pt[:, a0:a0 + m], pt[:, b0:b0 + m], OP.is_equal, pk, ["EQ%d" % L], 2 * m)
-            ek.append("EQ%d" % L)
-            x += m
-        TTo(T.EW[:, :], T.EQ[:, :], T.WT[:, :], OP.mult, ek + ["WT%d" % z for z in range(0, 384, 16)], ["EW"], 768)
-        TTo(T.E1[:, :], T.EW[:, 0:192], T.EW[:, 192:384], OP.max, ["EW"], ["E1"], 384)
-        TTo(T.E2[:, :], T.E1[:, 0:96], T.E1[:, 96:192], OP.max, ["E1"], ["E2"], 192)
-        TTo(T.E3[:, 0:48], T.E2[:, 0:48], T.E2[:, 48:96], OP.max, ["E2"], ["E3"], 96)
-        TTo(T.E3[:, 48:64], T.E3[:, 0:16], T.E3[:, 16:32], OP.max, ["E3"], ["E4"], 64)
-        JW, JF, JI, JU, JL, JJ, VJ, PJ = [JS[:, z * 16:z * 16 + 16] for z in range(8)]
-        TTo(JW, T.E3[:, 48:64], T.E3[:, 32:48], OP.max, ["E3", "E4"], ["JW"], 64)
-        TS(JF, JW, 0.5, OP.is_ge, ["JW"], ["JF"], 64)
-        TS(T.JR[:, :], JW, -0.2, OP.mult, ["JW"], ["JR"], 64, 5.6, OP.add)
-        TTo(JI, T.JR[:, :], JF, OP.mult, ["JR", "JF"], ["JI"], 64)
-        TS(JU, T.JR[:, :], -4.0, OP.mult, ["JR"], ["JU"], 64, 31.0, OP.add)
-        TTo(JL, JU, JW, OP.subtract, ["JU", "JW"], ["JL"], 64)
-        TTo(T.IL[:, 16:32], JL, JF, OP.mult, ["JL", "JF"], ["ILl"], 64)
-        TTo(JJ, T.IL[:, 16:32], JI, OP.subtract, ["ILl", "JI"], ["JJ"], 64)
-        for m in range(0, 5):
-            z = (5 + m) * 16
-            TS(T.VV[:, z:z + 16], JI, m + 0.5, OP.is_ge, ["JI"], ["VV%d" % (5 + m)], 64)
-            if m:
-                z = (5 - m) * 16
-                TS(T.VV[:, z:z + 16], JJ, m + 0.5, OP.is_ge, ["JJ"], ["VV%d" % (5 - m)], 64)
-        vk = ["VV%d" % i for i in range(11)]
-        MI, MJ = T.MI[:, 0:80], T.MI[:, 80:160]
-        TTo(MI, T.VV[:, 80:160], T.VV[:, 96:176], OP.subtract, vk, ["MI"], 160)
-        TTo(MJ, T.VV[:, 16:96], T.VV[:, 0:80], OP.subtract, vk, ["MJ"], 160)
-        TTo(T.JP[:, 0:80], MI, pt[:, 80:160], OP.mult, ["MI"] + pk, ["JP0"], 160)
-        TTo(T.JP[:, 80:160], MI, pt[:, 96:176], OP.mult, ["MI"] + pk, ["JP1"], 160)
-        TTo(T.JP[:, 160:240], MJ, pt[:, 16:96], OP.mult, ["MJ"] + pk, ["JP2"], 160)
+        J = PS["wA"]
+        MM(J[:, 0:400], T.ON[0:1, 0:128], T.IX[0:1, 0:400], True, False, ["ON", "IX"], ["#wA"], 128, 400)
+        terms = [(i, j, s) for i in range(1, 6) for j in range(1, 6) for s in (5 + i, 5 - j) if i + j > 2]
+        terms.sort(key=lambda x: (x[2] == 0, x[2] == 10))
+        for z, (i, j, s) in enumerate(terms):
+            x = I4K if s > 5 else NI4K
+            MM(J[:, (i - 1) * 5 + j - 1:400:25], SI[:, x:x + 128], slot(s), False, z == len(terms) - 1, ["SI%d" % x, pk[s]], ["#wA"], 128, 16)
+        S(T.JA[:, :], J[:, 0:400], FN.Abs, ["#wA"], ["JA"], 400)
+        V(lambda e: e.tensor_tensor_scan(T.JC[:, :], T.JD[:, :], T.JA[:, :], 0.0, OP.max, OP.min), ["JD", "JA"], ["JC"], 200)
+        JU, J0, JJ = T.JI[:, 0:16], T.JI[:, 16:32], T.JI[:, 32:48]
+        CP(JU, T.JC[:, 24::25], ["JC"], ["JU"], 64)
+        TS(J0, JU, 63, OP.bitwise_and, ["JU"], ["J0"], 64)
+        TS(JJ, JU, 7, OP.bitwise_and, ["JU"], ["JJ"], 64)
+        NM = T.NM
+        for m in range(1, 5):
+            TS(NM[:, (4 + m) * 16:(5 + m) * 16], J0, 8.0 * (m + 1), OP.is_lt, ["J0"], ["NM%d" % (4 + m)], 64, 2048.0, OP.mult)
+        for m in range(1, 5):
+            TS(NM[:, (4 - m) * 16:(5 - m) * 16], JJ, m + 1.0, OP.is_lt, ["JJ"], ["NM%d" % (4 - m)], 64, 2048.0, OP.mult)
+        TS(NM[:, 64:80], J0, 8.0, OP.is_lt, ["J0"], ["NM4"], 64, 2048.0, OP.mult)
+        nk = ["NM%d" % i for i in range(9)]
+        TTo(T.JP[:, 0:64], NM[:, 80:144], T.DX[:, 80:144], OP.mult, nk[5:9] + ["DXb"], ["JP0"], 128)
+        TTo(T.JP[:, 128:192], NM[:, 0:64], T.DX[:, 16:80], OP.mult, nk[0:4] + ["DXa"], ["JP2"], 128)
+        TTo(T.JP[:, 64:128], NM[:, 80:144], T.DX[:, 96:160], OP.mult, nk[5:9] + ["DXb", "DXc"], ["JP1"], 128)
         J = PS["kA"]
-        for z in range(3):
-            for k in range(5):
-                MM(J[:, z * 16:z * 16 + 16], I16, T.JP[:, z * 80 + k * 16:z * 80 + k * 16 + 16], k == 0, k == 4, ["hI", "JP%d" % z], ["#kA"], 128, 16)
-        TS(T.UJ[:, :], J[:, 0:48], 2.0, OP.mult, ["#kA"], ["UJ"], 64, 1.0, OP.add)
-        TS(VJ, J[:, 16:32], 592.0, OP.mult, ["#kA"], ["VJ"], 64)
-        TTo(PJ, T.UJ[:, 0:16], T.UJ[:, 32:48], OP.mult, ["UJ"], ["PJ"], 64)
-        TTo(T.TT[:, 144:160], PJ, VJ, OP.add, ["PJ", "VJ"], ["TTb"], 64)
+        for z, s, x in ((0, 9, I2), (2, 1, I2), (1, 10, I592)):
+            o = J[:, z * 16:z * 16 + 16]
+            MM(o, SI[:, x:x + 128], slot(s), True, False, ["SI%d" % x, pk[s]], ["#kA"], 128, 16)
+            if x == I2:
+                MM(o, T.ON[0:1, 0:128], T.IX[0:1, 528:544], False, False, ["ON", "IXd"], ["#kA"], 128, 16)
+            for k in range(4):
+                MM(o, SI[:, x:x + 128], T.JP[:, z * 64 + k * 16:z * 64 + k * 16 + 16], False, k == 3, ["SI%d" % x, "JP%d" % z], ["#kA"], 128, 16)
+        UA, PJ = JS[:, 0:16], JS[:, 16:32]
+        CP(UA, J[:, 0:16], ["#kA"], ["UA"], 64)
+        TTo(PJ, UA, J[:, 32:48], OP.mult, ["UA", "#kA"], ["PJ"], 64)
+        TTo(T.TT[:, 144:160], PJ, J[:, 16:32], OP.add, ["PJ", "#kA"], ["TTb"], 64)
         TS(T.HH[:, 144:160], T.TT[:, 144:160], 4, OP.arith_shift_right, ["TTb"], ["HHb"], 64, 2047, OP.bitwise_and)
-        hk = hw + ["HHb"]
-        TS(T.HS[:, :], T.HH[:, :], -2048.0, OP.add, hk, ["HS"], 160)
-        TTo(T.HV[:, 0:144], T.HS[:, 0:144], T.VV[:, 16:160], OP.mult, ["HS"] + vk, ["HVa"], 288)
-        TTo(T.HV[:, 144:160], T.HS[:, 144:160], T.VV[:, 80:96], OP.mult, ["HS"] + vk, ["HVb"], 64)
-        TS(T.TB[:, :], T.HH[:, :], 7, OP.arith_shift_right, hk, ["TB"], 160)
-        TS(T.TBP[:, :], T.TB[:, :], 2.0, OP.add, ["TB"], ["TBP"], 160)
-        TTo(T.TV[:, 0:144], T.TBP[:, 0:144], T.VV[:, 16:160], OP.mult, ["TBP"] + vk, ["TVa"], 288)
-        TTo(T.TV[:, 144:160], T.TBP[:, 144:160], T.VV[:, 80:96], OP.mult, ["TBP"] + vk, ["TVb"], 64)
+        TTo(T.HV[:, 0:80], T.HH[:, 0:80], NM[:, 0:80], OP.max, hw[0:2] + nk[0:5], ["HVa"], 160)
+        TTo(T.HV[:, 80:144], T.HH[:, 80:144], NM[:, 80:144], OP.max, [hw[0], hw[2]] + nk[5:9], ["HVb"], 128)
+        TTo(T.HV[:, 144:160], T.HH[:, 144:160], NM[:, 64:80], OP.max, ["HHb", "NM4"], ["HVc"], 64)
         X, X2 = PS["xA"], PS["xB"]
-        for b in (0, 1):
-            MM(X[0:80, b * 128:b * 128 + 128], T.HV[:, b::2], I16, True, True, ["HVa", "HVb", "hI"], ["#xA"], 80, 128)
-        CP(T.HT[:, :], X[0:80, 0:256], ["#xA"], ["HT"], 256)
-        MM(X2[:, 0:128], CH[0:80, 1104:1232], T.HT[:, 0::2], True, False, ["hPR", "HT"], ["#xB"], 128, 128)
-        MM(X2[:, 0:128], CH[0:80, 1360:1488], T.HT[:, 1::2], False, True, ["hPS", "HT"], ["#xB"], 128, 128)
-        for z in range(8):
-            MM(X2[:, 128:160], CH[64:80, 1488 + z * 128:1616 + z * 128], T.HT[64:80, z::8], z == 0, z == 7, ["hPS", "HT"], ["#xB"], 128, 32)
-        TS(T.OFR[:, 0:160], X2[:, 0:160], 2048.0, OP.add, ["#xB"], ["OFR"], 160)
+        MM(X[0:80, 0:128], T.HV[:, 0:80], I16, True, True, ["HVa", "hI"], ["#xA"], 80, 128)
+        CP(T.HT[:, 0:128], X[0:80, 0:128], ["#xA"], ["HT0"], 128)
+        MM(X[0:80, 128:256], T.HV[:, 80:160], I16, True, True, ["HVb", "HVc", "hI"], ["#xA"], 80, 128)
+        CP(T.HT[:, 128:256], X[0:80, 128:256], ["#xA"], ["HT1"], 128)
+        MM(X2[:, 0:128], CH[0:80, PR1:PR1 + 128], T.HT[:, 0:128], True, False, ["hPR", "HT0"], ["#xB"], 128, 128)
+        MM(X2[:, 0:128], CH[0:80, PR2:PR2 + 128], T.HT[:, 128:256], False, True, ["hPR", "HT1"], ["#xB"], 128, 128)
+        for z in range(4):
+            MM(X2[:, 128:160], CH[0:80, PTZ + z * 128:PTZ + z * 128 + 128], T.HT[:, 128 + z:256:4], z == 0, z == 3, ["hPR", "HT1"], ["#xB"], 128, 32)
+        CP(T.OFR[:, :], X2[:, 0:160], ["#xB"], ["OFR"], 160)
         win = tab[:, 0:2064]
-        for b in (1, 0):
-            for x0, ln in ((b * 1024, 1024), (2048 + b * 256, 256)):
+        for h in (1, 0):
+            for x0, ln in ((h * 1024, 1024), (2048 + h * 256, 256)):
                 xo, fo = T.XR[:, x0:x0 + ln], T.OFR[:, x0 // 16:(x0 + ln) // 16]
-                if b:
-                    op("s", lambda xo=xo, fo=fo: g.scalar.activation(xo, win.indirect(fo), FN.Copy), ["OFR", tk, tk + "z"], ["XR%d.%d" % (b, ln)], ln * 1.5 * CY + 0.07)
+                if h:
+                    SG(xo, win.indirect(fo), ["OFR", tk, tk + "z"], ["XR%d.%d" % (h, ln)], ln)
                 else:
-                    V(lambda e, xo=xo, fo=fo: e.tensor_copy(xo, win.indirect(fo)), ["OFR", tk, tk + "z"], ["XR%d.%d" % (b, ln)], ln * 1.5)
-        for b in (0, 1):
-            MM(X[0:80, b * 128:b * 128 + 128], T.TV[:, b::2], I16, True, True, ["TVa", "TVb", "hI"], ["#xA"], 80, 128)
-        S(T.TVL[:, :], X[0:80, 0:256], FN.Copy, ["#xA"], ["TVL"], 256)
-        hot(0, 16, "a", hk)
-        hot(128, 160, "b", hk)
-        B, W = PS["kB"], PS["wA"]
+                    V(lambda e, xo=xo, fo=fo: e.tensor_copy(xo, win.indirect(fo)), ["OFR", tk, tk + "z"], ["XR%d.%d" % (h, ln)], ln * GAT)
+        hot(0, 16, "a", hw[1:2])
+        hot(128, 144, "b", hw[2:3])
+        hot(144, 160, "c", ["HHb"])
+        B, W = PS["kB"], PS["wB"]
+        MM(W[0:80, 0:128], T.ON[0:1, 0:80], T.IX[0:1, 400:528], True, False, ["ON", "IXc"], ["#wB"], 80, 128)
         for b in (0, 1):
             for m in range(10):
-                xs = T.XR[:, b * 1024 + m:(b + 1) * 1024:8] if m < 8 else T.XR[:, 2040 + b * 256 + m:2304 + b * 256:2]
-                MM(B[:, b * 128:b * 128 + 128], IB, xs, m == 0, m == 9, ["cI", "XR%d.%d" % (b, 1024 if m < 8 else 256)], ["#kB"], 128, 128)
+                xs = T.XR[:, 2 * m + b:2048:16] if m < 8 else T.XR[:, 2032 + 2 * m + b:2560:4]
+                ln = 1024 if m < 8 else 256
+                MM(B[:, b * 128:b * 128 + 128], IB, xs, m == 0, m == 9, ["cI", "XR0.%d" % ln, "XR1.%d" % ln], ["#kB"], 128, 128)
+        TS(T.CMP[:, :], B[:, 0:256], T.THF[:, 0:1], OP.is_ge, ["#kB", "THF"], ["CMP"], 256)
         for b in (0, 1):
-            TS(T.CMP[:, b * 128:b * 128 + 128], B[:, b * 128:b * 128 + 128], T.THF[:, 0:1], OP.is_ge, ["#kB", "THF"], ["CMP%d" % b], 128)
-        MM(W[0:80, 0:256], CB[:, 1024:1104], T.CMP[:, :], True, True, ["CMP0", "CMP1", "cRC"], ["#wA"], 80, 256)
-        TS(T.HVY[:, :], W[0:80, 0:256], 8.5, OP.is_ge, ["#wA"], ["HVY"], 256)
-        TTo(T.TM[0:80, :], T.TVL[:, :], T.HVY[:, :], OP.mult, ["TVL", "HVY", "TMz"], ["TM"], 512)
-        C = PS["wB"]
+            MM(W[0:80, 0:128], T.RC[:, b * 80:b * 80 + 80], T.CMP[:, b * 128:b * 128 + 128], False, b == 1, ["CMP", "RC"], ["#wB"], 80, 128)
+        for h in (0, 1):
+            TTo(T.TM[0:80, h * 128:h * 128 + 128], T.HT[:, h * 128:h * 128 + 128], W[0:80, 0:128], OP.max, ["HT%d" % h, "#wB", "TMz"], ["TM%d" % h], 128)
         z = 0
-        for b in (0, 1):
-            for c0 in range(0, 1280, 512):
-                c1 = min(1280, c0 + 512)
-                bn = ("xA", "wA", "dA")[z % 3]
+        for c0, c1 in ((0, 384), (384, 768), (768, 1280)):
+            for h in (0, 1):
+                bn = ("xA", "wA", "kA")[z % 3]
                 z += 1
-                MM(PS[bn][:, 0:c1 - c0], T.TM[:, b * 128:b * 128 + 128], T.RT[:, c0:c1], True, True, ["TM", "TMz", "RT"], ["#" + bn], 128, c1 - c0)
-                S(T.TL[:, b * 1280 + c0:b * 1280 + c1], PS[bn][:, 0:c1 - c0], FN.Sigmoid, ["#" + bn, "CSz"], ["TL%d.%d" % (b, c0 // 512)], c1 - c0,
-                  bias=T.CS[:, 129:130], scale=200.0)
+                MM(PS[bn][:, 0:c1 - c0], T.TM[:, h * 128:h * 128 + 128], T.RH[:, c0:c1], True, True, ["TM%d" % h, "TMz", "RH"], ["#" + bn], 128, c1 - c0)
+                S(T.TL[:, h * 1280 + c0:h * 1280 + c1], PS[bn][:, 0:c1 - c0], FN.Sigmoid, ["#" + bn, "c100"], ["TL%d.%d" % (h, c0)], c1 - c0,
+                  bias=CC[:, 4:5], scale=-200.0)
+        for b, bn in ((0, "xB"), (1, "kB")):
+            for gr in range(8):
+                for m in range(10):
+                    col = m * 16 + b * 8 + gr
+                    l0 = (col % 80) * 16
+                    MM(PS[bn][:, gr:128:8], T.OH[:, col * 128:col * 128 + 128], T.TL[:, col * 16:col * 16 + 16], m == 0, m == 9,
+                       ["OH%d" % col, "TL%d.%d" % (col // 80, 0 if l0 < 384 else (384 if l0 < 768 else 768))], ["#" + bn], 128, 16)
+            CP(T.C2[:, 8 + b * 136:136 + b * 136], PS[bn][:, 0:128], ["#" + bn], ["C2%d" % b], 128)
         for b in (0, 1):
-            for th in (0, 1):
-                for gr in range(8):
-                    ms = [m for m in range(10) if (m in SHOT) == bool(th)]
-                    y = th * 256 + b * 128 + gr * 16
-                    for m in ms:
-                        col = m * 16 + gr * 2 + b
-                        l0 = (m * 8 + gr) * 16
-                        MM(C[:, y:y + 16], T.OH[:, col * 128:col * 128 + 128], T.TL[:, b * 1280 + l0:b * 1280 + l0 + 16], m == ms[0], m == ms[-1],
-                           ["OH%d" % col, "TL%d.%d" % (b, l0 // 512)], ["#wB"], 128, 16)
-        CP(T.C2[:, :], C[:, :], ["#wB"], ["C2"], 512)
-        C = PS["xB"]
-        for z in range(4):
-            MM(C[:, 0:128], CH[:, 1232:1360] if z > 1 else I16, T.C2[:, z * 128:z * 128 + 128], z == 0, z == 3, ["hDM", "hI", "C2"], ["#xB"], 128, 128)
-        TTo(T.CS[:, 0:128], C[:, 0:128], T.MT0[:, :], OP.mult, ["#xB", "MT0"], ["CS"], 128)
-        TTo(T.DD[:, :], C[:, 0:128], T.CS[:, 1:129], OP.subtract, ["#xB", "CS", "CSz"], ["DD"], 128)
-        TS(T.MK[:, :], T.DD[:, :], 1.0, OP.min, ["DD"], ["MK"], 128, -512.0, OP.mult)
-        MM(X[:, 0:128], T.MK[:, :], IB, True, True, ["MK", "cI"], ["#xA"], 128, 128)
-        S(T.MKT[:, :], X[:, 0:128], FN.Copy, ["#xA"], ["MKT"], 128)
+            y = b * 136
+            MM(W[:, 0:128], T.C2[:, 8 + y:136 + y], CH[:, DM:DM + 128], b == 0, False, ["C2%d" % b, "hDM"], ["#wB"], 128, 128)
+            MM(W[:, 0:128], T.C2[:, y:128 + y], CH[:, NDM:NDM + 128], False, b == 1, ["C2%d" % b, "C2y", "C2z", "hND"], ["#wB"], 128, 128)
+        S(T.MKT[:, :], W[:, 0:128], FN.Sign, ["#wB"], ["MKT"], 128)
 
     def show(t):
         P = "PT%d" % t
-        pt = T[P]
+        pt, JS = T[P], T.JS
         D, E = PS["dA"], PS["dB"]
-        TTo(T.IL[:, 0:16], T.JS[:, 32:48], T.JS[:, 16:32], OP.add, ["JI", "JF"], ["ILi"], 64)
+        J0, JJ = T.JI[:, 16:32], T.JI[:, 32:48]
+        TTo(JS[:, 32:48], J0, JJ, OP.subtract, ["J0", "JJ"], ["Y8"], 64)
+        TS(JS[:, 48:64], J0, 8.0, OP.is_ge, ["J0"], ["YF"], 64)
+        TS(JS[:, 64:80], JS[:, 32:48], 0.125, OP.mult, ["Y8"], ["YI"], 64)
+        TTo(T.IL[:, 0:16], JS[:, 64:80], JS[:, 48:64], OP.add, ["YI", "YF"], ["ILi"], 64)
+        TTo(JS[:, 80:96], JJ, JS[:, 48:64], OP.mult, ["JJ", "YF"], ["YJ"], 64)
+        TTo(T.IL[:, 16:32], JS[:, 64:80], JS[:, 80:96], OP.add, ["YI", "YJ"], ["ILl"], 64)
+        MM(E[0:96, 0:128], pt[:, 80:176], I16, True, True, [P + "s%d" % i for i in range(5, 11)] + ["hI"], ["#dB"], 96, 128)
+        CP(T.AT[:, :], E[0:96, 0:128], ["#dB"], ["AT"], 128)
+        for z, k in ((0, "ILi"), (1, "ILl")):
+            MM(D[0:16, z * 128:z * 128 + 128], T.IL[:, z * 16:z * 16 + 16], I16, True, True, [k, "hI"], ["#dA"], 16, 128)
+        CP(T.LT[:, :], D[0:16, 0:256], ["#dA"], ["LT"], 256)
         for b in (0, 1):
-            MM(D[0:8, b * 128:b * 128 + 128], pt[:, 160 + b:176:2], I16, True, True, [P + "s10", "hI"], ["#dA"], 8, 128)
-        for b in (0, 1):
-            MM(D[0:8, 256 + b * 128:384 + b * 128], T.IL[:, b:16:2], I16, True, True, ["ILi", "hI"], ["#dA"], 8, 128)
-        for b in (0, 1):
-            MM(E[0:8, b * 128:b * 128 + 128], T.IL[:, 16 + b:32:2], I16, True, True, ["ILl", "hI"], ["#dB"], 8, 128)
-        CP(NTs(5, 8), D[0:8, 0:256], ["#dA"], ["NT5"], 256)
-        CP(NTs(10, 8), D[0:8, 256:512], ["#dA"], ["NT10"], 256)
-        CP(NTs(11, 8), E[0:8, 0:256], ["#dB"], ["NT11"], 256)
-        for z in (0, 1):
-            MM(D[:, z * 256:z * 256 + 256], CW[:, 1280:1408], NTs(10 + z), True, True, ["wM", "NT%d" % (10 + z)], ["#dA"], 128, 256)
-        for i in range(6):
-            MM(E[:, 0:256], T.VH[:, i * 128:i * 128 + 128], NTs(i, 8), i == 0, i == 5, ["VH", "NT%d" % i], ["#dB"], 128, 256)
+            eb = CW[0:16, 1152 + b * 128:1280 + b * 128]
+            for z in (0, 1):
+                MM(D[:, z * 256 + b:z * 256 + 256:2], eb, T.LT[:, z * 128:z * 128 + 128], True, True, ["wE", "LT"], ["#dA"], 128, 128)
+            MM(E[:, b:256:2], CH[0:96, PAB + b * 128:PAB + b * 128 + 128], T.AT[:, :], True, True, ["hAB", "AT"], ["#dB"], 128, 128)
         R1, R2 = D[:, 0:256], D[:, 256:512]
-        TS(T.YN[:, :], R1, 0.5, OP.is_le, ["#dA"], ["YN"], 256)
-        TS(T.YM[:, :], R1, 0.5, OP.is_ge, ["#dA"], ["YM"], 256)
-        TTo(T.YP[:, :], T.YN[:, :], R2, OP.mult, ["#dA", "YN"], ["YP"], 256)
-        TS(T.YB[:, 256:512], R2, 0.5, OP.is_le, ["#dA"], ["YB1"], 256, -1.0, OP.mult)
-        TTo(T.YB[:, 0:256], T.YM[:, :], E[:, 0:256], OP.mult, ["#dB", "YM"], ["YB0"], 256)
+        TS(T.YM[:, :], R1, CC[:, 13:14], OP.is_ge, ["#dA", "cM5"], ["YM"], 256, 2048.0, OP.mult)
+        TTo(T.YP[:, :], T.YM[:, :], R2, OP.max, ["#dA", "YM"], ["YP"], 256)
+        TS(T.YB[:, 256:512], R2, CC[:, 13:14], OP.is_le, ["#dA", "cM5"], ["YB1"], 256, -1.0, OP.mult)
+        TTo(T.YB[:, 0:256], T.YM[:, :], E[:, 0:256], OP.min, ["#dB", "YM"], ["YB0"], 256)
         for j in range(1, 5):
-            k0 = (j - 1) * 256
-            MM(E[:, 256:512], CW[0:8, 1152:1280], NTs(5 + j, 8), True, True, ["wE", "NT%d" % (5 + j)], ["#dB"], 128, 256)
-            TS(T.YK[:, k0:k0 + 256], T.YP[:, :], float(j), OP.is_equal, ["YP"], ["YK%d" % j], 128)
-            TTo(T.YB[:, 256 + j * 256:512 + j * 256], T.YK[:, k0:k0 + 256], E[:, 256:512], OP.mult, ["YK%d" % j, "#dB"], ["YB%d" % (j + 1)], 256)
+            k0 = (j % 2) * 256
+            s = nt(t, 1, j)
+            for b in (0, 1):
+                MM(E[:, 256 + b:512:2], CW[0:16, 1152 + b * 128:1280 + b * 128], NTs(s, 16), True, True, ["wE", "NT%d" % s], ["#dB"], 128, 128)
+            TS(T.YK[:, k0:k0 + 256], T.YP[:, :], CC[:, 8 + j:9 + j], OP.is_equal, ["YP", "cM%d" % j], ["YK%d" % (j % 2)], 128)
+            TTo(T.YB[:, 256 + j * 256:512 + j * 256], T.YK[:, k0:k0 + 256], E[:, 256:512], OP.mult, ["YK%d" % (j % 2), "#dB"], ["YB%d" % (j + 1)], 256)
         for z in range(6):
             MM(D[:, 0:256], I16, T.YB[:, z * 256:z * 256 + 256], z == 0, z == 5, ["hI", "YB%d" % z], ["#dA"], 128, 256)
-        S(T.YR[:, t * 256:t * 256 + 256], D[:, 0:256], FN.Copy, ["#dA"], ["YR%d" % t], 256)
-        DMA("y", T.yr[:, t * 256:t * 256 + 256], T.YR[:, t * 256:t * 256 + 256], ["YR%d" % t], [])
+        S(T.YR[:, :], D[:, 0:256], FN.Copy, ["#dA"], ["YR"], 256)
+        DMA("y", T.yr[:, t * 256:t * 256 + 256], T.YR[:, :], ["YR"], [])
 
     start(0)
+    ring_constants()
+    lesser("EL0", T.TO, "TO")
+    for k in (4, 5):
+        send(k, ["TP0"])
+    arrive("TPn", "aTPn", (r + 2) % n, 50.0, ["sent4", "sent5"])
     for a in range(5):
         step(0, 0, a, T.TO, "TO")
         step(0, 1, a, T.TP0, "TP0")
-    late_constants()
-    lesser("EL0", T.TO, "TO")
     lesser("ELn", T.TPn, "TPn")
+    start(1)
     rings(0, T.TO, "TO")
     send(6)
-    arrive("MKP", "aMK", (r + 2) % n, 7.0, ["MKT"])
+    arrive("MKP", "aMK", (r + 2) % n, PLAN["mk"], ["sent6"])
     show(0)
-    lessen(T.TO, "TO", "MKT", "EL0", T.TO1, "T1q", ("kA", "kB", "xB", "wA"))
+    lessen(T.TO, "TO", "MKT", "EL0", T.TO1, "T1q", ("kA", "wA", "xA"))
     op(None, None, ["T1q%d" % q for q in range(4)], ["TO1"], 0.0, "n")
-    start(1)
-    lessen(T.TPn, "TPn", "MKP", "ELn", T.TP1, "P1q", ("dB",))
+    lessen(T.TPn, "TPn", "MKP", "ELn", T.TP1, "P1q", ("wB", "xB"))
     op(None, None, ["P1q%d" % q for q in range(4)], ["TP1"], 0.0, "n")
     for a in range(5):
         step(1, 0, a, T.TO1, "TO1")
         step(1, 1, a, T.TP1, "TP1")
-    lesser("EL1", T.TO1, "TO1")
+    lesser("EL0", T.TO1, "TO1")
     rings(1, T.TO1, "TO1")
     show(1)
-    lessen(T.TO1, "TO1", "MKT", "EL1", T.TO2, "T2q", ("kA", "kB", "xB", "wA"))
+    lessen(T.TO1, "TO1", "MKT", "EL0", T.TO2, "T2q", ("kA", "wA", "xA"))
     for qd in range(4):
         DMA("y" if qd % 2 == 0 else "s", T.ye[:, qd * 512:qd * 512 + 512], T.TO2[:, qd * 512:qd * 512 + 512], ["T2q%d" % qd], [])
     for o in ops:
@@ -674,58 +687,77 @@ def build(g, core, T, topo):
     return ops
 
 
-def schedule(ops):
+def place(ops, pred, rank):
     n = len(ops)
-    wake, same = 0.12, 0.04
-    succ = [[] for _ in range(n)]
-    need = [0] * n
-    for i, o in enumerate(ops):
-        for d in o["deps"]:
-            succ[d].append((i, False))
-            need[i] += 1
-        for d in o["order"]:
-            succ[d].append((i, True))
-            need[i] += 1
-    prio = [0.0] * n
-    for i in range(n - 1, -1, -1):
-        best = 0.0
-        for j, od in succ[i]:
-            best = max(best, prio[j] + (0.0 if od else (wake if ops[j]["q"] != ops[i]["q"] else same)))
-        prio[i] = best + ops[i]["cost"] + ops[i]["lat"]
-    prio = [prio[i] + ops[i]["bon"] for i in range(n)]
-    ready, free, order = {}, {}, []
-    tready, fin = [0.0] * n, [0.0] * n
+    succ, need = [[] for _ in range(n)], [len(p) for p in pred]
     for i in range(n):
-        if need[i] == 0:
-            ready.setdefault(ops[i]["q"], []).append(i)
-    while len(order) < n:
-        bq, bt = None, 1e18
-        for q in ready:
-            for i in ready[q]:
-                s = max(free.get(q, 0.0), tready[i])
-                if s < bt:
-                    bt, bq = s, q
-        lst = ready[bq]
-        pick, pp = None, -1e9
-        for i in lst:
-            if max(free.get(bq, 0.0), tready[i]) <= bt + 0.1 and prio[i] > pp:
-                pick, pp = i, prio[i]
-        lst.remove(pick)
-        if not lst:
-            del ready[bq]
-        o = ops[pick]
-        s = max(free.get(bq, 0.0), tready[pick])
-        if bq is not None:
-            free[bq] = s + o["cost"]
-        fin[pick] = s + o["cost"] + o["lat"]
-        order.append(pick)
-        for j, od in succ[pick]:
-            tj = s if od else fin[pick] + (wake if ops[j]["q"] != o["q"] else same)
-            tready[j] = max(tready[j], tj)
+        for d, lag in pred[i]:
+            succ[d].append(i)
+    start, seq, busy = [0.0] * n, [0] * n, {}
+    ready = [(rank[i], i) for i in range(n) if need[i] == 0]
+    k = 0
+    while ready:
+        best = min(ready)
+        ready.remove(best)
+        i = best[1]
+        o = ops[i]
+        s = max([start[d] + lag for d, lag in pred[i]] + [0.0])
+        if o["q"] is not None:
+            b, c = busy.setdefault(o["q"], []), o["cost"]
+            lo, hi = 0, len(b)
+            while lo < hi:
+                m = (lo + hi) // 2
+                if b[m][1] <= s:
+                    lo = m + 1
+                else:
+                    hi = m
+            while lo < len(b) and b[lo][0] < s + c:
+                s = max(s, b[lo][1])
+                lo += 1
+            if lo > 0 and b[lo - 1][1] >= s - 1e-9:
+                b[lo - 1][1] = s + c
+                if lo < len(b) and b[lo][0] <= s + c + 1e-9:
+                    b[lo - 1][1] = b[lo][1]
+                    del b[lo]
+            elif lo < len(b) and b[lo][0] <= s + c + 1e-9:
+                b[lo][0] = s
+            else:
+                b.insert(lo, [s, s + c])
+        start[i], seq[i] = s, k
+        k += 1
+        for j in succ[i]:
             need[j] -= 1
             if need[j] == 0:
-                ready.setdefault(ops[j]["q"], []).append(j)
-    return order
+                ready.append((rank[j], j))
+    return start, seq
+
+
+def schedule(ops):
+    n = len(ops)
+    full = [o["cost"] + o["lat"] for o in ops]
+    fwd, back = [[] for _ in range(n)], [[] for _ in range(n)]
+    for i, o in enumerate(ops):
+        for d in o["deps"]:
+            w = PLAN["wake"] if ops[d]["q"] != o["q"] else PLAN["same"]
+            fwd[i].append((d, full[d] + w))
+            back[d].append((i, o["cost"] + w + ops[d]["lat"]))
+        for d in o["order"]:
+            fwd[i].append((d, ops[d]["cost"]))
+            back[d].append((i, o["cost"]))
+    way = [0.0] * n
+    for i in range(n - 1, -1, -1):
+        way[i] = max([way[j] + lag - ops[j]["cost"] for j, lag in back[i]] + [ops[i]["lat"]]) + ops[i]["cost"]
+    rank = [-way[i] - ops[i]["bon"] for i in range(n)]
+    best = None
+    for z in range(PLAN["turns"]):
+        start, seq = place(ops, fwd, rank)
+        end = max(start[i] + full[i] for i in range(n))
+        ORDERS.setdefault("ends", []).append(end)
+        if best is None or end < best[0]:
+            best = (end, start, seq)
+        rs, _ = place(ops, back, [-(start[i] + full[i]) for i in range(n)])
+        rank = [-(rs[i] + ops[i]["cost"]) for i in range(n)]
+    return sorted(range(n), key=lambda i: (best[1][i], best[2][i]))
 
 
 def emit(g, T, ops, order):

@@ -6,24 +6,32 @@ FN = ActivationFunctionType
 BIG = float(2 ** 26)
 REST = 2041 * 8192
 F32, B16, H16, I32, U16 = "float32", "bfloat16", "float16", "int32", "uint16"
-NV = [1024, 2048, 2048, 2048, 1536]
-SHOT = [0, 1, 2, 8]
+NV = [1024, 2304, 2304, 2304, 2304, 1024, 2304, 2304, 2304, 2304]
+CHUNK = [512, 512, 512]
+SHOT = [0, 1, 2, 3, 8, 9]
+HIV = [2]
+XV = [640]
+QS = [2, 3]
+ND = [0, 0, 0, 0, 0, 0, 0, 0, 0, 0]
+NQW = 1536
 SCRATCH = {}
 for _n, _p, _w, _t in (
+        ("NQ", 128, NQW, B16),
         ("NB", 128, 1024, I32), ("XI", 128, 176, I32), ("XJ", 128, 176, I32), ("TO", 128, 2064, B16), ("TO1", 128, 2064, B16), ("TO2", 128, 2048, B16),
-        ("TP0", 128, 2048, B16), ("TPn", 128, 2048, B16), ("TP1", 128, 2048, B16), ("EL0", 128, 2048, B16), ("ELn", 128, 2048, B16),
-        ("TMP", 128, 2048, H16), ("ST", 128, 32, I32), ("SU", 128, 32, U16), ("STH", 128, 32, H16), ("TH", 128, 1, I32),
-        ("THF", 128, 1, F32), ("Q", 128, 256, B16), ("QR", 128, 4096, B16), ("QZ", 128, 2048, B16), ("ON", 128, 2048, B16), ("CB", 128, 1424, B16),
-        ("CH", 128, 2192, H16), ("SI", 128, 512, H16), ("CG", 128, 384, B16), ("CF", 17, 384, B16), ("CW", 17, 1408, H16), ("CC", 128, 32, F32),
-        ("VH", 16, 1024, H16), ("SELL", 128, 2048, B16), ("S8", 128, 8, B16), ("RC", 128, 160, B16), ("RS", 128, 16, F32),
-        ("CR", 33, 256, B16), ("IO", 128, 128, B16), ("RT", 97, 1280, B16), ("RH", 97, 1280, H16), ("IX", 1, 544, B16),
-        ("NT", 17, 1408, H16), ("NZ", 128, 256, H16), ("PT0", 128, 176, H16), ("PT1", 128, 176, H16), ("NP0", 128, 128, H16), ("NP1", 128, 128, H16),
+        ("TP0", 128, 2048, B16), ("TPn", 128, 2048, B16), ("TP1", 128, 2048, B16), ("EL0", 128, 2048, H16), ("ELn", 128, 2048, H16),
+        ("ST", 128, 32, I32), ("SU", 128, 32, U16), ("STH", 128, 32, H16), ("TH", 128, 1, I32),
+        ("THF", 128, 1, F32), ("Q", 128, 256, B16), ("QR", 128, 4096, B16), ("QZ", 128, 2048, B16), ("ON", 128, 512, B16), ("CB", 128, 2144, B16),
+        ("SI", 128, 640, B16), ("CG", 128, 384, B16), ("CF", 17, 384, B16), ("CW", 17, 1152, H16), ("CC", 128, 32, F32), ("C9", 128, 512, B16), ("C8", 1, 512, B16),
+        ("VH", 16, 1024, B16), ("SELL", 128, 2048, B16), ("S8", 128, 8, B16), ("RC", 128, 160, B16), ("RS", 128, 16, F32),
+        ("CR", 33, 256, B16), ("RT", 97, 2560, B16), ("IO", 128, 64, B16), ("IH", 128, 64, H16), ("IX", 1, 800, B16),
+        ("NT", 17, 1792, H16), ("MZ", 128, 128, F32), ("TZ", 128, 128, I32), ("BZ", 128, 128, I32), ("OZ", 128, 256, U16), ("BQZ", 128, 256, B16),
+        ("NZ", 128, 256, H16), ("PT0", 128, 176, H16), ("PT1", 128, 176, H16), ("NP0", 128, 128, H16), ("NP1", 128, 128, H16),
         ("DZ", 128, 128, F32), ("U", 128, 176, F32), ("PR", 128, 144, F32), ("V5", 128, 144, F32), ("PX", 128, 176, F32), ("DX", 128, 160, F32),
         ("TT", 128, 160, I32), ("HH", 128, 160, I32), ("JA", 128, 400, B16), ("JD", 128, 400, B16), ("JC", 128, 400, B16),
         ("JI", 128, 64, I32), ("JS", 128, 96, F32), ("IL", 128, 32, H16), ("NM", 128, 160, F32), ("JP", 128, 192, H16),
-        ("WW", 128, 160, I32), ("WS", 128, 160, F32), ("HV", 128, 160, H16), ("HT", 80, 256, H16), ("OFR", 128, 160, U16), ("XR", 128, 2560, B16),
-        ("CMP", 128, 256, B16), ("TM", 97, 256, H16), ("OH", 128, 20480, B16), ("TL", 128, 2560, B16), ("C2", 128, 272, H16),
-        ("MKT", 128, 128, B16), ("MKP", 128, 128, B16), ("AT", 96, 128, H16), ("LT", 16, 256, H16),
+        ("WW", 128, 160, I32), ("WS", 128, 160, F32), ("HV", 128, 160, H16), ("HT", 80, 256, H16), ("OFR", 128, 160, U16),
+        ("XR", 128, 2560, B16), ("CMP", 128, 256, B16), ("TM", 97, 256, H16), ("OH", 128, 10240, B16), ("TL", 128, 5120, B16), ("C3", 128, 528, H16),
+        ("MKT", 128, 128, B16), ("MKP", 128, 128, B16), ("AT", 96, 128, H16), ("LT", 16, 256, B16),
         ("YM", 128, 256, H16), ("YP", 128, 256, H16), ("YK", 128, 512, H16), ("YB", 128, 1536, H16), ("YR", 128, 256, F32)):
     SCRATCH[_n] = ("sbuf", [_p, _w], _t)
 for _c in "01":
@@ -36,10 +44,12 @@ for _b in BANKS:
     SCRATCH[_b] = ("psum", [128, 512], F32)
 NITEM = 7
 NDMA = 14
-SEMAPHORES = ["v", "s", "t", "gc", "aTP0", "aTPn", "aMK"] + ["d%d" % i for i in range(NDMA)]
+SEMAPHORES = ["v", "s", "t", "gc", "aTP0", "aTPn", "aMK", "ad0", "ad1"] + ["d%d" % i for i in range(NDMA)]
 SEMAPHORES += ["ri%d" % i for i in range(NITEM)] + ["lo%d" % i for i in range(NITEM)]
 
-PLAN = dict(cy=0.00100, tcy=0.00062, gat=1.5, wake=0.12, same=0.05, lead=6.0, tp0=12.0, mk=7.0, turns=3)
+PLAN = dict(cy=0.00100, tcy=0.00075, gat=1.5, wake=0.12, same=0.05, lead=1.0, tp0=12.0, mk=7.0, turns=8, shake=0.4, gd=1.0, ad=4.5)
+OTHERS = [dict(gat=1.0), dict(gat=0.8, t=1.15), dict(gat=1.25, t=0.85)]
+LEADS = [5.0, 5.5, 6.0, 6.5]
 HINT = {}
 ORDERS = {}
 
@@ -104,6 +114,7 @@ def build(g, core, T, topo):
 
     def op(q, fn, R, W, cost, kind="c", sem=None, val=1, lat=0.0):
         n = len(ops)
+        R = [{"hI": "cI", "hPV": "cPV", "hP0": "cP0", "w03": "cE0", "wE": "cEB", "hAB": "cAB"}.get(k, k) for k in R]
         deps, order = set(), set()
         for k in list(R) + list(W):
             if k[0] == "#":
@@ -129,10 +140,14 @@ def build(g, core, T, topo):
                 reads[k] = []
         deps.discard(n)
         order.discard(n)
-        ops.append(dict(q=q, fn=fn, deps=deps, order=(order - deps if q == "t" else set()), cost=cost, lat=lat, kind=kind, sem=sem, val=val, bon=bon[0] + hint(q, W)))
+        ops.append(dict(q=q, fn=fn, deps=deps, order=(order - deps if q == "t" else set()), cost=cost, lat=lat, kind=kind, sem=sem, val=val, bon=bon[0] + hint(q, W), gat=False))
 
     def V(fn, R, W, n):
         op("v", lambda: fn(g.vector), R, W, max(64, n) * CY + 0.03)
+
+    def VG(fn, R, W, n):
+        op("v", lambda: fn(g.vector), R, W, n * GAT * CY + 0.05)
+        ops[-1]["gat"] = True
 
     def TS(out, a, s1, o0, R, W, n, s2=None, o1=None):
         if o1 is None:
@@ -154,6 +169,7 @@ def build(g, core, T, topo):
 
     def SG(out, a, R, W, n):
         op("s", lambda: g.scalar.activation(out, a, FN.Copy), R, W, n * GAT * CY + 0.07)
+        ops[-1]["gat"] = True
 
     def MM(out, l, r, st, sp, R, W, m, n):
         op("t", lambda: g.tensor.matmul(out, l, r, st, sp), R, W, max(min(64, m), n) * TCY + 0.01)
@@ -164,11 +180,11 @@ def build(g, core, T, topo):
     def iota(out, pat, base, cm, R, W, n):
         GC(lambda: g.iota(out, pat, base, cm, allow_small_or_imprecise_dtypes=True), R, W, n)
 
-    def eqs(b, c0, pat, base, key, rows=128):
+    def eqs(b, c0, pat, base, key, rows=128, src="ON"):
         n = 1
         for p in pat:
             n *= p[1]
-        GC(lambda: g.affine_select(b[0:rows, c0:c0 + n], T.ON[0:rows, 0:n], pat, OP.is_equal, 0.0, base, 1), ["ON" if n <= 256 else "ONb"], [key], n)
+        GC(lambda: g.affine_select(b[0:rows, c0:c0 + n], T[src][0:rows, 0:n], pat, OP.is_equal, 0.0, base, 1), [src if n <= 256 else src + "b"], [key], n)
 
     nd = [0]
 
@@ -186,11 +202,11 @@ def build(g, core, T, topo):
     DMA("s", T.Q[:, :], T.q[:, :], [], ["Q"])
     DMA("y", T.TH[:, :], T.th[:, :], [], ["TH"])
 
-    CB, CH, CG, CF, CW, CC = T.CB, T.CH, T.CG, T.CF, T.CW, T.CC
+    CB, CH, CG, CF, CW, CC = T.CB, T.CB, T.CG, T.CF, T.CW, T.CC
     IB, I16, NEGI, BIGI, BIGP = CB[:, 8:136], CH[:, 8:136], CG[:, 0:128], CG[:, 128:256], CG[:, 256:384]
     PMV, PM0 = 144, 272
     fill(T.ON[:, 0:256], 1.0, [], ["ON"], 128)
-    fill(T.NT[:, :], 1.0, [], ["NT%d" % s for s in range(11)], 704)
+    fill(T.NT[:, :], 1.0, [], ["NT%d" % s for s in range(14)], 896)
     eqs(CB, 0, [[-1, 144]], 8, "cI")
     eqs(CB, PMV, [[-2, 8], [-1, 2], [-16, 8]], 0, "cPV")
     eqs(CB, PM0, [[-8, 2], [-16, 8], [-1, 8]], 0, "cP0")
@@ -201,9 +217,6 @@ def build(g, core, T, topo):
     iota(T.RS[:, :], [[2048, 16]], REST, 0, [], ["RS"], 16)
     CP(T.STH[:, :], T.ST[:, :], ["ST"], ["STH"], 64)
     CP(T.SU[:, :], T.ST[:, :], ["ST"], ["SU"], 64)
-    CP(CH[:, 0:144], CB[:, 0:144], ["cI"], ["hI"], 72)
-    CP(CH[:, PMV:PMV + 128], CB[:, PMV:PMV + 128], ["cPV"], ["hPV"], 64)
-    CP(CH[:, PM0:PM0 + 128], CB[:, PM0:PM0 + 128], ["cP0"], ["hP0"], 64)
     for z in (0, 1):
         V(lambda e, z=z: e.tensor_reduce(CC[:, z:z + 1], CB[:, PM0 + 64 * z:PM0 + 64 * z + 64], AxisListType.X, OP.add), ["cP0"], ["cR%d" % z], 64)
     for c in (0, 1):
@@ -214,11 +227,9 @@ def build(g, core, T, topo):
     TS(CC[0:17, 3:4], CB[0:17, 24:25], 1.0 / 594.0, OP.mult, ["cI"], ["cH2"], 64)
     TS(CW[:, 0:128], CF[:, 0:128], CC[0:17, 2:3], OP.add, ["cE0", "cH"], ["w01"], 64, 4.0, OP.mult)
     TS(CW[:, 128:256], CF[:, 0:128], CC[0:17, 3:4], OP.add, ["cE0", "cH2"], ["w02"], 64, 594.0, OP.mult)
-    CP(CW[:, 256:384], CF[:, 0:128], ["cE0"], ["w03"], 64)
     TS(CW[:, 384:640], CF[:, 128:384], CC[0:17, 2:3], OP.add, ["cEB", "cH"], ["wP"], 128, 4.0, OP.mult)
     TS(CW[:, 640:896], CF[:, 128:384], CC[0:17, 2:3], OP.add, ["cEB", "cH"], ["wQ"], 128, 2.0, OP.mult)
     TS(CW[:, 896:1152], CF[:, 128:384], 592.0, OP.mult, ["cEB"], ["wV"], 128)
-    CP(CW[:, 1152:1408], CF[:, 128:384], ["cEB"], ["wE"], 128)
     TS(T.XJ[:, 0:8], T.XI[:, 0:8], 4, OP.arith_shift_right, ["XI"], ["XJ"], 64)
     TS(T.S8[:, :], T.XJ[:, 0:8], 0.0, OP.is_equal, ["XJ"], ["S8"], 64, 8192.0, OP.mult)
     fill(T.CR[0:32, :], 0.0, ["CR"], ["CR"], 128)
@@ -232,52 +243,60 @@ def build(g, core, T, topo):
         TS(T["D" + c][:, 8::16], T.RS[:, :], 2047.0, OP.add, ["RS", "D" + c], ["D" + c], 64)
     QZ, QA = ["QZ%d" % k for k in range(8)], ["QR%d" % k for k in range(32)]
     for k in range(8):
-        if k % 2:
+        if k % QS[0]:
             CP(T.QZ[:, k::8], T.Q[:, :], ["Q"], [QZ[k]], 128)
         else:
             S(T.QZ[:, k::8], T.Q[:, :], FN.Copy, ["Q"], [QZ[k]], 256)
     for b in (0, 1):
         for k in range(16):
             o, i = T.QR[:, b * 2048 + k:b * 2048 + 2048:16], T.Q[:, b::2]
-            if k % 3:
+            if k % QS[1]:
                 CP(o, i, ["Q"], [QA[b * 16 + k]], 64)
             else:
                 S(o, i, FN.Copy, ["Q"], [QA[b * 16 + k]], 128)
+    if max(ND):
+        S(T.NQ[:, :], T.QR[:, 2048:2048 + NQW], FN.Copy, QA[16:], ["NQ"], NQW, scale=-1.0)
     for h, bn in ((0, "wB"), (1, "kB")):
         for z in range(4):
             x = PMV + (h * 4 + z) * 16
             MM(PS[bn][0:16, z * 128:z * 128 + 128], CH[:, x:x + 16], I16, True, True, ["hPV", "hI"], ["#" + bn], 16, 128)
         CP(T.VH[:, h * 512:h * 512 + 512], PS[bn][0:16, :], ["#" + bn], ["VH%d" % h], 512)
 
-    PR1, PR2, PTZ, PAB, I2, I592, I4K, NI4K, DM, NDM = 912, 1040, 1168, 1680, 0, 128, 256, 384, 1936, 2064
+    PR1, PR2, PTZ, PAB, DM, NDM, I64 = 912, 1040, 1168, 1680, 1936, 2000, 2064
+    I2, I592, I4K, NI4K, IQ = 0, 128, 256, 384, 512
+    RLK, RTK, SLK = ["RL%d" % z for z in range(9)], ["RT%d" % z for z in range(7)], ["SELL%d" % z for z in range(4)]
 
     def ring_constants():
-        fill(T.ON[:, 256:2048], 1.0, ["ON"], ["ONb"], 896)
+        fill(T.ON[:, 256:512], 1.0, ["ON"], ["ONb"], 128)
+        fill(T.C9[:, :], 1024.0, [], ["C9b"], 256)
         fill(T.TO[:, 2048:2064], 0.0, [], ["TOz"], 64)
         fill(T.TO1[:, 2048:2064], 0.0, [], ["TO1z"], 64)
-        iota(T.IO[:, :], [[1, 128]], 0, 0, [], ["IO"], 128)
-        eqs(CB, 400, [[-1, 8], [-16, 8], [-8, 2]], 0, "cR1", 80)
-        eqs(CB, 528, [[-1, 8], [-16, 8], [-8, 2]], 80, "cR2", 80)
+        iota(T.IO[:, 0:64], [[1, 64]], 0, 0, [], ["IO"], 64)
+        TS(T.IH[:, :], T.IO[:, 0:64], 200.0, OP.mult, ["IO"], ["IH"], 64)
+        eqs(CB, PR1, [[-1, 8], [-16, 8], [-8, 2]], 0, "cR1", 80)
+        eqs(CB, PR2, [[-1, 8], [-16, 8], [-8, 2]], 80, "cR2", 80)
         for z in range(4):
-            eqs(CB, 656 + z * 128, [[-1, 8], [1000, 4], [-8, 4]], -48 - 1000 * z, "cZ%d" % z, 80)
-        eqs(CB, 1168, [[-8, 2], [-1, 8], [-16, 16]], 0, "cAB", 96)
-        CP(CH[0:80, PR1:PR1 + 768], CB[0:80, 400:1168], ["cR1", "cR2"] + ["cZ%d" % z for z in range(4)], ["hPR"], 384)
-        CP(CH[0:96, PAB:PAB + 256], CB[0:96, 1168:1424], ["cAB"], ["hAB"], 128)
-        TTo(CH[:, DM:DM + 128], CB[:, 8:136], CB[:, 7:135], OP.subtract, ["cI"], ["hDM"], 256)
-        TTo(CH[:, NDM:NDM + 128], CB[:, 7:135], CB[:, 8:136], OP.subtract, ["cI"], ["hND"], 256)
+            eqs(CB, PTZ + z * 128, [[-1, 8], [1000, 4], [-8, 4]], -48 - 1000 * z, "cZ%d" % z, 80)
+        eqs(CB, PAB, [[-8, 2], [-1, 8], [-16, 16]], 0, "cAB", 96)
+        fill(CB[:, I64:I64 + 1], 0.0, [], ["c64z"], 64)
+        TTo(CB[:, I64 + 1:I64 + 65], CB[:, 8:72], CB[:, 72:136], OP.add, ["cI"], ["c64"], 128)
+        TTo(CB[:, DM:DM + 64], CB[:, I64 + 1:I64 + 65], CB[:, I64:I64 + 64], OP.subtract, ["c64", "c64z"], ["cDM"], 128)
+        TS(CB[:, NDM:NDM + 64], CB[:, DM:DM + 64], -1.0, OP.mult, ["cDM"], ["cND"], 64)
         for b in (0, 1):
             GC(lambda b=b: g.iota(T.XI[:, 16 + b * 80:96 + b * 80], [[0, 5], [1000, 2], [-16, 8]], -1000 * b, 1), [], ["XI%d" % b], 80)
         TS(T.XJ[:, 16:176], T.XI[:, 16:176], 4, OP.arith_shift_right, ["XI0", "XI1"], ["XJb"], 160)
         TS(T.RC[:, :], T.XJ[:, 16:176], 0.0, OP.is_equal, ["XJb"], ["RC"], 160, -4096.0, OP.mult)
-        eqs(T.RT, 0, [[-1, 80], [0, 16]], 0, "RT", 97)
-        iota(T.RT[96:97, :], [[0, 80], [-128, 16]], -128, 0, ["RT"], ["RT"], 1280)
-        CP(T.RH[:, :], T.RT[:, :], ["RT"], ["RH"], 640)
-        eqs(T.SELL, 0, [[-8, 16], [-1, 8], [0, 16]], 0, "SELL")
-        S(T.SELL[:, :], T.SELL[:, :], FN.Copy, ["SELL"], ["SELL"], 2048, scale=-512.0)
+        for b in (0, 1):
+            for z, m in enumerate((2, 2, 1)):
+                eqs(T.RT, b * 1280 + z * 512, [[-16, m], [-1, 8], [0, 32]], -8 * b - 32 * z, RTK[b * 3 + z], 96)
+        for z in range(5):
+            iota(T.RT[96:97, z * 512:z * 512 + 512], [[0, 16], [64, 2], [-128, 16]], -128, 0, [RTK[6]], [RTK[6]], 512)
+        for z in range(4):
+            eqs(T.SELL, z * 512, [[-8, 4], [-1, 8], [0, 16]], -32 * z, SLK[z], 128, "C9")
         iota(T.IX[0:1, 0:400], [[0, 16], [8, 5], [1, 5]], 9, 0, [], ["IX"], 400)
         fill(T.IX[0:1, 0:400:25], 64.0, ["IX"], ["IX"], 64)
         fill(T.IX[0:1, 400:528], 34816.0, [], ["IXc"], 64)
-        fill(T.IX[0:1, 528:544], 1.0, [], ["IXd"], 64)
+        fill(T.IX[0:1, 544:800], 0.0, [], ["IXz"], 128)
         fill(T.JD[:, :], 0.0, [], ["JD"], 200)
         fill(T.JD[:, 0::25], 64.0, ["JD"], ["JD"], 64)
         for x, f in ((I2, 2.0), (I592, 592.0), (I4K, 4096.0), (NI4K, -4096.0)):
@@ -285,9 +304,10 @@ def build(g, core, T, topo):
         CP(T.THF[:, :], T.TH[:, :], ["TH"], ["THF"], 64)
         fill(T.TM[:, :], 0.0, [], ["TMz"], 128)
         fill(T.TM[96:97, :], 1.0, ["TMz"], ["TMz"], 128)
-        fill(T.C2[:, 0:8], 0.0, [], ["C2y"], 64)
-        fill(T.C2[:, 136:144], 0.0, [], ["C2z"], 64)
+        fill(T.C3[:, :], 0.0, [], ["C3%d%d" % (b, h) for b in (0, 1) for h in (0, 1)], 264)
         fill(CC[:, 4:5], -100.0, [], ["c100"], 64)
+        fill(CC[:, 5:6], 100.0, [], ["c101"], 64)
+        fill(CC[:, 6:7], 0.5, [], ["c05"], 64)
         GC(lambda: g.iota(T.JI[:, 48:56], [[0, 8]], 0, 1), [], ["cm"], 8)
         TS(T.JI[:, 56:64], T.JI[:, 48:56], 15, OP.bitwise_and, ["cm"], ["cm2"], 64)
         for j in range(6):
@@ -320,39 +340,39 @@ def build(g, core, T, topo):
     NB = T.NB[:, 0:1024]
 
     def nt(t, c, a):
-        return t if a == 0 else (1 + a if c == 0 else 6 + a)
+        return t if a == 0 else (1 + a if c == 0 else 5 + a + 4 * t)
 
     def NTs(s, rows=17):
         return T.NT[0:rows, s * 128:s * 128 + 128]
 
-    def offsets(C, w):
+    def offsets(C, out, ok, w):
         TS(T["B" + C][:, 0:w], T["T" + C][:, 0:w], 4, OP.arith_shift_right, ["T" + C], ["B" + C], w, 2047, OP.bitwise_and)
-        CP(T["OF" + C][:, 0:w], T["B" + C][:, 0:w], ["B" + C], ["OF" + C], w)
+        CP(out, T["B" + C][:, 0:w], ["B" + C], [ok], w)
 
-    def start(t):
+    def start(t, banks):
         P = "PT%d" % t
-        X = PS["dA"]
+        X, XB = PS[banks[0]], "#" + banks[0]
         for z in range(8):
-            MM(X[0:16, z:128:8], CH[:, PMV + z * 16:PMV + z * 16 + 16], T.STH[:, t * 16:t * 16 + 16], True, True, ["hPV", "STH"], ["#dA"], 16, 16)
-        CP(NTs(t, 16), X[0:16, 0:128], ["#dA"], ["NT%d" % t], 128)
-        MM(X[:, 128:144], NTs(t, 16), CH[0:16, 8:24], True, True, ["NT%d" % t, "hI"], ["#dA"], 128, 16)
-        CP(T[P][:, 80:96], X[:, 128:144], ["#dA"], [P + "s5"], 64)
+            MM(X[0:16, z:128:8], CH[:, PMV + z * 16:PMV + z * 16 + 16], T.STH[:, t * 16:t * 16 + 16], True, True, ["hPV", "STH"], [XB], 16, 16)
+        CP(NTs(t, 16), X[0:16, 0:128], [XB], ["NT%d" % t], 128)
+        MM(X[:, 128:144], NTs(t, 16), CH[0:16, 8:24], True, True, ["NT%d" % t, "hI"], [XB], 128, 16)
+        CP(T[P][:, 80:96], X[:, 128:144], [XB], [P + "s5"], 64)
         TTo(T.DZ[:, 0::8], T[P][:, 80:96], T.RS[:, :], OP.add, [P + "s5", "RS", "DZ"], ["DZ"], 64)
-        V(lambda e: e.tensor_copy(T.NZ[:, :], NB.indirect(T.SU[:, t * 16:t * 16 + 16])), ["NB", "SU"], ["NZ"], 256 * GAT)
-        for c, bn in ((0, "dA"), (1, "dB")):
+        VG(lambda e: e.tensor_copy(T.NZ[:, :], NB.indirect(T.SU[:, t * 16:t * 16 + 16])), ["NB", "SU"], ["NZ"], 256)
+        for c, bn in enumerate(banks):
             C, X = str(c), PS[bn]
             bon[0] = PLAN["lead"] * (1 - c)
             for b in (0, 1):
                 x = 400 + (2 * c + b) * 128
                 MM(X[:, 0:128], CH[:, x:x + 128], T.NZ[:, b::2], b == 0, b == 1, ["hP4%d%d" % (c, b), "NZ"], ["#" + bn], 128, 128)
             for z in range(3):
-                MM(X[:, 128 + z * 128:256 + z * 128], CW[:, z * 128:z * 128 + 128], NTs(t), True, True, ["w0%d" % (z + 1), "NT%d" % t], ["#" + bn], 128, 128)
+                MM(X[:, 128 + z * 128:256 + z * 128], CW[:, z * 128:z * 128 + 128] if z < 2 else CF[:, 0:128], NTs(t), True, True, ["w0%d" % (z + 1), "NT%d" % t], ["#" + bn], 128, 128)
             np_ = T["NP" + C][:, :]
             CP(np_, X[:, 0:128], ["#" + bn], ["NP" + C], 128)
-            TTo(T["M" + C][:, 0:128], np_, X[:, 128:256], OP.mult, ["NP" + C, "#" + bn], ["M%s0" % C], 128)
-            TTo(T["T" + C][:, 0:128], T["M" + C][:, 0:128], X[:, 256:384], OP.add, ["M%s0" % C, "#" + bn], ["T" + C], 128)
-            TTo(T["BQ" + C][:, 0:128], np_, X[:, 384:512], OP.is_equal, ["NP" + C, "#" + bn], ["BQ%s0" % C], 128)
-            offsets(C, 128)
+            TTo(T.MZ[:, :], np_, X[:, 128:256], OP.mult, ["NP" + C, "#" + bn], ["MZ"], 128)
+            TTo(T.TZ[:, :], T.MZ[:, :], X[:, 256:384], OP.add, ["MZ", "#" + bn], ["TZ"], 128)
+            TTo(T.BQZ[:, c * 128:c * 128 + 128], np_, X[:, 384:512], OP.is_equal, ["NP" + C, "#" + bn], ["BQZ" + C], 128)
+            offsets("Z", T.OZ[:, c * 128:c * 128 + 128], "OZ" + C, 128)
         bon[0] = 0.0
 
     def step(t, c, a, tab, tkey):
@@ -363,13 +383,13 @@ def build(g, core, T, topo):
         K, W, X, D = PS[kb], PS[wb], PS[xb], PS[db]
         KB, WB, XB, DB = "#" + kb, "#" + wb, "#" + xb, "#" + db
         nn, nnk = T["NN" + C], "NN" + C
-        nv = NV[a]
+        nv = NV[t * 5 + a]
         tot, qr, QK = (2048, T.QZ, QZ) if a == 0 else (4096, T.QR, QA)
 
         def sl(i):
             return 5 + i if c == 0 else 5 - i
         if a:
-            V(lambda e: e.tensor_copy(nn[:, :], NB.indirect(T["VL" + C][:, 0:16])), ["NB", "VL" + C], [nnk], 256 * GAT)
+            VG(lambda e: e.tensor_copy(nn[:, :], NB.indirect(T["VL" + C][:, 0:16])), ["NB", "VL" + C], [nnk], 256)
             s0, s1 = nt(t, c, a - 1), nt(t, c, a)
             for b in (0, 1):
                 y = b * 128
@@ -382,36 +402,43 @@ def build(g, core, T, topo):
                 y = b * 128
                 TTo(T["M" + C][:, y:y + 128], nn[:, b::2], W[:, y:y + 128], OP.mult, [nnk, WB], ["M%s%d" % (C, b)], 128)
             TTo(T["T" + C][:, :], T["M" + C][:, :], W[:, 256:512], OP.add, ["M%s0" % C, "M%s1" % C, WB], ["T" + C], 256)
-            offsets(C, 256)
+            offsets(C, T["OF" + C][:, :], "OF" + C, 256)
+        of, o0, ofk = (T.OZ, c * 128, "OZ" + C) if a == 0 else (T["OF" + C], 0, "OF" + C)
         win = tab[:, 0:2048]
         dv, ab, xg = T["DV" + C], T["AB" + C], T["XG" + C]
-        parts, p = [], tot
-        while p > nv:
-            parts.insert(0, (max(nv, p - 512), p, "s"))
-            p = parts[0][0]
-        parts += [(z, min(nv, z + 512), "v") for z in range(0, nv, 512)]
+
+        def cut(p0, p1, w, e):
+            return [(z, min(p1, z + w), e) for z in range(p0, p1, w)]
+        nd = nv + ND[t * 5 + a]
+        parts = cut(nd, tot, 512, "s") + cut(0, nv, CHUNK[1], "v") + cut(nv, nd, 1024, "d")
 
         def keys(nm, p0, p1):
             return ["%s%s.%d" % (nm, C, z) for z in range(p0 // 128, (p1 + 127) // 128)]
-        for p0, p1, e in parts:
-            off = T["OF" + C][:, p0 // 16:p1 // 16]
+        for p0, p1, e in cut(nv, nd, 1024, "d") + cut(nd, tot, CHUNK[2], "s") + cut(0, nv, CHUNK[0], "v"):
+            off = of[:, o0 + p0 // 16:o0 + p1 // 16]
             if e == "v":
-                V(lambda en, p0=p0, p1=p1, off=off: en.tensor_tensor(dv[:, p0:p1], win.indirect(off), qr[:, p0:p1], OP.subtract),
-                  ["OF" + C, tkey] + QK, keys("dv", p0, p1), (p1 - p0) * GAT)
+                VG(lambda en, p0=p0, p1=p1, off=off: en.tensor_tensor(dv[:, p0:p1], win.indirect(off), qr[:, p0:p1], OP.subtract),
+                   [ofk, tkey] + QK, keys("dv", p0, p1), p1 - p0)
             else:
-                SG(xg[:, p0 - nv:p1 - nv], win.indirect(off), ["OF" + C, tkey], keys("XG", p0 - nv, p1 - nv), p1 - p0)
+                SG(xg[:, p0 - nv:p1 - nv], win.indirect(off), [ofk, tkey], keys("XG", p0 - nv, p1 - nv), p1 - p0)
+            if e == "d":
+                kk = keys("XG", p0 - nv, p1 - nv)
+                op("g", lambda p0=p0, p1=p1: g.dma_start(xg[:, p0 - nv:p1 - nv], T.NQ[:, p0 - 2048:p1 - 2048], accum_op=OP.add),
+                   kk + ["NQ"], kk, PLAN["gd"], "d", "ad" + C, 16, PLAN["ad"])
         kw = tot // 16
         MM(K[:, 0:kw], T.ON[0:33, 0:128], T.CR[:, 0:kw], True, False, ["ON", "CR"], [KB], 128, kw)
         BQ = T["BQ" + C]
         if a == 0:
             MM(K[:, 0:128], T["NP" + C][:, :], CH[:, PM0:PM0 + 128], False, False, ["NP" + C, "hP0"], [KB], 128, 128)
-            MM(K[:, 0:128], BQ[:, 0:128], BIGP, False, False, ["BQ%s0" % C, "BIGP"], [KB], 128, 128)
+            MM(K[:, 0:128], T.BQZ[:, c * 128:c * 128 + 128], BIGP, False, False, ["BQZ" + C, "BIGP"], [KB], 128, 128)
         else:
             for b in (0, 1):
                 MM(K[:, b * 128:b * 128 + 128], nn[:, b::2], I16, False, False, [nnk, "hI"], [KB], 128, 128)
         for p0, p1, e in parts:
             if e == "v":
                 S(ab[:, p0:p1], dv[:, p0:p1], FN.Abs, keys("dv", p0, p1), keys("ab", p0, p1), p1 - p0)
+            elif e == "d":
+                S(ab[:, p0:p1], xg[:, p0 - nv:p1 - nv], FN.Abs, keys("XG", p0 - nv, p1 - nv), keys("ab", p0, p1), p1 - p0)
             else:
                 w = p1 - p0
                 MM(D[:, 0:w], IB, xg[:, p0 - nv:p1 - nv], True, False, ["cI"] + keys("XG", p0 - nv, p1 - nv), [DB], 128, w)
@@ -430,7 +457,7 @@ def build(g, core, T, topo):
             s = nt(t, c, j)
             x0, j0 = (j % 2) * 256, j * 256
             for b in (0, 1):
-                MM(X[:, x0 + b:x0 + 256:2], CW[0:16, 1152 + b * 128:1280 + b * 128], NTs(s, 16), True, True, ["wE", "NT%d" % s], [XB], 128, 128)
+                MM(X[:, x0 + b:x0 + 256:2], CF[0:16, 128 + b * 128:256 + b * 128], NTs(s, 16), True, True, ["wE", "NT%d" % s], [XB], 128, 128)
             bk = "BQ%s%d" % (C, j)
             TTo(BQ[:, j0:j0 + 256], nn[:, :], X[:, x0:x0 + 256], OP.is_equal, [nnk, XB], [bk], 256)
             for b in (0, 1):
@@ -467,33 +494,34 @@ def build(g, core, T, topo):
     def lesser(el, tab, tk):
         for h in (0, 1):
             y = h * 1024
-            TS(T.TMP[:, y:y + 1024], tab[:, y:y + 1024], 0.75, OP.mult, [tk], ["TMP%d" % h], 512, 1024.375, OP.add)
-            TS(T[el][:, y:y + 1024], T.TMP[:, y:y + 1024], -1024.0, OP.add, ["TMP%d" % h], ["%s.%d" % (el, h)], 512)
+            TS(T[el][:, y:y + 1024], tab[:, y:y + 1024], 0.75, OP.mult, [tk], ["%s.%d" % (el, h)], 512, 1024.375, OP.add)
 
     def lessen(tab, tk, mk, el, out, okey, banks):
         for qd in range(4):
             b = banks[qd % len(banks)]
-            B = PS[b]
-            MM(B[:, :], IB, tab[:, qd * 512:qd * 512 + 512], True, False, ["cI", tk], ["#" + b], 128, 512)
+            B, ek, x = PS[b], "%s.%d" % (el, qd // 2), qd * 512
+            MM(B[:, :], IB, T[el][:, x:x + 512], True, False, ["cI", ek], ["#" + b], 128, 512)
             for z in range(4):
                 tt = (qd * 4 + z) * 128
-                MM(B[:, z * 128:z * 128 + 128], T.SELL[:, tt:tt + 128], T[mk][:, :], False, z == 3, ["SELL", mk], ["#" + b], 128, 128)
-            TTo(out[:, qd * 512:qd * 512 + 512], B[:, :], T[el][:, qd * 512:qd * 512 + 512], OP.max, ["#" + b, "%s.%d" % (el, qd // 2)], ["%s%d" % (okey, qd)], 512)
+                MM(B[:, z * 128:z * 128 + 128], T.SELL[:, tt:tt + 128], T[mk][:, :], False, z == 3, [SLK[qd], mk], ["#" + b], 128, 128)
+            TTo(out[:, x:x + 512], B[:, :], tab[:, x:x + 512], OP.min, ["#" + b, tk], ["%s%d" % (okey, qd)], 512)
 
-    def hot(c0, c1, kz, hk):
-        TS(T.WW[:, c0:c1], T.HH[:, c0:c1], 127, OP.bitwise_and, hk, ["WW" + kz], c1 - c0)
-        for m in range(c0 // 16, c1 // 16):
-            ws, ww = T.WS[:, m * 16:m * 16 + 16], T.WW[:, m * 16:m * 16 + 16]
-            if m in SHOT:
-                TS(ws, ww, -200.0, OP.mult, ["WW" + kz], ["WS%d" % m], 64, 100.0, OP.add)
-            else:
-                CP(ws, ww, ["WW" + kz], ["WS%d" % m], 64)
-        for col in sorted(range(c0, c1), key=lambda z: (z % 16, z)):
-            o, wk = T.OH[:, col * 128:col * 128 + 128], "WS%d" % (col // 16)
+    def thermo(out, bn, w, key, onv, low):
+        if onv:
+            TS(out, PS[bn][:, 0:w], 0.5 if low else -0.5, OP.is_le, ["#" + bn], [key], w)
+        else:
+            S(out, PS[bn][:, 0:w], FN.Sigmoid, ["#" + bn, "c100", "c101"], [key], w, bias=CC[:, 5:6] if low else CC[:, 4:5], scale=-200.0)
+
+    def hot(m0, m1, hk):
+        c0, c1, kz = m0 * 16, m1 * 16, str(m0)
+        TS(T.WW[:, c0:c1], T.HH[:, c0:c1], 63, OP.bitwise_and, hk, ["WW" + kz], c1 - c0)
+        TS(T.WS[:, c0:c1], T.WW[:, c0:c1], -200.0, OP.mult, ["WW" + kz], ["WS" + kz], c1 - c0, 100.0, OP.add)
+        for col in range(c0, c1):
+            o, w = T.OH[:, col * 64:col * 64 + 64], T.WS[:, col:col + 1]
             if col // 16 in SHOT:
-                S(o, T.IO[:, :], FN.Sigmoid, ["IO", wk], ["OH%d" % col], 128, bias=T.WS[:, col:col + 1], scale=200.0)
+                S(o, T.IO[:, 0:64], FN.Sigmoid, ["IO", "WS" + kz], ["OH%d" % col], 64, bias=w, scale=200.0)
             else:
-                TS(o, T.IO[:, :], T.WS[:, col:col + 1], OP.is_ge, ["IO", wk], ["OH%d" % col], 64)
+                TS(o, T.IH[:, :], w, OP.add, ["IH", "WS" + kz], ["OH%d" % col], 64, 0.0, OP.is_ge)
 
     def rings(t, tab, tk):
         P = "PT%d" % t
@@ -515,7 +543,9 @@ def build(g, core, T, topo):
         TTo(T.DX[:, 16:80], T.PX[:, 32:96], T.PX[:, 16:80], OP.subtract, ["PXa"], ["DXa"], 128)
         TTo(T.DX[:, 80:144], T.PX[:, 80:144], T.PX[:, 96:160], OP.subtract, ["PXa"], ["DXb"], 128)
         TTo(T.DX[:, 144:160], T.PX[:, 144:160], T.PX[:, 160:176], OP.subtract, ["PXa", "PXb"], ["DXc"], 64)
-        hot(16, 128, "e", ["HHe"])
+        hot(1, 8, ["HHe"])
+        hot(8, 9, hw[2:3])
+        hot(0, 1, hw[1:2])
         J = PS["wA"]
         MM(J[:, 0:400], T.ON[0:1, 0:128], T.IX[0:1, 0:400], True, False, ["ON", "IX"], ["#wA"], 128, 400)
         terms = [(i, j, s) for i in range(1, 6) for j in range(1, 6) for s in (5 + i, 5 - j) if i + j > 2]
@@ -544,7 +574,7 @@ def build(g, core, T, topo):
             o = J[:, z * 16:z * 16 + 16]
             MM(o, SI[:, x:x + 128], slot(s), True, False, ["SI%d" % x, pk[s]], ["#kA"], 128, 16)
             if x == I2:
-                MM(o, T.ON[0:1, 0:128], T.IX[0:1, 528:544], False, False, ["ON", "IXd"], ["#kA"], 128, 16)
+                MM(o, T.ON[0:1, 0:128], T.ON[0:1, 0:16], False, False, ["ON"], ["#kA"], 128, 16)
             for k in range(4):
                 MM(o, SI[:, x:x + 128], T.JP[:, z * 64 + k * 16:z * 64 + k * 16 + 16], False, k == 3, ["SI%d" % x, "JP%d" % z], ["#kA"], 128, 16)
         UA, PJ = JS[:, 0:16], JS[:, 16:32]
@@ -560,60 +590,65 @@ def build(g, core, T, topo):
         CP(T.HT[:, 0:128], X[0:80, 0:128], ["#xA"], ["HT0"], 128)
         MM(X[0:80, 128:256], T.HV[:, 80:160], I16, True, True, ["HVb", "HVc", "hI"], ["#xA"], 80, 128)
         CP(T.HT[:, 128:256], X[0:80, 128:256], ["#xA"], ["HT1"], 128)
-        MM(X2[:, 0:128], CH[0:80, PR1:PR1 + 128], T.HT[:, 0:128], True, False, ["hPR", "HT0"], ["#xB"], 128, 128)
-        MM(X2[:, 0:128], CH[0:80, PR2:PR2 + 128], T.HT[:, 128:256], False, True, ["hPR", "HT1"], ["#xB"], 128, 128)
+        MM(X2[:, 0:128], CH[0:80, PR1:PR1 + 128], T.HT[:, 0:128], True, False, ["cR1", "HT0"], ["#xB"], 128, 128)
+        MM(X2[:, 0:128], CH[0:80, PR2:PR2 + 128], T.HT[:, 128:256], False, True, ["cR2", "HT1"], ["#xB"], 128, 128)
         for z in range(4):
-            MM(X2[:, 128:160], CH[0:80, PTZ + z * 128:PTZ + z * 128 + 128], T.HT[:, 128 + z:256:4], z == 0, z == 3, ["hPR", "HT1"], ["#xB"], 128, 32)
+            MM(X2[:, 128:160], CH[0:80, PTZ + z * 128:PTZ + z * 128 + 128], T.HT[:, 128 + z:256:4], z == 0, z == 3, ["cZ%d" % z, "HT1"], ["#xB"], 128, 32)
         CP(T.OFR[:, :], X2[:, 0:160], ["#xB"], ["OFR"], 160)
         win = tab[:, 0:2064]
-        for h in (1, 0):
-            for x0, ln in ((h * 1024, 1024), (2048 + h * 256, 256)):
+        for h in (0, 1):
+            for e, x0, ln in (("v", h * 1024, XV[0]), ("s", h * 1024 + XV[0], 1024 - XV[0]), ("s", 2048 + h * 256, 256)):
                 xo, fo = T.XR[:, x0:x0 + ln], T.OFR[:, x0 // 16:(x0 + ln) // 16]
-                if h:
-                    SG(xo, win.indirect(fo), ["OFR", tk, tk + "z"], ["XR%d.%d" % (h, ln)], ln)
+                if e == "s":
+                    SG(xo, win.indirect(fo), ["OFR", tk, tk + "z"], ["XR%d" % x0], ln)
                 else:
-                    V(lambda e, xo=xo, fo=fo: e.tensor_copy(xo, win.indirect(fo)), ["OFR", tk, tk + "z"], ["XR%d.%d" % (h, ln)], ln * GAT)
-        hot(0, 16, "a", hw[1:2])
-        hot(128, 144, "b", hw[2:3])
-        hot(144, 160, "c", ["HHb"])
+                    VG(lambda e, xo=xo, fo=fo: e.tensor_copy(xo, win.indirect(fo)), ["OFR", tk, tk + "z"], ["XR%d" % x0], ln)
+        hot(9, 10, ["HHb"])
         B, W = PS["kB"], PS["wB"]
         MM(W[0:80, 0:128], T.ON[0:1, 0:80], T.IX[0:1, 400:528], True, False, ["ON", "IXc"], ["#wB"], 80, 128)
-        for b in (0, 1):
-            for m in range(10):
-                xs = T.XR[:, 2 * m + b:2048:16] if m < 8 else T.XR[:, 2032 + 2 * m + b:2560:4]
-                ln = 1024 if m < 8 else 256
-                MM(B[:, b * 128:b * 128 + 128], IB, xs, m == 0, m == 9, ["cI", "XR0.%d" % ln, "XR1.%d" % ln], ["#kB"], 128, 128)
+        for h in (0, 1):
+            for b in (0, 1):
+                for m in range(10):
+                    x0 = h * 1024 if m < 8 else 2048 + h * 256
+                    xs = T.XR[:, x0 + 2 * m + b:x0 + 1024:16] if m < 8 else T.XR[:, x0 + 2 * m - 16 + b:x0 + 256:4]
+                    y = b * 128 + h * 64
+                    MM(B[:, y:y + 64], IB, xs, m == 0, m == 9, ["cI", "XR%d" % x0] + (["XR%d" % (x0 + XV[0])] if m < 8 else []), ["#kB"], 128, 64)
         TS(T.CMP[:, :], B[:, 0:256], T.THF[:, 0:1], OP.is_ge, ["#kB", "THF"], ["CMP"], 256)
         for b in (0, 1):
             MM(W[0:80, 0:128], T.RC[:, b * 80:b * 80 + 80], T.CMP[:, b * 128:b * 128 + 128], False, b == 1, ["CMP", "RC"], ["#wB"], 80, 128)
         for h in (0, 1):
             TTo(T.TM[0:80, h * 128:h * 128 + 128], T.HT[:, h * 128:h * 128 + 128], W[0:80, 0:128], OP.max, ["HT%d" % h, "#wB", "TMz"], ["TM%d" % h], 128)
         z = 0
-        for c0, c1 in ((0, 384), (384, 768), (768, 1280)):
+        for b, cn in ((0, "xB"), (1, "kB")):
+            C = PS[cn]
+            MM(C[:, 0:256], T.ON[0:1, 0:128], T.IX[0:1, 544:800], True, False, ["ON", "IXz"], ["#" + cn], 128, 256)
             for h in (0, 1):
-                bn = ("xA", "wA", "kA")[z % 3]
-                z += 1
-                MM(PS[bn][:, 0:c1 - c0], T.TM[:, h * 128:h * 128 + 128], T.RH[:, c0:c1], True, True, ["TM%d" % h, "TMz", "RH"], ["#" + bn], 128, c1 - c0)
-                S(T.TL[:, h * 1280 + c0:h * 1280 + c1], PS[bn][:, 0:c1 - c0], FN.Sigmoid, ["#" + bn, "c100"], ["TL%d.%d" % (h, c0)], c1 - c0,
-                  bias=CC[:, 4:5], scale=-200.0)
-        for b, bn in ((0, "xB"), (1, "kB")):
-            for gr in range(8):
-                for m in range(10):
-                    col = m * 16 + b * 8 + gr
-                    l0 = (col % 80) * 16
-                    MM(PS[bn][:, gr:128:8], T.OH[:, col * 128:col * 128 + 128], T.TL[:, col * 16:col * 16 + 16], m == 0, m == 9,
-                       ["OH%d" % col, "TL%d.%d" % (col // 80, 0 if l0 < 384 else (384 if l0 < 768 else 768))], ["#" + bn], 128, 16)
-            CP(T.C2[:, 8 + b * 136:136 + b * 136], PS[bn][:, 0:128], ["#" + bn], ["C2%d" % b], 128)
-        for b in (0, 1):
-            y = b * 136
-            MM(W[:, 0:128], T.C2[:, 8 + y:136 + y], CH[:, DM:DM + 128], b == 0, False, ["C2%d" % b, "hDM"], ["#wB"], 128, 128)
-            MM(W[:, 0:128], T.C2[:, y:128 + y], CH[:, NDM:NDM + 128], False, b == 1, ["C2%d" % b, "C2y", "C2z", "hND"], ["#wB"], 128, 128)
-        S(T.MKT[:, :], W[:, 0:128], FN.Sign, ["#wB"], ["MKT"], 128)
+                for y, ms in enumerate(((0, 1), (2, 3), (4,))):
+                    bn, w = ("xA", "wA", "kA")[z % 3], 256 * len(ms)
+                    x = (b * 2 + h) * 1280 + y * 512
+                    MM(PS[bn][:, 0:w], T.TM[:, h * 128:h * 128 + 128], T.RT[:, b * 1280 + y * 512:b * 1280 + y * 512 + w], True, True,
+                       ["TM%d" % h, "TMz", RTK[b * 3 + y], RTK[6]], ["#" + bn], 128, w)
+                    thermo(T.TL[:, x:x + w], bn, w, "TL%d" % z, HIV[0] and z % HIV[0] == HIV[0] - 1, False)
+                    for m in ms:
+                        for gp in range(4):
+                            col, l0 = (h * 5 + m) * 16 + b * 8, (b * 2 + h) * 1280 + m * 256 + gp * 64
+                            MM(C[:, gp:256:4], T.OH[:, (col + 2 * gp) * 64:(col + 2 * gp) * 64 + 128], T.TL[:, l0:l0 + 64], False,
+                               h == 1 and m == 4 and gp == 3, ["OH%d" % (col + 2 * gp), "OH%d" % (col + 2 * gp + 1), "TL%d" % z], ["#" + cn], 128, 64)
+                    z += 1
+            for h in (0, 1):
+                CP(T.C3[h * 64:h * 64 + 64, b * 264 + 8 + h:b * 264 + 264:2], C[h * 64:h * 64 + 64, h * 128:h * 128 + 128], ["#" + cn], ["C3%d%d" % (b, h)], 128)
+        for x, p0, p1 in ((64, 8, 136), (0, 136, 0)):
+            for b in (0, 1):
+                y, ck = b * 264, ["C3%d0" % b, "C3%d1" % b]
+                MM(W[:, x:x + 64], T.C3[:, y + p0:y + p0 + 128], CB[:, DM:DM + 64], b == 0, False, ck + ["cDM"], ["#wB"], 128, 64)
+                MM(W[:, x:x + 64], T.C3[:, y + p1:y + p1 + 128], CB[:, NDM:NDM + 64], False, b == 1, ck + ["cND"], ["#wB"], 128, 64)
+        S(T.MKT[:, :], W[:, 0:128], FN.Sign, ["#wB", "c05"], ["MKT"], 128, bias=CC[:, 6:7], scale=-1.0)
 
-    def show(t):
+    def show(t, bn):
         P = "PT%d" % t
         pt, JS = T[P], T.JS
-        D, E = PS["dA"], PS["dB"]
+        D = E = PS[bn]
+        DB = "#" + bn
         J0, JJ = T.JI[:, 16:32], T.JI[:, 32:48]
         TTo(JS[:, 32:48], J0, JJ, OP.subtract, ["J0", "JJ"], ["Y8"], 64)
         TS(JS[:, 48:64], J0, 8.0, OP.is_ge, ["J0"], ["YF"], 64)
@@ -621,59 +656,68 @@ def build(g, core, T, topo):
         TTo(T.IL[:, 0:16], JS[:, 64:80], JS[:, 48:64], OP.add, ["YI", "YF"], ["ILi"], 64)
         TTo(JS[:, 80:96], JJ, JS[:, 48:64], OP.mult, ["JJ", "YF"], ["YJ"], 64)
         TTo(T.IL[:, 16:32], JS[:, 64:80], JS[:, 80:96], OP.add, ["YI", "YJ"], ["ILl"], 64)
-        MM(E[0:96, 0:128], pt[:, 80:176], I16, True, True, [P + "s%d" % i for i in range(5, 11)] + ["hI"], ["#dB"], 96, 128)
-        CP(T.AT[:, :], E[0:96, 0:128], ["#dB"], ["AT"], 128)
+        MM(E[0:96, 0:128], pt[:, 80:176], I16, True, True, [P + "s%d" % i for i in range(5, 11)] + ["hI"], [DB], 96, 128)
         for z, k in ((0, "ILi"), (1, "ILl")):
-            MM(D[0:16, z * 128:z * 128 + 128], T.IL[:, z * 16:z * 16 + 16], I16, True, True, [k, "hI"], ["#dA"], 16, 128)
-        CP(T.LT[:, :], D[0:16, 0:256], ["#dA"], ["LT"], 256)
+            MM(D[0:16, 128 + z * 128:256 + z * 128], T.IL[:, z * 16:z * 16 + 16], I16, True, True, [k, "hI"], [DB], 16, 128)
+        CP(T.AT[:, :], E[0:96, 0:128], [DB], ["AT"], 128)
+        S(T.LT[:, :], D[0:16, 128:384], FN.Copy, [DB], ["LT"], 256)
         for b in (0, 1):
-            eb = CW[0:16, 1152 + b * 128:1280 + b * 128]
+            eb = CF[0:16, 128 + b * 128:256 + b * 128]
             for z in (0, 1):
-                MM(D[:, z * 256 + b:z * 256 + 256:2], eb, T.LT[:, z * 128:z * 128 + 128], True, True, ["wE", "LT"], ["#dA"], 128, 128)
-            MM(E[:, b:256:2], CH[0:96, PAB + b * 128:PAB + b * 128 + 128], T.AT[:, :], True, True, ["hAB", "AT"], ["#dB"], 128, 128)
+                MM(D[:, z * 256 + b:z * 256 + 256:2], eb, T.LT[:, z * 128:z * 128 + 128], True, True, ["wE", "LT"], [DB], 128, 128)
         R1, R2 = D[:, 0:256], D[:, 256:512]
-        TS(T.YM[:, :], R1, CC[:, 13:14], OP.is_ge, ["#dA", "cM5"], ["YM"], 256, 2048.0, OP.mult)
-        TTo(T.YP[:, :], T.YM[:, :], R2, OP.max, ["#dA", "YM"], ["YP"], 256)
-        TS(T.YB[:, 256:512], R2, CC[:, 13:14], OP.is_le, ["#dA", "cM5"], ["YB1"], 256, -1.0, OP.mult)
-        TTo(T.YB[:, 0:256], T.YM[:, :], E[:, 0:256], OP.min, ["#dB", "YM"], ["YB0"], 256)
-        for j in range(1, 5):
-            k0 = (j % 2) * 256
-            s = nt(t, 1, j)
-            for b in (0, 1):
-                MM(E[:, 256 + b:512:2], CW[0:16, 1152 + b * 128:1280 + b * 128], NTs(s, 16), True, True, ["wE", "NT%d" % s], ["#dB"], 128, 128)
-            TS(T.YK[:, k0:k0 + 256], T.YP[:, :], CC[:, 8 + j:9 + j], OP.is_equal, ["YP", "cM%d" % j], ["YK%d" % (j % 2)], 128)
-            TTo(T.YB[:, 256 + j * 256:512 + j * 256], T.YK[:, k0:k0 + 256], E[:, 256:512], OP.mult, ["YK%d" % (j % 2), "#dB"], ["YB%d" % (j + 1)], 256)
+        TS(T.YM[:, :], R1, CC[:, 13:14], OP.is_ge, [DB, "cM5"], ["YM"], 256, 2048.0, OP.mult)
+        TTo(T.YP[:, :], T.YM[:, :], R2, OP.max, [DB, "YM"], ["YP"], 256)
+        TS(T.YB[:, 256:512], R2, CC[:, 13:14], OP.is_le, [DB, "cM5"], ["YB1"], 256, -1.0, OP.mult)
+        for j0, js in ((0, (0, 1)), (2, (2, 3)), (4, (4,))):
+            for j in js:
+                x, s = (j - j0) * 256, nt(t, 1, j)
+                for b in (0, 1):
+                    if j:
+                        MM(E[:, x + b:x + 256:2], CF[0:16, 128 + b * 128:256 + b * 128], NTs(s, 16), True, True, ["wE", "NT%d" % s], [DB], 128, 128)
+                    else:
+                        MM(E[:, b:256:2], CH[0:96, PAB + b * 128:PAB + b * 128 + 128], T.AT[:, :], True, True, ["hAB", "AT"], [DB], 128, 128)
+            for j in js:
+                x, k0 = (j - j0) * 256, (j % 2) * 256
+                if j:
+                    TS(T.YK[:, k0:k0 + 256], T.YP[:, :], CC[:, 8 + j:9 + j], OP.is_equal, ["YP", "cM%d" % j], ["YK%d" % (j % 2)], 128)
+                    TTo(T.YB[:, 256 + j * 256:512 + j * 256], T.YK[:, k0:k0 + 256], E[:, x:x + 256], OP.mult, ["YK%d" % (j % 2), DB], ["YB%d" % (j + 1)], 256)
+                else:
+                    TTo(T.YB[:, 0:256], T.YM[:, :], E[:, 0:256], OP.min, [DB, "YM"], ["YB0"], 256)
         for z in range(6):
-            MM(D[:, 0:256], I16, T.YB[:, z * 256:z * 256 + 256], z == 0, z == 5, ["hI", "YB%d" % z], ["#dA"], 128, 256)
-        S(T.YR[:, :], D[:, 0:256], FN.Copy, ["#dA"], ["YR"], 256)
+            MM(D[:, 0:256], I16, T.YB[:, z * 256:z * 256 + 256], z == 0, z == 5, ["hI", "YB%d" % z], [DB], 128, 256)
+        S(T.YR[:, :], D[:, 0:256], FN.Copy, [DB], ["YR"], 256)
         DMA("y", T.yr[:, t * 256:t * 256 + 256], T.YR[:, :], ["YR"], [])
 
-    start(0)
+    start(0, ("dA", "dB"))
     ring_constants()
-    lesser("EL0", T.TO, "TO")
+    own = "EL0"
+    lesser(own, T.TO, "TO")
     for k in (4, 5):
         send(k, ["TP0"])
     arrive("TPn", "aTPn", (r + 2) % n, 50.0, ["sent4", "sent5"])
     for a in range(5):
         step(0, 0, a, T.TO, "TO")
         step(0, 1, a, T.TP0, "TP0")
+        if a == 1:
+            start(1, ("wA", "wB"))
     lesser("ELn", T.TPn, "TPn")
-    start(1)
     rings(0, T.TO, "TO")
     send(6)
     arrive("MKP", "aMK", (r + 2) % n, PLAN["mk"], ["sent6"])
-    show(0)
-    lessen(T.TO, "TO", "MKT", "EL0", T.TO1, "T1q", ("kA", "wA", "xA"))
+    lessen(T.TO, "TO", "MKT", own, T.TO1, "T1q", ("dA", "dB", "xA", "wA"))
     op(None, None, ["T1q%d" % q for q in range(4)], ["TO1"], 0.0, "n")
     lessen(T.TPn, "TPn", "MKP", "ELn", T.TP1, "P1q", ("wB", "xB"))
     op(None, None, ["P1q%d" % q for q in range(4)], ["TP1"], 0.0, "n")
     for a in range(5):
         step(1, 0, a, T.TO1, "TO1")
         step(1, 1, a, T.TP1, "TP1")
-    lesser("EL0", T.TO1, "TO1")
+        if a == 0:
+            show(0, "wA")
+    lesser(own, T.TO1, "TO1")
     rings(1, T.TO1, "TO1")
-    show(1)
-    lessen(T.TO1, "TO1", "MKT", "EL0", T.TO2, "T2q", ("kA", "wA", "xA"))
+    show(1, "dB")
+    lessen(T.TO1, "TO1", "MKT", own, T.TO2, "T2q", ("dA", "xA", "wA", "kA"))
     for qd in range(4):
         DMA("y" if qd % 2 == 0 else "s", T.ye[:, qd * 512:qd * 512 + 512], T.TO2[:, qd * 512:qd * 512 + 512], ["T2q%d" % qd], [])
     for o in ops:
@@ -747,16 +791,32 @@ def schedule(ops):
     way = [0.0] * n
     for i in range(n - 1, -1, -1):
         way[i] = max([way[j] + lag - ops[j]["cost"] for j, lag in back[i]] + [ops[i]["lat"]]) + ops[i]["cost"]
-    rank = [-way[i] - ops[i]["bon"] for i in range(n)]
-    best = None
-    for z in range(PLAN["turns"]):
-        start, seq = place(ops, fwd, rank)
-        end = max(start[i] + full[i] for i in range(n))
+    def lasts(order, f):
+        fin, free = [0.0] * n, {}
+        for i in order:
+            o = ops[i]
+            q, s = o["q"], free.get(o["q"], 0.0) if o["q"] else 0.0
+            for d in o["deps"]:
+                s = max(s, fin[d] + (PLAN["wake"] if ops[d]["q"] != q else PLAN["same"]))
+            free[q] = s + o["cost"] * f.get(q, 1.0) * (f["gat"] if o["gat"] else 1.0)
+            fin[i] = free[q] + o["lat"]
+        return max(fin)
+
+    def turn(start, shake):
+        rank = []
+        for i in range(n):
+            seed[0] = (seed[0] * 1103515245 + 12345) % 2147483648
+            rank.append(-(start[i] + full[i]) + shake * seed[0] / 2147483648.0)
+        rs, _ = place(ops, back, rank)
+        start, seq = place(ops, fwd, [-(rs[i] + ops[i]["cost"]) for i in range(n)])
+        order = sorted(range(n), key=lambda i: (start[i], seq[i]))
+        end = sum(lasts(order, f) for f in OTHERS) / len(OTHERS)
         ORDERS.setdefault("ends", []).append(end)
-        if best is None or end < best[0]:
-            best = (end, start, seq)
-        rs, _ = place(ops, back, [-(start[i] + full[i]) for i in range(n)])
-        rank = [-(rs[i] + ops[i]["cost"]) for i in range(n)]
+        return end, start, seq
+    seed = [1]
+    best = min(turn(place(ops, fwd, [-way[i] - lead * ops[i]["bon"] for i in range(n)])[0], 0.0) for lead in LEADS)
+    for z in range(PLAN["turns"]):
+        best = min(best, turn(best[1], PLAN["shake"]))
     return sorted(range(n), key=lambda i: (best[1][i], best[2][i]))
 
 
@@ -797,7 +857,8 @@ def emit(g, T, ops, order):
             mark[i] = (s, count[s])
         elif o["kind"] == "d":
             ins.then_inc(T.sem[o["sem"]], 16)
-            mark[i] = (o["sem"], 16)
+            count[o["sem"]] = count.get(o["sem"], 0) + 16
+            mark[i] = (o["sem"], count[o["sem"]])
         else:
             mark[i] = (o["sem"], o["val"])
         final[mark[i][0]] = mark[i][1]

@@ -6,51 +6,44 @@ FN = ActivationFunctionType
 BIG = float(2 ** 26)
 REST = 2041 * 8192
 F32, B16, H16, I32, U16 = "float32", "bfloat16", "float16", "int32", "uint16"
-NV = [1024, 2304, 2304, 2304, 2304, 1024, 2304, 2304, 2304, 2304]
-CHUNK = [512, 512, 512]
-SHOT = [0, 1, 2, 3, 8, 9]
-HIV = [2]
-XV = [640]
-QS = [2, 3]
-ND = [0, 0, 0, 0, 0, 0, 0, 0, 0, 0]
-NQW = 1536
+NV = [1024, 2304, 2432, 2304, 2432]
+HIV = [7, 15]
+XV = 640
 SCRATCH = {}
 for _n, _p, _w, _t in (
-        ("NQ", 128, NQW, B16),
-        ("NB", 128, 1024, I32), ("XI", 128, 176, I32), ("XJ", 128, 176, I32), ("TO", 128, 2064, B16), ("TO1", 128, 2064, B16), ("TO2", 128, 2048, B16),
+        ("NB", 128, 1024, I32), ("XI", 128, 8, I32), ("XJ", 128, 8, I32), ("DH", 128, 32, F32), ("TO", 128, 2064, B16), ("TO1", 128, 2064, B16), ("TO2", 128, 2048, B16),
         ("TP0", 128, 2048, B16), ("TPn", 128, 2048, B16), ("TP1", 128, 2048, B16), ("EL0", 128, 2048, H16), ("ELn", 128, 2048, H16),
         ("ST", 128, 32, I32), ("SU", 128, 32, U16), ("STH", 128, 32, H16), ("TH", 128, 1, I32),
         ("THF", 128, 1, F32), ("Q", 128, 256, B16), ("QR", 128, 4096, B16), ("QZ", 128, 2048, B16), ("ON", 128, 512, B16), ("CB", 128, 2144, B16),
-        ("SI", 128, 640, B16), ("CG", 128, 384, B16), ("CF", 17, 384, B16), ("CW", 17, 1152, H16), ("CC", 128, 32, F32), ("C9", 128, 512, B16), ("C8", 1, 512, B16),
-        ("VH", 16, 1024, B16), ("SELL", 128, 2048, B16), ("S8", 128, 8, B16), ("RC", 128, 160, B16), ("RS", 128, 16, F32),
-        ("CR", 33, 256, B16), ("RT", 97, 2560, B16), ("IO", 128, 64, B16), ("IH", 128, 64, H16), ("IX", 1, 800, B16),
+        ("SI", 128, 640, B16), ("CG", 128, 384, B16), ("CF", 17, 384, B16), ("CW", 17, 1152, H16), ("CC", 128, 32, F32), ("C9", 128, 512, B16),
+        ("VH", 16, 1024, B16), ("SELL", 128, 2048, B16), ("S8", 128, 8, B16), ("RS", 128, 16, F32),
+        ("CR", 33, 256, B16), ("RT", 97, 2560, B16), ("IO", 128, 128, B16), ("DF", 128, 130, F32), ("IX", 1, 800, B16),
         ("NT", 17, 1792, H16), ("MZ", 128, 128, F32), ("TZ", 128, 128, I32), ("BZ", 128, 128, I32), ("OZ", 128, 256, U16), ("BQZ", 128, 256, B16),
         ("NZ", 128, 256, H16), ("PT0", 128, 176, H16), ("PT1", 128, 176, H16), ("NP0", 128, 128, H16), ("NP1", 128, 128, H16),
         ("DZ", 128, 128, F32), ("U", 128, 176, F32), ("PR", 128, 144, F32), ("V5", 128, 144, F32), ("PX", 128, 176, F32), ("DX", 128, 160, F32),
         ("TT", 128, 160, I32), ("HH", 128, 160, I32), ("JA", 128, 400, B16), ("JD", 128, 400, B16), ("JC", 128, 400, B16),
-        ("JI", 128, 64, I32), ("JS", 128, 96, F32), ("IL", 128, 32, H16), ("NM", 128, 160, F32), ("JP", 128, 192, H16),
-        ("WW", 128, 160, I32), ("WS", 128, 160, F32), ("HV", 128, 160, H16), ("HT", 80, 256, H16), ("OFR", 128, 160, U16),
-        ("XR", 128, 2560, B16), ("CMP", 128, 256, B16), ("TM", 97, 256, H16), ("OH", 128, 10240, B16), ("TL", 128, 5120, B16), ("C3", 128, 528, H16),
+        ("JI", 128, 80, I32), ("JS", 128, 96, F32), ("IL", 128, 32, H16), ("NM", 128, 160, F32), ("JP", 128, 192, H16),
+        ("WX", 128, 160, I32), ("WS", 128, 160, B16), ("HV", 128, 160, H16), ("HT", 97, 256, H16), ("HY", 128, 16, B16), ("OFR", 128, 160, U16),
+        ("XR", 128, 2560, B16), ("CMP", 128, 256, B16), ("OH", 128, 10240, B16), ("TL", 128, 5120, B16), ("C3", 128, 264, F32),
         ("MKT", 128, 128, B16), ("MKP", 128, 128, B16), ("AT", 96, 128, H16), ("LT", 16, 256, B16),
-        ("YM", 128, 256, H16), ("YP", 128, 256, H16), ("YK", 128, 512, H16), ("YB", 128, 1536, H16), ("YR", 128, 256, F32)):
+        ("NE", 16, 256, B16), ("YK", 128, 1536, B16), ("YB", 128, 1280, H16), ("YR", 128, 256, F32)):
     SCRATCH[_n] = ("sbuf", [_p, _w], _t)
 for _c in "01":
     for _n, _w, _t in (("NN", 256, H16), ("M", 256, F32), ("T", 256, I32), ("B", 256, I32), ("OF", 256, U16), ("DV", 2560, B16),
-                       ("AB", 4096, B16), ("XG", 3072, B16), ("BQ", 1280, B16), ("D", 256, F32), ("SC", 256, F32),
-                       ("K", 32, I32), ("KD", 48, F32), ("SH", 32, I32), ("R", 32, I32), ("VL", 16, U16)):
+                       ("AB", 4096, B16), ("XG", 2048, B16), ("BQ", 1280, B16), ("D", 256, F32), ("SC", 256, I32),
+                       ("K", 32, I32), ("L", 32, I32), ("R", 16, I32), ("VL", 16, U16)):
         SCRATCH[_n + _c] = ("sbuf", [128, _w], _t)
 BANKS = ("kA", "kB", "wA", "wB", "xA", "xB", "dA", "dB")
 for _b in BANKS:
     SCRATCH[_b] = ("psum", [128, 512], F32)
 NITEM = 7
-NDMA = 14
-SEMAPHORES = ["v", "s", "t", "gc", "aTP0", "aTPn", "aMK", "ad0", "ad1"] + ["d%d" % i for i in range(NDMA)]
+NDMA = 17
+SEMAPHORES = ["v", "s", "t", "gc", "aTP0", "aTPn", "aMK"] + ["d%d" % i for i in range(NDMA)]
 SEMAPHORES += ["ri%d" % i for i in range(NITEM)] + ["lo%d" % i for i in range(NITEM)]
 
-PLAN = dict(cy=0.00100, tcy=0.00075, gat=1.5, wake=0.12, same=0.05, lead=1.0, tp0=12.0, mk=7.0, turns=8, shake=0.4, gd=1.0, ad=4.5)
-OTHERS = [dict(gat=1.0), dict(gat=0.8, t=1.15), dict(gat=1.25, t=0.85)]
+PLAN = dict(cy=0.00100, tcy=0.00075, gat=1.5, wake=0.12, same=0.05, tp0=12.0, mk=7.0, turns=900, shake=0.5, wide=10.0)
+OTHERS = [dict(gat=1.0, far=0.0), dict(gat=0.8, t=1.15, far=0.3), dict(gat=1.25, t=0.85, far=-0.3)]
 LEADS = [5.0, 5.5, 6.0, 6.5]
-HINT = {}
 ORDERS = {}
 
 
@@ -100,21 +93,14 @@ def hand_on(g, core, T, topo):
 def build(g, core, T, topo):
     ops = []
     lastw, reads, bank = {}, {}, {}
-    bon = [0.0]
+    bon = [0.0, False]
     CY, TCY, GAT = PLAN["cy"], PLAN["tcy"], PLAN["gat"]
 
-    def hint(q, W):
-        if not W or q is None:
-            return 0.0
-        w = W[0].split(".")[0]
-        for name in (w, w[:3], "".join(c for c in w if not c.isdigit())):
-            if q + name in HINT:
-                return HINT[q + name]
-        return 0.0
+    same = {"hI": "cI", "hPV": "cPV", "hP0": "cP0", "w03": "cE0", "wE": "cEB", "hAB": "cAB"}
 
     def op(q, fn, R, W, cost, kind="c", sem=None, val=1, lat=0.0):
         n = len(ops)
-        R = [{"hI": "cI", "hPV": "cPV", "hP0": "cP0", "w03": "cE0", "wE": "cEB", "hAB": "cAB"}.get(k, k) for k in R]
+        R = [same.get(k, k) for k in R]
         deps, order = set(), set()
         for k in list(R) + list(W):
             if k[0] == "#":
@@ -124,7 +110,7 @@ def build(g, core, T, topo):
                         order.add(b[e][-1])
                     elif e != "last":
                         deps.update(b[e])
-                b[q] = b[q] + [n] if b.get("last") == [q] else [n]
+                b[q] = b[q] + [n] if b.get("last") == [q] and q != "t" else [n]
                 b["last"] = [q]
         for k in R:
             if k[0] != "#":
@@ -140,7 +126,7 @@ def build(g, core, T, topo):
                 reads[k] = []
         deps.discard(n)
         order.discard(n)
-        ops.append(dict(q=q, fn=fn, deps=deps, order=(order - deps if q == "t" else set()), cost=cost, lat=lat, kind=kind, sem=sem, val=val, bon=bon[0] + hint(q, W), gat=False))
+        ops.append(dict(q=q, fn=fn, deps=deps, order=(order - deps if q == "t" else set()), cost=cost, lat=lat, kind=kind, sem=sem, val=val, bon=bon[0], gat=False))
 
     def V(fn, R, W, n):
         op("v", lambda: fn(g.vector), R, W, max(64, n) * CY + 0.03)
@@ -165,7 +151,9 @@ def build(g, core, T, topo):
         V(lambda e: e.memset(ap, c), R, W, n)
 
     def S(out, a, f, R, W, n, **kw):
-        op("s", lambda: g.scalar.activation(out, a, f, **kw), R, W, max(64, n) * CY + 0.05)
+        first = 1.3 if f == FN.Sigmoid and not bon[1] else 0.0
+        bon[1] = bon[1] or f == FN.Sigmoid
+        op("s", lambda: g.scalar.activation(out, a, f, **kw), R, W, max(64, n) * CY + 0.05 + first)
 
     def SG(out, a, R, W, n):
         op("s", lambda: g.scalar.activation(out, a, FN.Copy), R, W, n * GAT * CY + 0.07)
@@ -188,18 +176,20 @@ def build(g, core, T, topo):
 
     nd = [0]
 
-    def DMA(q, out, a, R, W):
+    def DMA(q, out, a, R, W, lat=2.5):
         s = "d%d" % nd[0]
         nd[0] += 1
         eng = g.sync if q == "y" else g.scalar
-        op(q, lambda: eng.dma_start(out, a), R, W, 0.06, "d", s, 16, 2.5)
+        op(q, lambda: eng.dma_start(out, a), R, W, 0.06, "d", s, 16, lat)
 
     PS = {b: T[b] for b in BANKS}
 
     DMA("y", T.ST[:, :], T.st[:, :], [], ["ST"])
-    DMA("s", T.TO[:, 0:2048], T.ang[:, :], [], ["TO"])
-    DMA("y", T.NB[:, :], T.nb[:, :], [], ["NB"])
-    DMA("s", T.Q[:, :], T.q[:, :], [], ["Q"])
+    for z, x in enumerate((0, 1024, 512, 1536)):
+        DMA("s", T.TO[:, x:x + 512], T.ang[:, x:x + 512], [], ["TO%d" % x], 2.8 + 0.6 * z)
+    op(None, None, ["TO%d" % x for x in range(0, 2048, 512)], ["TO"], 0.0, "n")
+    DMA("y", T.NB[:, :], T.nb[:, :], [], ["NB"], 4.8)
+    DMA("s", T.Q[:, :], T.q[:, :], [], ["Q"], 3.0)
     DMA("y", T.TH[:, :], T.th[:, :], [], ["TH"])
 
     CB, CH, CG, CF, CW, CC = T.CB, T.CB, T.CG, T.CF, T.CW, T.CC
@@ -234,84 +224,85 @@ def build(g, core, T, topo):
     TS(T.S8[:, :], T.XJ[:, 0:8], 0.0, OP.is_equal, ["XJ"], ["S8"], 64, 8192.0, OP.mult)
     fill(T.CR[0:32, :], 0.0, ["CR"], ["CR"], 128)
     fill(T.CR[0:1, :], -16711680.0, ["CR"], ["CR"], 128)
-    TS(NEGI, IB, -1.0, OP.mult, ["cI"], ["NEGI"], 64)
-    TS(BIGI, IB, BIG, OP.mult, ["cI"], ["BIGI"], 64)
-    TS(BIGP, CB[:, PM0:PM0 + 128], BIG, OP.mult, ["cP0"], ["BIGP"], 64)
-    fill(T.DZ[:, :], -BIG, [], ["DZ"], 128)
+    S(NEGI, IB, FN.Copy, ["cI"], ["NEGI"], 128, scale=-1.0)
+    S(BIGI, IB, FN.Copy, ["cI"], ["BIGI"], 128, scale=BIG)
+    S(BIGP, CB[:, PM0:PM0 + 128], FN.Copy, ["cP0"], ["BIGP"], 128, scale=BIG)
+    S(T.DZ[:, :], T.ON[:, 0:128], FN.Copy, ["ON"], ["DZ"], 128, scale=-BIG)
     for c in "01":
-        fill(T["D" + c][:, :], -BIG, [], ["D" + c], 256)
-        TS(T["D" + c][:, 8::16], T.RS[:, :], 2047.0, OP.add, ["RS", "D" + c], ["D" + c], 64)
+        S(T["D" + c][:, :], T.ON[:, 0:256], FN.Copy, ["ON"], ["D" + c], 256, scale=-BIG)
+        S(T["D" + c][:, 8::16], T.RS[:, :], FN.Copy, ["RS", "D" + c], ["D" + c], 64, bias=2047.0)
+    fill(T.DH[:, 0::2], BIG, [], ["DH0"], 64)
+    fill(T.DH[:, 1::2], -1024.0, [], ["DH1"], 64)
     QZ, QA = ["QZ%d" % k for k in range(8)], ["QR%d" % k for k in range(32)]
     for k in range(8):
-        if k % QS[0]:
+        if k % 2:
             CP(T.QZ[:, k::8], T.Q[:, :], ["Q"], [QZ[k]], 128)
         else:
             S(T.QZ[:, k::8], T.Q[:, :], FN.Copy, ["Q"], [QZ[k]], 256)
     for b in (0, 1):
         for k in range(16):
             o, i = T.QR[:, b * 2048 + k:b * 2048 + 2048:16], T.Q[:, b::2]
-            if k % QS[1]:
+            if k % 3:
                 CP(o, i, ["Q"], [QA[b * 16 + k]], 64)
             else:
                 S(o, i, FN.Copy, ["Q"], [QA[b * 16 + k]], 128)
-    if max(ND):
-        S(T.NQ[:, :], T.QR[:, 2048:2048 + NQW], FN.Copy, QA[16:], ["NQ"], NQW, scale=-1.0)
     for h, bn in ((0, "wB"), (1, "kB")):
         for z in range(4):
             x = PMV + (h * 4 + z) * 16
             MM(PS[bn][0:16, z * 128:z * 128 + 128], CH[:, x:x + 16], I16, True, True, ["hPV", "hI"], ["#" + bn], 16, 128)
-        CP(T.VH[:, h * 512:h * 512 + 512], PS[bn][0:16, :], ["#" + bn], ["VH%d" % h], 512)
+        S(T.VH[:, h * 512:h * 512 + 512], PS[bn][0:16, :], FN.Copy, ["#" + bn], ["VH%d" % h], 512)
 
-    PR1, PR2, PTZ, PAB, DM, NDM, I64 = 912, 1040, 1168, 1680, 1936, 2000, 2064
-    I2, I592, I4K, NI4K, IQ = 0, 128, 256, 384, 512
-    RLK, RTK, SLK = ["RL%d" % z for z in range(9)], ["RT%d" % z for z in range(7)], ["SELL%d" % z for z in range(4)]
+    PR1, PR2, PTZ, PAB, I64 = 912, 1040, 1168, 1680, 2064
+    I2, I592, I4K, NI4K = 0, 128, 256, 384
+    RTK, SLK = ["RT%d" % z for z in range(7)], ["SELL%d" % z for z in range(4)]
 
     def ring_constants():
         fill(T.ON[:, 256:512], 1.0, ["ON"], ["ONb"], 128)
-        fill(T.C9[:, :], 1024.0, [], ["C9b"], 256)
+        S(T.C9[:, :], T.ON[:, :], FN.Copy, ["ONb"], ["C9b"], 512, scale=1024.0)
         fill(T.TO[:, 2048:2064], 0.0, [], ["TOz"], 64)
         fill(T.TO1[:, 2048:2064], 0.0, [], ["TO1z"], 64)
-        iota(T.IO[:, 0:64], [[1, 64]], 0, 0, [], ["IO"], 64)
-        TS(T.IH[:, :], T.IO[:, 0:64], 200.0, OP.mult, ["IO"], ["IH"], 64)
+        iota(T.IO[:, :], [[127, 2], [1, 64]], 1, 0, [], ["IO"], 128)
         eqs(CB, PR1, [[-1, 8], [-16, 8], [-8, 2]], 0, "cR1", 80)
         eqs(CB, PR2, [[-1, 8], [-16, 8], [-8, 2]], 80, "cR2", 80)
         for z in range(4):
             eqs(CB, PTZ + z * 128, [[-1, 8], [1000, 4], [-8, 4]], -48 - 1000 * z, "cZ%d" % z, 80)
         eqs(CB, PAB, [[-8, 2], [-1, 8], [-16, 16]], 0, "cAB", 96)
-        fill(CB[:, I64:I64 + 1], 0.0, [], ["c64z"], 64)
-        TTo(CB[:, I64 + 1:I64 + 65], CB[:, 8:72], CB[:, 72:136], OP.add, ["cI"], ["c64"], 128)
-        TTo(CB[:, DM:DM + 64], CB[:, I64 + 1:I64 + 65], CB[:, I64:I64 + 64], OP.subtract, ["c64", "c64z"], ["cDM"], 128)
-        TS(CB[:, NDM:NDM + 64], CB[:, DM:DM + 64], -1.0, OP.mult, ["cDM"], ["cND"], 64)
-        for b in (0, 1):
-            GC(lambda b=b: g.iota(T.XI[:, 16 + b * 80:96 + b * 80], [[0, 5], [1000, 2], [-16, 8]], -1000 * b, 1), [], ["XI%d" % b], 80)
-        TS(T.XJ[:, 16:176], T.XI[:, 16:176], 4, OP.arith_shift_right, ["XI0", "XI1"], ["XJb"], 160)
-        TS(T.RC[:, :], T.XJ[:, 16:176], 0.0, OP.is_equal, ["XJb"], ["RC"], 160, -4096.0, OP.mult)
-        for b in (0, 1):
-            for z, m in enumerate((2, 2, 1)):
-                eqs(T.RT, b * 1280 + z * 512, [[-16, m], [-1, 8], [0, 32]], -8 * b - 32 * z, RTK[b * 3 + z], 96)
-        for z in range(5):
-            iota(T.RT[96:97, z * 512:z * 512 + 512], [[0, 16], [64, 2], [-128, 16]], -128, 0, [RTK[6]], [RTK[6]], 512)
+        DF = T.DF
+        fill(CB[:, I64:I64 + 66:65], 0.0, [], ["c64z"], 64)
+        TTo(CB[:, I64 + 1:I64 + 65], CB[:, 8:72], CB[:, 72:136], OP.subtract, ["cI"], ["c64"], 128)
+        TTo(DF[:, 0:64], CB[:, I64 + 2:I64 + 66], CB[:, I64:I64 + 64], OP.add, ["c64", "c64z"], ["cDM"], 128)
+        S(DF[:, 64:128], CB[:, I64 + 1:I64 + 65], FN.Copy, ["c64"], ["cND"], 64, scale=-2.0)
+        TTo(DF[:, 0:64], DF[:, 0:64], DF[:, 64:128], OP.add, ["cDM", "cND"], ["cDM"], 128)
+        TS(DF[:, 128:129], CB[:, 72:73], -127.0 / 128, OP.mult, ["cI"], ["cD0"], 64, CB[:, 8:9], OP.add)
+        TS(DF[:, 129:130], CB[:, 71:72], 65.0 / 64, OP.mult, ["cI"], ["cD1"], 64, CB[:, 135:136], OP.subtract)
+        TTo(DF[:, 0:64:63], DF[:, 0:64:63], DF[:, 128:130], OP.add, ["cDM", "cD0", "cD1"], ["cDM"], 64)
+        S(DF[:, 64:128], DF[:, 0:64], FN.Copy, ["cDM"], ["cND"], 64, scale=-1.0)
+        for z in range(6):
+            eqs(T.RT, z * 480, [[-1, 3 if z < 5 else 1], [0, 32], [-16, 5]], -3 * z, RTK[z], 96, "ON")
+        for z in range(16):
+            iota(T.RT[96:97, z * 160:z * 160 + 160], [[64, 2], [-128, 16], [0, 5]], -128, 0, [RTK[6]], [RTK[6]], 160)
         for z in range(4):
             eqs(T.SELL, z * 512, [[-8, 4], [-1, 8], [0, 16]], -32 * z, SLK[z], 128, "C9")
         iota(T.IX[0:1, 0:400], [[0, 16], [8, 5], [1, 5]], 9, 0, [], ["IX"], 400)
         fill(T.IX[0:1, 0:400:25], 64.0, ["IX"], ["IX"], 64)
-        fill(T.IX[0:1, 400:528], 34816.0, [], ["IXc"], 64)
-        fill(T.IX[0:1, 544:800], 0.0, [], ["IXz"], 128)
         fill(T.JD[:, :], 0.0, [], ["JD"], 200)
         fill(T.JD[:, 0::25], 64.0, ["JD"], ["JD"], 64)
         for x, f in ((I2, 2.0), (I592, 592.0), (I4K, 4096.0), (NI4K, -4096.0)):
-            TS(T.SI[:, x:x + 128], I16, f, OP.mult, ["hI"], ["SI%d" % x], 64)
-        CP(T.THF[:, :], T.TH[:, :], ["TH"], ["THF"], 64)
-        fill(T.TM[:, :], 0.0, [], ["TMz"], 128)
-        fill(T.TM[96:97, :], 1.0, ["TMz"], ["TMz"], 128)
-        fill(T.C3[:, :], 0.0, [], ["C3%d%d" % (b, h) for b in (0, 1) for h in (0, 1)], 264)
+            S(T.SI[:, x:x + 128], I16, FN.Copy, ["hI"], ["SI%d" % x], 128, scale=f)
+        TS(T.THF[:, :], T.TH[:, :], -200.0, OP.mult, ["TH"], ["THF"], 64, 100.0, OP.add)
+        fill(T.HT[64:96, :], 0.0, [], ["HTz"], 128)
+        fill(T.HT[96:97, :], 1.0, ["HTz"], ["HTz"], 128)
+        S(T.C3[:, 0:264], T.ON[:, 0:264], FN.Copy, ["ONb"], ["C30", "C31"], 264, scale=0.0)
         fill(CC[:, 4:5], -100.0, [], ["c100"], 64)
-        fill(CC[:, 5:6], 100.0, [], ["c101"], 64)
         fill(CC[:, 6:7], 0.5, [], ["c05"], 64)
+        iota(CC[:, 16:32], [[0, 8], [127, 2]], 1, 0, [], ["cP"], 16)
+        S(T.NE[:, :], CF[0:16, 128:384], FN.Copy, ["cEB"], ["NE"], 256, scale=-1.0)
         GC(lambda: g.iota(T.JI[:, 48:56], [[0, 8]], 0, 1), [], ["cm"], 8)
         TS(T.JI[:, 56:64], T.JI[:, 48:56], 15, OP.bitwise_and, ["cm"], ["cm2"], 64)
-        for j in range(6):
-            TS(CC[:, 8 + j:9 + j], T.JI[:, 56:57], float(j) if j < 5 else 0.5, OP.add, ["cm2"], ["cM%d" % j], 64)
+        TS(CC[:, 8:9], T.JI[:, 56:57], -200.0, OP.mult, ["cm2"], ["cM0"], 64, 100.0, OP.add)
+        for j in range(1, 5):
+            S(CC[:, 8 + j:9 + j], CC[:, 8:9], FN.Copy, ["cM0"], ["cM%d" % j], 64, bias=-200.0 * j)
+        S(CC[:, 13:14], CC[:, 8:9], FN.Copy, ["cM0"], ["cM5"], 64, bias=-900.0, scale=8.0)
 
     n = len(T.cores)
     r = T.rank_of(core)
@@ -325,7 +316,7 @@ def build(g, core, T, topo):
                 remote(g, T, topo, core, dst, T[land][:, c0:c1], T[buf][:, c0:c1], asem, "lo%d" % k)
             else:
                 remote(g, T, topo, core, rel, T[land][:, c0:c1], T[buf][:, c0:c1], "ri%d" % k, "lo%d" % k)
-        op("g", fn, [buf] + list(after), ["sent%d" % k], 0.5 if k else 2.5, "r", "lo%d" % k, len(topo.engines(core, dst if rel is None else rel)))
+        op("g", fn, [buf + str(c0) if k < 4 else buf] + list(after), ["sent%d" % k], 0.5 if k else 2.5, "r", "lo%d" % k, len(topo.engines(core, dst if rel is None else rel)))
 
     def arrive(land, asem, giver, lat, after):
         tot = 0
@@ -361,7 +352,7 @@ def build(g, core, T, topo):
         VG(lambda e: e.tensor_copy(T.NZ[:, :], NB.indirect(T.SU[:, t * 16:t * 16 + 16])), ["NB", "SU"], ["NZ"], 256)
         for c, bn in enumerate(banks):
             C, X = str(c), PS[bn]
-            bon[0] = PLAN["lead"] * (1 - c)
+            bon[0] = 1.0 - c
             for b in (0, 1):
                 x = 400 + (2 * c + b) * 128
                 MM(X[:, 0:128], CH[:, x:x + 128], T.NZ[:, b::2], b == 0, b == 1, ["hP4%d%d" % (c, b), "NZ"], ["#" + bn], 128, 128)
@@ -378,12 +369,12 @@ def build(g, core, T, topo):
     def step(t, c, a, tab, tkey):
         C = str(c)
         P = "PT%d" % t
-        bon[0] = PLAN["lead"] * (1 - c)
+        bon[0] = 1.0 - c
         kb, wb, xb, db = ("kA", "wA", "xA", "dA") if c == 0 else ("kB", "wB", "xB", "dB")
         K, W, X, D = PS[kb], PS[wb], PS[xb], PS[db]
         KB, WB, XB, DB = "#" + kb, "#" + wb, "#" + xb, "#" + db
         nn, nnk = T["NN" + C], "NN" + C
-        nv = NV[t * 5 + a]
+        nv = NV[a]
         tot, qr, QK = (2048, T.QZ, QZ) if a == 0 else (4096, T.QR, QA)
 
         def sl(i):
@@ -406,28 +397,25 @@ def build(g, core, T, topo):
         of, o0, ofk = (T.OZ, c * 128, "OZ" + C) if a == 0 else (T["OF" + C], 0, "OF" + C)
         win = tab[:, 0:2048]
         dv, ab, xg = T["DV" + C], T["AB" + C], T["XG" + C]
-
-        def cut(p0, p1, w, e):
-            return [(z, min(p1, z + w), e) for z in range(p0, p1, w)]
-        nd = nv + ND[t * 5 + a]
-        parts = cut(nd, tot, 512, "s") + cut(0, nv, CHUNK[1], "v") + cut(nv, nd, 1024, "d")
+        parts = [(z, min(p1, z + 512), e) for p0, p1, e in ((nv, tot, "s"), (0, nv, "v")) for z in range(p0, p1, 512)]
 
         def keys(nm, p0, p1):
             return ["%s%s.%d" % (nm, C, z) for z in range(p0 // 128, (p1 + 127) // 128)]
-        for p0, p1, e in cut(nv, nd, 1024, "d") + cut(nd, tot, CHUNK[2], "s") + cut(0, nv, CHUNK[0], "v"):
+        for p0, p1, e in parts:
             off = of[:, o0 + p0 // 16:o0 + p1 // 16]
             if e == "v":
                 VG(lambda en, p0=p0, p1=p1, off=off: en.tensor_tensor(dv[:, p0:p1], win.indirect(off), qr[:, p0:p1], OP.subtract),
                    [ofk, tkey] + QK, keys("dv", p0, p1), p1 - p0)
             else:
                 SG(xg[:, p0 - nv:p1 - nv], win.indirect(off), [ofk, tkey], keys("XG", p0 - nv, p1 - nv), p1 - p0)
-            if e == "d":
-                kk = keys("XG", p0 - nv, p1 - nv)
-                op("g", lambda p0=p0, p1=p1: g.dma_start(xg[:, p0 - nv:p1 - nv], T.NQ[:, p0 - 2048:p1 - 2048], accum_op=OP.add),
-                   kk + ["NQ"], kk, PLAN["gd"], "d", "ad" + C, 16, PLAN["ad"])
         kw = tot // 16
-        MM(K[:, 0:kw], T.ON[0:33, 0:128], T.CR[:, 0:kw], True, False, ["ON", "CR"], [KB], 128, kw)
         BQ = T["BQ" + C]
+        if a == 1:
+            for b in (0, 1):
+                MM(K[:, 256 + b:512:2], CF[0:16, 128 + b * 128:256 + b * 128], NTs(t, 16), True, True, ["wE", "NT%d" % t], [KB], 128, 128)
+        if a:
+            TTo(BQ[:, 0:256], nn[:, :], K[:, 256:512], OP.is_equal, [nnk, KB], ["BQ%s0" % C], 256)
+        MM(K[:, 0:kw], T.ON[0:33, 0:128], T.CR[:, 0:kw], True, False, ["ON", "CR"], [KB], 128, kw)
         if a == 0:
             MM(K[:, 0:128], T["NP" + C][:, :], CH[:, PM0:PM0 + 128], False, False, ["NP" + C, "hP0"], [KB], 128, 128)
             MM(K[:, 0:128], T.BQZ[:, c * 128:c * 128 + 128], BIGP, False, False, ["BQZ" + C, "BIGP"], [KB], 128, 128)
@@ -437,8 +425,6 @@ def build(g, core, T, topo):
         for p0, p1, e in parts:
             if e == "v":
                 S(ab[:, p0:p1], dv[:, p0:p1], FN.Abs, keys("dv", p0, p1), keys("ab", p0, p1), p1 - p0)
-            elif e == "d":
-                S(ab[:, p0:p1], xg[:, p0 - nv:p1 - nv], FN.Abs, keys("XG", p0 - nv, p1 - nv), keys("ab", p0, p1), p1 - p0)
             else:
                 w = p1 - p0
                 MM(D[:, 0:w], IB, xg[:, p0 - nv:p1 - nv], True, False, ["cI"] + keys("XG", p0 - nv, p1 - nv), [DB], 128, w)
@@ -456,31 +442,28 @@ def build(g, core, T, topo):
         for j in range(a + 1 if a else 0):
             s = nt(t, c, j)
             x0, j0 = (j % 2) * 256, j * 256
-            for b in (0, 1):
-                MM(X[:, x0 + b:x0 + 256:2], CF[0:16, 128 + b * 128:256 + b * 128], NTs(s, 16), True, True, ["wE", "NT%d" % s], [XB], 128, 128)
             bk = "BQ%s%d" % (C, j)
-            TTo(BQ[:, j0:j0 + 256], nn[:, :], X[:, x0:x0 + 256], OP.is_equal, [nnk, XB], [bk], 256)
+            if j:
+                for b in (0, 1):
+                    MM(X[:, x0 + b:x0 + 256:2], CF[0:16, 128 + b * 128:256 + b * 128], NTs(s, 16), True, True, ["wE", "NT%d" % s], [XB], 128, 128)
+                TTo(BQ[:, j0:j0 + 256], nn[:, :], X[:, x0:x0 + 256], OP.is_equal, [nnk, XB], [bk], 256)
             for b in (0, 1):
                 MM(K[:, b * 128:b * 128 + 128], BQ[:, j0 + b:j0 + 256:2], BIGI, False, False, [bk, "BIGI"], [KB], 128, 128)
         score(1, True)
-        SC, KD, Kt, Rt, SHt = T["SC" + C], T["KD" + C], T["K" + C], T["R" + C], T["SH" + C]
+        SC, Kt, Lt, Rt = T["SC" + C], T["K" + C], T["L" + C], T["R" + C]
         dd, dk = (T.DZ, "DZ") if a == 0 else (T["D" + C], "D" + C)
         if a:
             TTo(dd[:, 0::16], T[P][:, sl(a) * 16:sl(a) * 16 + 16], T.RS[:, :], OP.add, [P + "s%d" % sl(a), "RS", dk], [dk], 64)
         V(lambda e: e.tensor_tensor_scan(SC[:, 0:kw], dd[:, 0:kw], K[:, 0:kw], -BIG, OP.max, OP.min), [dk, KB], ["SC" + C], kw)
-        CP(Kt[:, 0:kw // 8], SC[:, 7:kw:8], ["SC" + C], ["K" + C], 64)
         ns = sl(a + 1)
         out, ok = T[P][:, ns * 16:ns * 16 + 16], P + "s%d" % ns
         if a == 0:
-            TS(Rt[:, 0:16], Kt[:, 0:16], 1023, OP.bitwise_and, ["K" + C], ["R" + C], 64)
-            CP(out, Rt[:, 0:16], ["R" + C], [ok], 64)
+            TS(Rt[:, :], SC[:, 7:kw:8], 1023, OP.bitwise_and, ["SC" + C], ["R" + C], 64)
         else:
-            TS(SHt[:, :], Kt[:, :], 13, OP.arith_shift_right, ["K" + C], ["SH" + C], 64)
-            TS(Rt[:, :], Kt[:, :], 1023, OP.bitwise_and, ["K" + C], ["R" + C], 64)
-            TTo(KD[:, 0:16], SHt[:, 0::2], SHt[:, 1::2], OP.is_gt, ["SH" + C], ["SL" + C], 64)
-            TTo(KD[:, 16:32], Rt[:, 1::2], Rt[:, 0::2], OP.subtract, ["R" + C], ["DF" + C], 64)
-            TTo(KD[:, 32:48], KD[:, 16:32], KD[:, 0:16], OP.mult, ["DF" + C, "SL" + C], ["D2" + C], 64)
-            TTo(out, Rt[:, 0::2], KD[:, 32:48], OP.add, ["R" + C, "D2" + C], [ok], 64)
+            TS(Kt[:, :], SC[:, 7:kw:8], ~7168, OP.bitwise_and, ["SC" + C], ["K" + C], 64)
+            V(lambda e: e.tensor_tensor_scan(Lt[:, :], T.DH[:, :], Kt[:, :], 0.0, OP.add, OP.min), ["DH0", "DH1", "K" + C], ["L" + C], 64)
+            TS(Rt[:, :], Lt[:, 1::2], 1023, OP.bitwise_and, ["L" + C], ["R" + C], 64)
+        CP(out, Rt[:, :], ["R" + C], [ok], 64)
         if a < 4:
             s = nt(t, c, a + 1)
             MM(X[0:16, 0:128], out, I16, True, True, [ok, "hI"], [XB], 16, 128)
@@ -492,36 +475,31 @@ def build(g, core, T, topo):
         bon[0] = 0.0
 
     def lesser(el, tab, tk):
-        for h in (0, 1):
-            y = h * 1024
-            TS(T[el][:, y:y + 1024], tab[:, y:y + 1024], 0.75, OP.mult, [tk], ["%s.%d" % (el, h)], 512, 1024.375, OP.add)
+        for h in range(4):
+            y = h * 512
+            TS(T[el][:, y:y + 512], tab[:, y:y + 512], 0.75, OP.mult, [tk], ["%s.%d" % (el, h)], 256, 1024.375, OP.add)
 
     def lessen(tab, tk, mk, el, out, okey, banks):
         for qd in range(4):
             b = banks[qd % len(banks)]
-            B, ek, x = PS[b], "%s.%d" % (el, qd // 2), qd * 512
+            B, ek, x = PS[b], "%s.%d" % (el, qd), qd * 512
             MM(B[:, :], IB, T[el][:, x:x + 512], True, False, ["cI", ek], ["#" + b], 128, 512)
             for z in range(4):
                 tt = (qd * 4 + z) * 128
                 MM(B[:, z * 128:z * 128 + 128], T.SELL[:, tt:tt + 128], T[mk][:, :], False, z == 3, [SLK[qd], mk], ["#" + b], 128, 128)
             TTo(out[:, x:x + 512], B[:, :], tab[:, x:x + 512], OP.min, ["#" + b, tk], ["%s%d" % (okey, qd)], 512)
 
-    def thermo(out, bn, w, key, onv, low):
-        if onv:
-            TS(out, PS[bn][:, 0:w], 0.5 if low else -0.5, OP.is_le, ["#" + bn], [key], w)
-        else:
-            S(out, PS[bn][:, 0:w], FN.Sigmoid, ["#" + bn, "c100", "c101"], [key], w, bias=CC[:, 5:6] if low else CC[:, 4:5], scale=-200.0)
-
     def hot(m0, m1, hk):
         c0, c1, kz = m0 * 16, m1 * 16, str(m0)
-        TS(T.WW[:, c0:c1], T.HH[:, c0:c1], 63, OP.bitwise_and, hk, ["WW" + kz], c1 - c0)
-        TS(T.WS[:, c0:c1], T.WW[:, c0:c1], -200.0, OP.mult, ["WW" + kz], ["WS" + kz], c1 - c0, 100.0, OP.add)
-        for col in range(c0, c1):
-            o, w = T.OH[:, col * 64:col * 64 + 64], T.WS[:, col:col + 1]
-            if col // 16 in SHOT:
-                S(o, T.IO[:, 0:64], FN.Sigmoid, ["IO", "WS" + kz], ["OH%d" % col], 64, bias=w, scale=200.0)
-            else:
-                TS(o, T.IH[:, :], w, OP.add, ["IH", "WS" + kz], ["OH%d" % col], 64, 0.0, OP.is_ge)
+        TS(T.WX[:, c0:c1], T.HH[:, c0:c1], 63, OP.bitwise_and, hk, ["WW" + kz], c1 - c0)
+        if c1 - c0 > 16:
+            TS(T.WS[:, c0:c1:2], T.WX[:, c0:c1:2], 1.0, OP.add, ["WW" + kz], ["WS" + kz], (c1 - c0) // 2)
+            TS(T.WS[:, c0 + 1:c1:2], T.WX[:, c0 + 1:c1:2], 128.0, OP.add, ["WW" + kz], ["WT" + kz], (c1 - c0) // 2)
+        else:
+            TTo(T.WS[:, c0:c1], T.WX[:, c0:c1], CC[:, 16:32], OP.add, ["WW" + kz, "cP"], ["WS" + kz, "WT" + kz], 64)
+        for col in range(c0, c1, 2):
+            TS(T.OH[:, col * 64:col * 64 + 128], T.IO[:, :], T.WS[:, col:col + 1], OP.max, ["IO", "WS" + kz, "WT" + kz],
+               ["OH%d" % col, "OH%d" % (col + 1)], 64, T.WS[:, col + 1:col + 2], OP.min)
 
     def rings(t, tab, tk):
         P = "PT%d" % t
@@ -535,15 +513,16 @@ def build(g, core, T, topo):
             TS(T.U[:, c0:c1], pt[:, c0:c1], 2.0, OP.mult, kk, [uk[z]], c1 - c0, 1.0, OP.add)
         for z, (c0, c1, kk, ku) in enumerate(((16, 128, pk[1:10], uk[0:1]), (0, 16, pk[0:3], uk[0:2]), (128, 144, pk[8:11], [uk[0], uk[2]]))):
             TTo(T.PR[:, c0:c1], T.U[:, c0:c1], T.U[:, c0 + 32:c1 + 32], OP.mult, ku, ["PR%d" % z], 2 * (c1 - c0))
-            TS(T.V5[:, c0:c1], pt[:, c0 + 16:c1 + 16], 592.0, OP.mult, kk[1:2] if z else kk, ["V5%d" % z], c1 - c0)
-            TTo(T.TT[:, c0:c1], T.PR[:, c0:c1], T.V5[:, c0:c1], OP.add, ["PR%d" % z, "V5%d" % z], ["TT%d" % z], 2 * (c1 - c0))
+            if z == 0:
+                S(T.V5[:, :], T.U[:, 16:160], FN.Copy, uk[0:1], ["V5"], 144, bias=-296.0, scale=296.0)
+            TTo(T.TT[:, c0:c1], T.PR[:, c0:c1], T.V5[:, c0:c1], OP.add, ["PR%d" % z, "V5"], ["TT%d" % z], 2 * (c1 - c0))
             TS(T.HH[:, c0:c1], T.TT[:, c0:c1], 4, OP.arith_shift_right, ["TT%d" % z], [hw[z]], c1 - c0, 2047, OP.bitwise_and)
-        TS(T.PX[:, 16:160], pt[:, 16:160], 1.0 / 2048, OP.mult, pk[1:10], ["PXa"], 144)
-        TS(T.PX[:, 160:176], slot(10), 1.0 / 2048, OP.mult, pk[10:11], ["PXb"], 64)
+        S(T.PX[:, 16:160], T.U[:, 16:160], FN.Copy, uk[0:1], ["PXa"], 144, scale=1.0 / 4096)
+        S(T.PX[:, 160:176], T.U[:, 160:176], FN.Copy, uk[2:3], ["PXb"], 64, scale=1.0 / 4096)
         TTo(T.DX[:, 16:80], T.PX[:, 32:96], T.PX[:, 16:80], OP.subtract, ["PXa"], ["DXa"], 128)
         TTo(T.DX[:, 80:144], T.PX[:, 80:144], T.PX[:, 96:160], OP.subtract, ["PXa"], ["DXb"], 128)
         TTo(T.DX[:, 144:160], T.PX[:, 144:160], T.PX[:, 160:176], OP.subtract, ["PXa", "PXb"], ["DXc"], 64)
-        hot(1, 8, ["HHe"])
+        hot(1, 8, hw[0:1])
         hot(8, 9, hw[2:3])
         hot(0, 1, hw[1:2])
         J = PS["wA"]
@@ -587,17 +566,17 @@ def build(g, core, T, topo):
         TTo(T.HV[:, 144:160], T.HH[:, 144:160], NM[:, 64:80], OP.max, ["HHb", "NM4"], ["HVc"], 64)
         X, X2 = PS["xA"], PS["xB"]
         MM(X[0:80, 0:128], T.HV[:, 0:80], I16, True, True, ["HVa", "hI"], ["#xA"], 80, 128)
-        CP(T.HT[:, 0:128], X[0:80, 0:128], ["#xA"], ["HT0"], 128)
+        CP(T.HT[0:80, 0:128], X[0:80, 0:128], ["#xA", "HTz"], ["HT0"], 128)
         MM(X[0:80, 128:256], T.HV[:, 80:160], I16, True, True, ["HVb", "HVc", "hI"], ["#xA"], 80, 128)
-        CP(T.HT[:, 128:256], X[0:80, 128:256], ["#xA"], ["HT1"], 128)
-        MM(X2[:, 0:128], CH[0:80, PR1:PR1 + 128], T.HT[:, 0:128], True, False, ["cR1", "HT0"], ["#xB"], 128, 128)
-        MM(X2[:, 0:128], CH[0:80, PR2:PR2 + 128], T.HT[:, 128:256], False, True, ["cR2", "HT1"], ["#xB"], 128, 128)
+        CP(T.HT[0:80, 128:256], X[0:80, 128:256], ["#xA", "HTz"], ["HT1"], 128)
+        MM(X2[:, 0:128], CH[0:80, PR1:PR1 + 128], T.HT[0:80, 0:128], True, False, ["cR1", "HT0"], ["#xB"], 128, 128)
+        MM(X2[:, 0:128], CH[0:80, PR2:PR2 + 128], T.HT[0:80, 128:256], False, True, ["cR2", "HT1"], ["#xB"], 128, 128)
         for z in range(4):
-            MM(X2[:, 128:160], CH[0:80, PTZ + z * 128:PTZ + z * 128 + 128], T.HT[:, 128 + z:256:4], z == 0, z == 3, ["cZ%d" % z, "HT1"], ["#xB"], 128, 32)
+            MM(X2[:, 128:160], CH[0:80, PTZ + z * 128:PTZ + z * 128 + 128], T.HT[0:80, 128 + z:256:4], z == 0, z == 3, ["cZ%d" % z, "HT1"], ["#xB"], 128, 32)
         CP(T.OFR[:, :], X2[:, 0:160], ["#xB"], ["OFR"], 160)
         win = tab[:, 0:2064]
         for h in (0, 1):
-            for e, x0, ln in (("v", h * 1024, XV[0]), ("s", h * 1024 + XV[0], 1024 - XV[0]), ("s", 2048 + h * 256, 256)):
+            for e, x0, ln in (("v", h * 1024, XV), ("s", h * 1024 + XV, 1024 - XV), ("s", 2048 + h * 256, 256)):
                 xo, fo = T.XR[:, x0:x0 + ln], T.OFR[:, x0 // 16:(x0 + ln) // 16]
                 if e == "s":
                     SG(xo, win.indirect(fo), ["OFR", tk, tk + "z"], ["XR%d" % x0], ln)
@@ -605,43 +584,42 @@ def build(g, core, T, topo):
                     VG(lambda e, xo=xo, fo=fo: e.tensor_copy(xo, win.indirect(fo)), ["OFR", tk, tk + "z"], ["XR%d" % x0], ln)
         hot(9, 10, ["HHb"])
         B, W = PS["kB"], PS["wB"]
-        MM(W[0:80, 0:128], T.ON[0:1, 0:80], T.IX[0:1, 400:528], True, False, ["ON", "IXc"], ["#wB"], 80, 128)
+        for z, u in enumerate((0, 1, 8, 9, 2, 3, 10, 11, 4, 5, 12, 13, 6, 7, 14, 15)):
+            bn, tl = ("wA", "kA")[z % 2], T.TL[:, u * 320:u * 320 + 320]
+            for h in (0, 1):
+                MM(PS[bn][:, h:320:2], T.HT[:, h * 128:h * 128 + 128], T.RT[:, u * 160:u * 160 + 160], True, True,
+                   ["HT%d" % h, "HTz", RTK[u // 3], RTK[6]], ["#" + bn], 128, 160)
+            if u in HIV:
+                TS(tl, PS[bn][:, 0:320], -0.5, OP.is_le, ["#" + bn], ["TL%d" % u], 320)
+            else:
+                S(tl, PS[bn][:, 0:320], FN.Sigmoid, ["#" + bn, "c100"], ["TL%d" % u], 320, bias=CC[:, 4:5], scale=-200.0)
         for h in (0, 1):
             for b in (0, 1):
                 for m in range(10):
                     x0 = h * 1024 if m < 8 else 2048 + h * 256
                     xs = T.XR[:, x0 + 2 * m + b:x0 + 1024:16] if m < 8 else T.XR[:, x0 + 2 * m - 16 + b:x0 + 256:4]
                     y = b * 128 + h * 64
-                    MM(B[:, y:y + 64], IB, xs, m == 0, m == 9, ["cI", "XR%d" % x0] + (["XR%d" % (x0 + XV[0])] if m < 8 else []), ["#kB"], 128, 64)
-        TS(T.CMP[:, :], B[:, 0:256], T.THF[:, 0:1], OP.is_ge, ["#kB", "THF"], ["CMP"], 256)
+                    MM(B[:, y:y + 64], IB, xs, m == 0, m == 9, ["cI", "XR%d" % x0] + (["XR%d" % (x0 + XV)] if m < 8 else []), ["#kB"], 128, 64)
+        S(T.CMP[:, :], B[:, 0:256], FN.Sigmoid, ["#kB", "THF"], ["CMP"], 256, bias=T.THF[:, 0:1], scale=200.0)
         for b in (0, 1):
-            MM(W[0:80, 0:128], T.RC[:, b * 80:b * 80 + 80], T.CMP[:, b * 128:b * 128 + 128], False, b == 1, ["CMP", "RC"], ["#wB"], 80, 128)
-        for h in (0, 1):
-            TTo(T.TM[0:80, h * 128:h * 128 + 128], T.HT[:, h * 128:h * 128 + 128], W[0:80, 0:128], OP.max, ["HT%d" % h, "#wB", "TMz"], ["TM%d" % h], 128)
-        z = 0
-        for b, cn in ((0, "xB"), (1, "kB")):
-            C = PS[cn]
-            MM(C[:, 0:256], T.ON[0:1, 0:128], T.IX[0:1, 544:800], True, False, ["ON", "IXz"], ["#" + cn], 128, 256)
-            for h in (0, 1):
-                for y, ms in enumerate(((0, 1), (2, 3), (4,))):
-                    bn, w = ("xA", "wA", "kA")[z % 3], 256 * len(ms)
-                    x = (b * 2 + h) * 1280 + y * 512
-                    MM(PS[bn][:, 0:w], T.TM[:, h * 128:h * 128 + 128], T.RT[:, b * 1280 + y * 512:b * 1280 + y * 512 + w], True, True,
-                       ["TM%d" % h, "TMz", RTK[b * 3 + y], RTK[6]], ["#" + bn], 128, w)
-                    thermo(T.TL[:, x:x + w], bn, w, "TL%d" % z, HIV[0] and z % HIV[0] == HIV[0] - 1, False)
-                    for m in ms:
-                        for gp in range(4):
-                            col, l0 = (h * 5 + m) * 16 + b * 8, (b * 2 + h) * 1280 + m * 256 + gp * 64
-                            MM(C[:, gp:256:4], T.OH[:, (col + 2 * gp) * 64:(col + 2 * gp) * 64 + 128], T.TL[:, l0:l0 + 64], False,
-                               h == 1 and m == 4 and gp == 3, ["OH%d" % (col + 2 * gp), "OH%d" % (col + 2 * gp + 1), "TL%d" % z], ["#" + cn], 128, 64)
-                    z += 1
-            for h in (0, 1):
-                CP(T.C3[h * 64:h * 64 + 64, b * 264 + 8 + h:b * 264 + 264:2], C[h * 64:h * 64 + 64, h * 128:h * 128 + 128], ["#" + cn], ["C3%d%d" % (b, h)], 128)
-        for x, p0, p1 in ((64, 8, 136), (0, 136, 0)):
+            MM(W[:, b * 8:b * 8 + 8], T.CMP[:, b * 128:b * 128 + 128], T.S8[:, :], True, True, ["CMP", "S8"], ["#wB"], 128, 8)
+        TS(T.HY[:, 0:16], W[:, 0:16], 8.5 * 8192, OP.is_ge, ["#wB"], ["HY"], 64)
+        cn = "xB"
+        C = PS[cn]
+        for gp in range(4):
             for b in (0, 1):
-                y, ck = b * 264, ["C3%d0" % b, "C3%d1" % b]
-                MM(W[:, x:x + 64], T.C3[:, y + p0:y + p0 + 128], CB[:, DM:DM + 64], b == 0, False, ck + ["cDM"], ["#wB"], 128, 64)
-                MM(W[:, x:x + 64], T.C3[:, y + p1:y + p1 + 128], CB[:, NDM:NDM + 64], False, b == 1, ck + ["cND"], ["#wB"], 128, 64)
+                for u in (b * 8 + 2 * gp, b * 8 + 2 * gp + 1):
+                    tl = T.TL[:, u * 320:u * 320 + 320]
+                    TS(tl, tl, T.HY[:, u:u + 1], OP.mult, ["TL%d" % u, "HY"], ["TL%d" % u], 160)
+                for m in range(10):
+                    col, l0 = m * 16 + b * 8 + 2 * gp, (b * 8 + 2 * gp) * 320
+                    MM(C[:, gp:256:4], T.OH[:, col * 64:col * 64 + 128], T.TL[:, l0 + (m % 5) * 2 + m // 5:l0 + 640:10], m + b == 0, m + b == 10,
+                       ["OH%d" % col, "OH%d" % (col + 1), "TL%d" % (col % 16), "TL%d" % (col % 16 + 1)], ["#" + cn], 128, 64)
+        for h in (0, 1):
+            S(T.C3[h * 64:h * 64 + 64, 8 + h:264:2], C[h * 64:h * 64 + 64, h * 128:h * 128 + 128], FN.Copy, ["#" + cn], ["C3%d" % h], 128)
+        for x, p0, p1 in ((64, 8, 136), (0, 136, 0)):
+            MM(W[:, x:x + 64], T.C3[:, p0:p0 + 128], T.DF[:, 0:64], True, False, ["C30", "C31", "cDM"], ["#wB"], 128, 256)
+            MM(W[:, x:x + 64], T.C3[:, p1:p1 + 128], T.DF[:, 64:128], False, True, ["C30", "C31", "cND"], ["#wB"], 128, 256)
         S(T.MKT[:, :], W[:, 0:128], FN.Sign, ["#wB", "c05"], ["MKT"], 128, bias=CC[:, 6:7], scale=-1.0)
 
     def show(t, bn):
@@ -650,12 +628,10 @@ def build(g, core, T, topo):
         D = E = PS[bn]
         DB = "#" + bn
         J0, JJ = T.JI[:, 16:32], T.JI[:, 32:48]
-        TTo(JS[:, 32:48], J0, JJ, OP.subtract, ["J0", "JJ"], ["Y8"], 64)
-        TS(JS[:, 48:64], J0, 8.0, OP.is_ge, ["J0"], ["YF"], 64)
-        TS(JS[:, 64:80], JS[:, 32:48], 0.125, OP.mult, ["Y8"], ["YI"], 64)
-        TTo(T.IL[:, 0:16], JS[:, 64:80], JS[:, 48:64], OP.add, ["YI", "YF"], ["ILi"], 64)
-        TTo(JS[:, 80:96], JJ, JS[:, 48:64], OP.mult, ["JJ", "YF"], ["YJ"], 64)
-        TTo(T.IL[:, 16:32], JS[:, 64:80], JS[:, 80:96], OP.add, ["YI", "YJ"], ["ILl"], 64)
+        YI = T.JI[:, 64:80]
+        TS(YI, J0, 3, OP.arith_shift_right, ["J0"], ["YI"], 64)
+        CP(T.IL[:, 0:16], J0, ["J0"], ["ILi"], 64)
+        TTo(T.IL[:, 16:32], YI, JJ, OP.add, ["YI", "JJ"], ["ILl"], 64)
         MM(E[0:96, 0:128], pt[:, 80:176], I16, True, True, [P + "s%d" % i for i in range(5, 11)] + ["hI"], [DB], 96, 128)
         for z, k in ((0, "ILi"), (1, "ILl")):
             MM(D[0:16, 128 + z * 128:256 + z * 128], T.IL[:, z * 16:z * 16 + 16], I16, True, True, [k, "hI"], [DB], 16, 128)
@@ -665,28 +641,30 @@ def build(g, core, T, topo):
             eb = CF[0:16, 128 + b * 128:256 + b * 128]
             for z in (0, 1):
                 MM(D[:, z * 256 + b:z * 256 + 256:2], eb, T.LT[:, z * 128:z * 128 + 128], True, True, ["wE", "LT"], [DB], 128, 128)
-        R1, R2 = D[:, 0:256], D[:, 256:512]
-        TS(T.YM[:, :], R1, CC[:, 13:14], OP.is_ge, [DB, "cM5"], ["YM"], 256, 2048.0, OP.mult)
-        TTo(T.YP[:, :], T.YM[:, :], R2, OP.max, [DB, "YM"], ["YP"], 256)
-        TS(T.YB[:, 256:512], R2, CC[:, 13:14], OP.is_le, [DB, "cM5"], ["YB1"], 256, -1.0, OP.mult)
+        YK = [T.YK[:, j * 256:j * 256 + 256] for j in range(6)]
+        S(YK[0], D[:, 0:256], FN.Sigmoid, [DB, "cM5"], ["YK0"], 256, bias=CC[:, 13:14], scale=200.0)
+        S(YK[5], D[:, 256:512], FN.Sigmoid, [DB, "cM1"], ["YK5"], 256, bias=CC[:, 9:10], scale=200.0)
+        for b in (0, 1):
+            MM(D[:, b:256:2], CF[0:16, 128 + b * 128:256 + b * 128], T.LT[:, 128:256], True, False, ["wE", "LT"], [DB], 128, 128)
+            MM(D[:, b:256:2], T.SI[:, NI4K:NI4K + 128], T.YK[:, b:256:2], False, True, ["SI%d" % NI4K, "YK0"], [DB], 128, 128)
+        for j in range(1, 5):
+            S(YK[j], D[:, 0:256], FN.Sigmoid, [DB, "cM%d" % j], ["YK%d" % j], 256, bias=CC[:, 8 + j:9 + j], scale=200.0)
         for j0, js in ((0, (0, 1)), (2, (2, 3)), (4, (4,))):
             for j in js:
                 x, s = (j - j0) * 256, nt(t, 1, j)
                 for b in (0, 1):
                     if j:
-                        MM(E[:, x + b:x + 256:2], CF[0:16, 128 + b * 128:256 + b * 128], NTs(s, 16), True, True, ["wE", "NT%d" % s], [DB], 128, 128)
+                        MM(E[:, x + b:x + 256:2], CF[0:16, 128 + b * 128:256 + b * 128], NTs(s, 16), True, j == 1, ["wE", "NT%d" % s], [DB], 128, 128)
+                        if j > 1:
+                            MM(E[:, x + b:x + 256:2], T.NE[:, b * 128:b * 128 + 128], NTs(s - 1, 16), False, True, ["NE", "NT%d" % (s - 1)], [DB], 128, 128)
                     else:
                         MM(E[:, b:256:2], CH[0:96, PAB + b * 128:PAB + b * 128 + 128], T.AT[:, :], True, True, ["hAB", "AT"], [DB], 128, 128)
             for j in js:
-                x, k0 = (j - j0) * 256, (j % 2) * 256
-                if j:
-                    TS(T.YK[:, k0:k0 + 256], T.YP[:, :], CC[:, 8 + j:9 + j], OP.is_equal, ["YP", "cM%d" % j], ["YK%d" % (j % 2)], 128)
-                    TTo(T.YB[:, 256 + j * 256:512 + j * 256], T.YK[:, k0:k0 + 256], E[:, x:x + 256], OP.mult, ["YK%d" % (j % 2), DB], ["YB%d" % (j + 1)], 256)
-                else:
-                    TTo(T.YB[:, 0:256], T.YM[:, :], E[:, 0:256], OP.min, [DB, "YM"], ["YB0"], 256)
+                x = (j - j0) * 256
+                TTo(T.YB[:, j * 256:256 + j * 256], YK[j], E[:, x:x + 256], OP.mult, ["YK%d" % j, DB], ["YB%d" % j], 256)
         for z in range(6):
-            MM(D[:, 0:256], I16, T.YB[:, z * 256:z * 256 + 256], z == 0, z == 5, ["hI", "YB%d" % z], [DB], 128, 256)
-        S(T.YR[:, :], D[:, 0:256], FN.Copy, [DB], ["YR"], 256)
+            MM(D[:, 0:256], I16, T.YB[:, z * 256:z * 256 + 256] if z < 5 else YK[5], z == 0, z == 5, ["hI", "YB%d" % z if z < 5 else "YK5"], [DB], 128, 256)
+        S(T.YR[:, :], D[:, 0:256], FN.Copy, [DB], ["YR"], 256, bias=-1.0)
         DMA("y", T.yr[:, t * 256:t * 256 + 256], T.YR[:, :], ["YR"], [])
 
     start(0, ("dA", "dB"))
@@ -704,20 +682,19 @@ def build(g, core, T, topo):
     lesser("ELn", T.TPn, "TPn")
     rings(0, T.TO, "TO")
     send(6)
+    show(0, "kB")
     arrive("MKP", "aMK", (r + 2) % n, PLAN["mk"], ["sent6"])
-    lessen(T.TO, "TO", "MKT", own, T.TO1, "T1q", ("dA", "dB", "xA", "wA"))
+    lessen(T.TO, "TO", "MKT", own, T.TO1, "T1q", ("dB", "dA", "xA", "wA"))
     op(None, None, ["T1q%d" % q for q in range(4)], ["TO1"], 0.0, "n")
-    lessen(T.TPn, "TPn", "MKP", "ELn", T.TP1, "P1q", ("wB", "xB"))
+    lessen(T.TPn, "TPn", "MKP", "ELn", T.TP1, "P1q", ("wB", "xB", "dB"))
     op(None, None, ["P1q%d" % q for q in range(4)], ["TP1"], 0.0, "n")
     for a in range(5):
         step(1, 0, a, T.TO1, "TO1")
         step(1, 1, a, T.TP1, "TP1")
-        if a == 0:
-            show(0, "wA")
     lesser(own, T.TO1, "TO1")
     rings(1, T.TO1, "TO1")
-    show(1, "dB")
-    lessen(T.TO1, "TO1", "MKT", own, T.TO2, "T2q", ("dA", "xA", "wA", "kA"))
+    show(1, "kB")
+    lessen(T.TO1, "TO1", "MKT", own, T.TO2, "T2q", ("dB", "dA", "xA", "wA"))
     for qd in range(4):
         DMA("y" if qd % 2 == 0 else "s", T.ye[:, qd * 512:qd * 512 + 512], T.TO2[:, qd * 512:qd * 512 + 512], ["T2q%d" % qd], [])
     for o in ops:
@@ -731,23 +708,21 @@ def build(g, core, T, topo):
     return ops
 
 
-def place(ops, pred, rank):
+def place(ops, pred, rank, way):
     n = len(ops)
-    succ, need = [[] for _ in range(n)], [len(p) for p in pred]
-    for i in range(n):
+    for i in way:
         for d, lag in pred[i]:
-            succ[d].append(i)
-    start, seq, busy = [0.0] * n, [0] * n, {}
-    ready = [(rank[i], i) for i in range(n) if need[i] == 0]
-    k = 0
-    while ready:
-        best = min(ready)
-        ready.remove(best)
-        i = best[1]
-        o = ops[i]
-        s = max([start[d] + lag for d, lag in pred[i]] + [0.0])
-        if o["q"] is not None:
-            b, c = busy.setdefault(o["q"], []), o["cost"]
+            if rank[d] >= rank[i]:
+                rank[i] = rank[d] + 1e-7
+    start, seq, busy = [0.0] * n, [0] * n, {q: [] for q in "vstgy"}
+    for k, i in enumerate(sorted(way, key=lambda i: rank[i])):
+        q, c = ops[i]
+        s = 0.0
+        for d, lag in pred[i]:
+            if start[d] + lag > s:
+                s = start[d] + lag
+        if q is not None:
+            b = busy[q]
             lo, hi = 0, len(b)
             while lo < hi:
                 m = (lo + hi) // 2
@@ -768,11 +743,6 @@ def place(ops, pred, rank):
             else:
                 b.insert(lo, [s, s + c])
         start[i], seq[i] = s, k
-        k += 1
-        for j in succ[i]:
-            need[j] -= 1
-            if need[j] == 0:
-                ready.append((rank[j], j))
     return start, seq
 
 
@@ -791,32 +761,45 @@ def schedule(ops):
     way = [0.0] * n
     for i in range(n - 1, -1, -1):
         way[i] = max([way[j] + lag - ops[j]["cost"] for j, lag in back[i]] + [ops[i]["lat"]]) + ops[i]["cost"]
-    def lasts(order, f):
-        fin, free = [0.0] * n, {}
-        for i in order:
-            o = ops[i]
-            q, s = o["q"], free.get(o["q"], 0.0) if o["q"] else 0.0
-            for d in o["deps"]:
-                s = max(s, fin[d] + (PLAN["wake"] if ops[d]["q"] != q else PLAN["same"]))
-            free[q] = s + o["cost"] * f.get(q, 1.0) * (f["gat"] if o["gat"] else 1.0)
-            fin[i] = free[q] + o["lat"]
-        return max(fin)
+    qc, up, down = [(o["q"], o["cost"]) for o in ops], list(range(n)), list(range(n - 1, -1, -1))
+    waits = [[(d, ops[d]["lat"] + (PLAN["wake"] if ops[d]["q"] != o["q"] else PLAN["same"])) for d in o["deps"]] for o in ops]
+    costs = [[o["lat"] * f["far"] if o["kind"] == "x" else o["cost"] * f.get(o["q"], 1.0) * (f["gat"] if o["gat"] else 1.0) for o in ops] for f in OTHERS]
 
-    def turn(start, shake):
-        rank = []
-        for i in range(n):
-            seed[0] = (seed[0] * 1103515245 + 12345) % 2147483648
-            rank.append(-(start[i] + full[i]) + shake * seed[0] / 2147483648.0)
-        rs, _ = place(ops, back, rank)
-        start, seq = place(ops, fwd, [-(rs[i] + ops[i]["cost"]) for i in range(n)])
+    def lasts(order, cost):
+        fin, free = [0.0] * n, {q: 0.0 for q in "vstgy"}
+        free[None] = 0.0
+        for i in order:
+            q = qc[i][0]
+            s = free[q]
+            for d, w in waits[i]:
+                if fin[d] + w > s:
+                    s = fin[d] + w
+            fin[i] = s + cost[i]
+            if q:
+                free[q] = fin[i]
+        return max(fin[i] + ops[i]["lat"] for i in order[-200:])
+
+    def rnd():
+        seed[0] = (seed[0] * 1103515245 + 12345) % 2147483648
+        return seed[0] / 2147483648.0
+
+    def turn(start, shake, z):
+        t0, w = rnd() * max(start), PLAN["wide"] * (0.3 + rnd())
+        e = [shake * rnd() if abs(start[i] - t0) < w else 0.0 for i in range(n)]
+        if z % 3 == 2:
+            rank = [start[i] + e[i] for i in range(n)]
+        else:
+            rs, _ = place(qc, back, [-(start[i] + full[i]) + e[i] * (1 - z % 3) for i in range(n)], down)
+            rank = [-(rs[i] + ops[i]["cost"]) + e[i] * (z % 3) for i in range(n)]
+        start, seq = place(qc, fwd, rank, up)
         order = sorted(range(n), key=lambda i: (start[i], seq[i]))
-        end = sum(lasts(order, f) for f in OTHERS) / len(OTHERS)
+        end = sum(lasts(order, f) for f in costs) / len(costs)
         ORDERS.setdefault("ends", []).append(end)
         return end, start, seq
     seed = [1]
-    best = min(turn(place(ops, fwd, [-way[i] - lead * ops[i]["bon"] for i in range(n)])[0], 0.0) for lead in LEADS)
+    best = min(turn(place(qc, fwd, [-way[i] - lead * ops[i]["bon"] for i in range(n)], up)[0], 0.0, 0) for lead in LEADS)
     for z in range(PLAN["turns"]):
-        best = min(best, turn(best[1], PLAN["shake"]))
+        best = min(best, turn(best[1], PLAN["shake"] * (0.5, 1.0, 2.0, 4.0)[z % 4], z))
     return sorted(range(n), key=lambda i: (best[1][i], best[2][i]))
 
 

from concourse.mybir import dt, AluOpType, AxisListType, ActivationFunctionType
import comms_topo

OP = AluOpType
FN = ActivationFunctionType
BIG = float(2 ** 26)
REST = 2041 * 8192
F32, B16, H16, I32, U16 = "float32", "bfloat16", "float16", "int32", "uint16"
NV = [1024, 2304, 2432, 2304, 2432]
HIV = [7, 15]
XV = 640
SCRATCH = {}
for _n, _p, _w, _t in (
        ("NB", 128, 1024, I32), ("XI", 128, 8, I32), ("XJ", 128, 8, I32), ("DH", 128, 32, F32), ("TO", 128, 2064, B16), ("TO1", 128, 2064, B16), ("TO2", 128, 2048, B16),
        ("TP0", 128, 2048, B16), ("TPn", 128, 2048, B16), ("TP1", 128, 2048, B16), ("EL0", 128, 2048, H16), ("ELn", 128, 2048, H16),
        ("ST", 128, 32, I32), ("SU", 128, 32, U16), ("STH", 128, 32, H16), ("TH", 128, 1, I32),
        ("THF", 128, 1, F32), ("Q", 128, 256, B16), ("QR", 128, 4096, B16), ("QZ", 128, 2048, B16), ("ON", 128, 512, B16), ("CB", 128, 2144, B16),
        ("SI", 128, 640, B16), ("CG", 128, 384, B16), ("CF", 17, 384, B16), ("CW", 17, 1152, H16), ("CC", 128, 32, F32), ("C9", 128, 512, B16),
        ("VH", 16, 1024, B16), ("SELL", 128, 2048, B16), ("S8", 128, 8, B16), ("RS", 128, 16, F32),
        ("CR", 33, 256, B16), ("RT", 97, 2560, B16), ("IO", 128, 128, B16), ("DF", 128, 130, F32), ("IX", 1, 800, B16),
        ("NT", 17, 1792, H16), ("MZ", 128, 128, F32), ("TZ", 128, 128, I32), ("BZ", 128, 128, I32), ("OZ", 128, 256, U16), ("BQZ", 128, 256, B16),
        ("NZ", 128, 256, H16), ("PT0", 128, 176, H16), ("PT1", 128, 176, H16), ("NP0", 128, 128, H16), ("NP1", 128, 128, H16),
        ("DZ", 128, 128, F32), ("U", 128, 176, F32), ("PR", 128, 144, F32), ("V5", 128, 144, F32), ("PX", 128, 176, F32), ("DX", 128, 160, F32),
        ("TT", 128, 160, I32), ("HH", 128, 160, I32), ("JA", 128, 400, B16), ("JD", 128, 400, B16), ("JC", 128, 400, B16),
        ("JI", 128, 80, I32), ("JS", 128, 96, F32), ("IL", 128, 32, H16), ("NM", 128, 160, F32), ("JP", 128, 192, H16),
        ("WX", 128, 160, I32), ("WS", 128, 160, B16), ("HV", 128, 160, H16), ("HT", 97, 256, H16), ("HY", 128, 16, B16), ("OFR", 128, 160, U16),
        ("XR", 128, 2560, B16), ("CMP", 128, 256, B16), ("OH", 128, 10240, B16), ("TL", 128, 5120, B16), ("C3", 128, 264, F32),
        ("MKT", 128, 128, B16), ("MKP", 128, 128, B16), ("AT", 96, 128, H16), ("LT", 16, 256, B16),
        ("NE", 16, 256, B16), ("YK", 128, 1536, B16), ("YB", 128, 1280, H16), ("YR", 128, 256, F32)):
    SCRATCH[_n] = ("sbuf", [_p, _w], _t)
for _c in "01":
    for _n, _w, _t in (("NN", 256, H16), ("M", 256, F32), ("T", 256, I32), ("B", 256, I32), ("OF", 256, U16), ("DV", 2560, B16),
                       ("AB", 4096, B16), ("XG", 2048, B16), ("BQ", 1280, B16), ("D", 256, F32), ("SC", 256, I32),
                       ("K", 32, I32), ("L", 32, I32), ("R", 16, I32), ("VL", 16, U16)):
        SCRATCH[_n + _c] = ("sbuf", [128, _w], _t)
BANKS = ("kA", "kB", "wA", "wB", "xA", "xB", "dA", "dB")
for _b in BANKS:
    SCRATCH[_b] = ("psum", [128, 512], F32)
NITEM = 7
NDMA = 17
SEMAPHORES = ["v", "s", "t", "gc", "aTP0", "aTPn", "aMK"] + ["d%d" % i for i in range(NDMA)]
SEMAPHORES += ["ri%d" % i for i in range(NITEM)] + ["lo%d" % i for i in range(NITEM)]

PLAN = dict(cy=0.00100, tcy=0.00075, gat=1.5, wake=0.12, same=0.05, tp0=12.0, mk=7.0, turns=900, shake=0.5, wide=10.0)
OTHERS = [dict(gat=1.0, far=0.0), dict(gat=0.8, t=1.15, far=0.3), dict(gat=1.25, t=0.85, far=-0.3)]
LEADS = [5.0, 5.5, 6.0, 6.5]
ORDERS = {}


def items(x, T, topo):
    me = T.cores[x]
    n = len(T.cores)

    def via(dst, other):
        if not other and topo.may_write(me, dst):
            return None
        for c in topo.cores_of(me):
            if c != me and topo.may_write(c, dst) and (topo.die(c) != topo.die(me)) == bool(other):
                return c
        for c in topo.cores_of(me):
            if c != me and topo.may_write(c, dst):
                return c
        return None
    out = []
    d0, d1 = T.cores[(x - 1) % n], T.cores[(x - 2) % n]
    for h, c0 in ((0, 0), (1, 1024), (0, 512), (1, 1536)):
        out.append(("TO", c0, c0 + 512, "TP0", "aTP0", d0, via(d0, h)))
    for h in (0, 1):
        out.append(("TO", h * 1024, h * 1024 + 1024, "TPn", "aTPn", d1, via(d1, h)))
    out.append(("MKT", 0, 128, "MKP", "aMK", d1, via(d1, 0)))
    return out


def remote(g, T, topo, core, dst, out, src, rsem, lsem):
    rid, pid = topo.addr(dst, core)
    g.remote_dma(out, src, T.sem[rsem], T.sem[lsem], pid, rid, topo.mask(core, dst))


def hand_on(g, core, T, topo):
    todo = []
    for x in range(len(T.cores)):
        for k, it in enumerate(items(x, T, topo)):
            if it[6] == core:
                todo.append((k, it, len(topo.engines(T.cores[x], core))))
    for k, it, ne in todo:
        g.wait_ge(T.sem["ri%d" % k], ne)
        ap = T[it[3]][:, it[1]:it[2]]
        remote(g, T, topo, core, it[5], ap, ap, it[4], "lo%d" % k)
    for k, it, ne in todo:
        g.wait_ge(T.sem["lo%d" % k], len(topo.engines(core, it[5])))


def build(g, core, T, topo):
    ops = []
    lastw, reads, bank = {}, {}, {}
    bon = [0.0, False]
    CY, TCY, GAT = PLAN["cy"], PLAN["tcy"], PLAN["gat"]

    same = {"hI": "cI", "hPV": "cPV", "hP0": "cP0", "w03": "cE0", "wE": "cEB", "hAB": "cAB"}

    def op(q, fn, R, W, cost, kind="c", sem=None, val=1, lat=0.0):
        n = len(ops)
        R = [same.get(k, k) for k in R]
        deps, order = set(), set()
        for k in list(R) + list(W):
            if k[0] == "#":
                b = bank.setdefault(k, {})
                for e in b:
                    if e == q:
                        order.add(b[e][-1])
                    elif e != "last":
                        deps.update(b[e])
                b[q] = b[q] + [n] if b.get("last") == [q] and q != "t" else [n]
                b["last"] = [q]
        for k in R:
            if k[0] != "#":
                if k in lastw:
                    deps.add(lastw[k])
                reads.setdefault(k, []).append(n)
        for k in W:
            if k[0] != "#":
                if k in lastw:
                    deps.add(lastw[k])
                deps.update(reads.get(k, []))
                lastw[k] = n
                reads[k] = []
        deps.discard(n)
        order.discard(n)
        ops.append(dict(q=q, fn=fn, deps=deps, order=(order - deps if q == "t" else set()), cost=cost, lat=lat, kind=kind, sem=sem, val=val, bon=bon[0], gat=False))

    def V(fn, R, W, n):
        op("v", lambda: fn(g.vector), R, W, max(64, n) * CY + 0.03)

    def VG(fn, R, W, n):
        op("v", lambda: fn(g.vector), R, W, n * GAT * CY + 0.05)
        ops[-1]["gat"] = True

    def TS(out, a, s1, o0, R, W, n, s2=None, o1=None):
        if o1 is None:
            V(lambda e: e.tensor_scalar(out, a, s1, None, o0), R, W, n)
        else:
            V(lambda e: e.tensor_scalar(out, a, s1, s2, o0, o1), R, W, n)

    def TTo(out, a, b, o, R, W, n):
        V(lambda e: e.tensor_tensor(out, a, b, o), R, W, n)

    def CP(out, a, R, W, n):
        V(lambda e: e.tensor_copy(out, a), R, W, n)

    def fill(ap, c, R, W, n):
        V(lambda e: e.memset(ap, c), R, W, n)

    def S(out, a, f, R, W, n, **kw):
        first = 1.3 if f == FN.Sigmoid and not bon[1] else 0.0
        bon[1] = bon[1] or f == FN.Sigmoid
        op("s", lambda: g.scalar.activation(out, a, f, **kw), R, W, max(64, n) * CY + 0.05 + first)

    def SG(out, a, R, W, n):
        op("s", lambda: g.scalar.activation(out, a, FN.Copy), R, W, n * GAT * CY + 0.07)
        ops[-1]["gat"] = True

    def MM(out, l, r, st, sp, R, W, m, n):
        op("t", lambda: g.tensor.matmul(out, l, r, st, sp), R, W, max(min(64, m), n) * TCY + 0.01)

    def GC(fn, R, W, n):
        op("g", fn, R, W, 0.18 + 2 * n * CY)

    def iota(out, pat, base, cm, R, W, n):
        GC(lambda: g.iota(out, pat, base, cm, allow_small_or_imprecise_dtypes=True), R, W, n)

    def eqs(b, c0, pat, base, key, rows=128, src="ON"):
        n = 1
        for p in pat:
            n *= p[1]
        GC(lambda: g.affine_select(b[0:rows, c0:c0 + n], T[src][0:rows, 0:n], pat, OP.is_equal, 0.0, base, 1), [src if n <= 256 else src + "b"], [key], n)

    nd = [0]

    def DMA(q, out, a, R, W, lat=2.5):
        s = "d%d" % nd[0]
        nd[0] += 1
        eng = g.sync if q == "y" else g.scalar
        op(q, lambda: eng.dma_start(out, a), R, W, 0.06, "d", s, 16, lat)

    PS = {b: T[b] for b in BANKS}

    DMA("y", T.ST[:, :], T.st[:, :], [], ["ST"])
    for z, x in enumerate((0, 1024, 512, 1536)):
        DMA("s", T.TO[:, x:x + 512], T.ang[:, x:x + 512], [], ["TO%d" % x], 2.8 + 0.6 * z)
    op(None, None, ["TO%d" % x for x in range(0, 2048, 512)], ["TO"], 0.0, "n")
    DMA("y", T.NB[:, :], T.nb[:, :], [], ["NB"], 4.8)
    DMA("s", T.Q[:, :], T.q[:, :], [], ["Q"], 3.0)
    DMA("y", T.TH[:, :], T.th[:, :], [], ["TH"])

    CB, CH, CG, CF, CW, CC = T.CB, T.CB, T.CG, T.CF, T.CW, T.CC
    IB, I16, NEGI, BIGI, BIGP = CB[:, 8:136], CH[:, 8:136], CG[:, 0:128], CG[:, 128:256], CG[:, 256:384]
    PMV, PM0 = 144, 272
    fill(T.ON[:, 0:256], 1.0, [], ["ON"], 128)
    fill(T.NT[:, :], 1.0, [], ["NT%d" % s for s in range(14)], 896)
    eqs(CB, 0, [[-1, 144]], 8, "cI")
    eqs(CB, PMV, [[-2, 8], [-1, 2], [-16, 8]], 0, "cPV")
    eqs(CB, PM0, [[-8, 2], [-16, 8], [-1, 8]], 0, "cP0")
    eqs(CF, 0, [[-1, 8], [-8, 2], [0, 8]], 0, "cE0", 17)
    eqs(CF, 128, [[-8, 2], [-1, 8], [0, 16]], 0, "cEB", 17)
    GC(lambda: g.iota(T.XI[:, 0:8], [[-16, 8]], 0, 1), [], ["XI"], 8)
    iota(T.CR[:, :], [[0, 32], [1024, 8]], 0, 0, [], ["CR"], 256)
    iota(T.RS[:, :], [[2048, 16]], REST, 0, [], ["RS"], 16)
    CP(T.STH[:, :], T.ST[:, :], ["ST"], ["STH"], 64)
    CP(T.SU[:, :], T.ST[:, :], ["ST"], ["SU"], 64)
    for z in (0, 1):
        V(lambda e, z=z: e.tensor_reduce(CC[:, z:z + 1], CB[:, PM0 + 64 * z:PM0 + 64 * z + 64], AxisListType.X, OP.add), ["cP0"], ["cR%d" % z], 64)
    for c in (0, 1):
        for b in (0, 1):
            x = 8 + 8 * (c - b)
            TS(CH[:, 400 + (2 * c + b) * 128:528 + (2 * c + b) * 128], CH[:, x:x + 128], CC[:, c:c + 1], OP.mult, ["hI", "cR%d" % c], ["hP4%d%d" % (c, b)], 64)
    TS(CC[0:17, 2:3], CB[0:17, 24:25], 0.5, OP.mult, ["cI"], ["cH"], 64)
    TS(CC[0:17, 3:4], CB[0:17, 24:25], 1.0 / 594.0, OP.mult, ["cI"], ["cH2"], 64)
    TS(CW[:, 0:128], CF[:, 0:128], CC[0:17, 2:3], OP.add, ["cE0", "cH"], ["w01"], 64, 4.0, OP.mult)
    TS(CW[:, 128:256], CF[:, 0:128], CC[0:17, 3:4], OP.add, ["cE0", "cH2"], ["w02"], 64, 594.0, OP.mult)
    TS(CW[:, 384:640], CF[:, 128:384], CC[0:17, 2:3], OP.add, ["cEB", "cH"], ["wP"], 128, 4.0, OP.mult)
    TS(CW[:, 640:896], CF[:, 128:384], CC[0:17, 2:3], OP.add, ["cEB", "cH"], ["wQ"], 128, 2.0, OP.mult)
    TS(CW[:, 896:1152], CF[:, 128:384], 592.0, OP.mult, ["cEB"], ["wV"], 128)
    TS(T.XJ[:, 0:8], T.XI[:, 0:8], 4, OP.arith_shift_right, ["XI"], ["XJ"], 64)
    TS(T.S8[:, :], T.XJ[:, 0:8], 0.0, OP.is_equal, ["XJ"], ["S8"], 64, 8192.0, OP.mult)
    fill(T.CR[0:32, :], 0.0, ["CR"], ["CR"], 128)
    fill(T.CR[0:1, :], -16711680.0, ["CR"], ["CR"], 128)
    S(NEGI, IB, FN.Copy, ["cI"], ["NEGI"], 128, scale=-1.0)
    S(BIGI, IB, FN.Copy, ["cI"], ["BIGI"], 128, scale=BIG)
    S(BIGP, CB[:, PM0:PM0 + 128], FN.Copy, ["cP0"], ["BIGP"], 128, scale=BIG)
    S(T.DZ[:, :], T.ON[:, 0:128], FN.Copy, ["ON"], ["DZ"], 128, scale=-BIG)
    for c in "01":
        S(T["D" + c][:, :], T.ON[:, 0:256], FN.Copy, ["ON"], ["D" + c], 256, scale=-BIG)
        S(T["D" + c][:, 8::16], T.RS[:, :], FN.Copy, ["RS", "D" + c], ["D" + c], 64, bias=2047.0)
    fill(T.DH[:, 0::2], BIG, [], ["DH0"], 64)
    fill(T.DH[:, 1::2], -1024.0, [], ["DH1"], 64)
    QZ, QA = ["QZ%d" % k for k in range(8)], ["QR%d" % k for k in range(32)]
    for k in range(8):
        if k % 2:
            CP(T.QZ[:, k::8], T.Q[:, :], ["Q"], [QZ[k]], 128)
        else:
            S(T.QZ[:, k::8], T.Q[:, :], FN.Copy, ["Q"], [QZ[k]], 256)
    for b in (0, 1):
        for k in range(16):
            o, i = T.QR[:, b * 2048 + k:b * 2048 + 2048:16], T.Q[:, b::2]
            if k % 3:
                CP(o, i, ["Q"], [QA[b * 16 + k]], 64)
            else:
                S(o, i, FN.Copy, ["Q"], [QA[b * 16 + k]], 128)
    for h, bn in ((0, "wB"), (1, "kB")):
        for z in range(4):
            x = PMV + (h * 4 + z) * 16
            MM(PS[bn][0:16, z * 128:z * 128 + 128], CH[:, x:x + 16], I16, True, True, ["hPV", "hI"], ["#" + bn], 16, 128)
        S(T.VH[:, h * 512:h * 512 + 512], PS[bn][0:16, :], FN.Copy, ["#" + bn], ["VH%d" % h], 512)

    PR1, PR2, PTZ, PAB, I64 = 912, 1040, 1168, 1680, 2064
    I2, I592, I4K, NI4K = 0, 128, 256, 384
    RTK, SLK = ["RT%d" % z for z in range(7)], ["SELL%d" % z for z in range(4)]

    def ring_constants():
        fill(T.ON[:, 256:512], 1.0, ["ON"], ["ONb"], 128)
        S(T.C9[:, :], T.ON[:, :], FN.Copy, ["ONb"], ["C9b"], 512, scale=1024.0)
        fill(T.TO[:, 2048:2064], 0.0, [], ["TOz"], 64)
        fill(T.TO1[:, 2048:2064], 0.0, [], ["TO1z"], 64)
        iota(T.IO[:, :], [[127, 2], [1, 64]], 1, 0, [], ["IO"], 128)
        eqs(CB, PR1, [[-1, 8], [-16, 8], [-8, 2]], 0, "cR1", 80)
        eqs(CB, PR2, [[-1, 8], [-16, 8], [-8, 2]], 80, "cR2", 80)
        for z in range(4):
            eqs(CB, PTZ + z * 128, [[-1, 8], [1000, 4], [-8, 4]], -48 - 1000 * z, "cZ%d" % z, 80)
        eqs(CB, PAB, [[-8, 2], [-1, 8], [-16, 16]], 0, "cAB", 96)
        DF = T.DF
        fill(CB[:, I64:I64 + 66:65], 0.0, [], ["c64z"], 64)
        TTo(CB[:, I64 + 1:I64 + 65], CB[:, 8:72], CB[:, 72:136], OP.subtract, ["cI"], ["c64"], 128)
        TTo(DF[:, 0:64], CB[:, I64 + 2:I64 + 66], CB[:, I64:I64 + 64], OP.add, ["c64", "c64z"], ["cDM"], 128)
        S(DF[:, 64:128], CB[:, I64 + 1:I64 + 65], FN.Copy, ["c64"], ["cND"], 64, scale=-2.0)
        TTo(DF[:, 0:64], DF[:, 0:64], DF[:, 64:128], OP.add, ["cDM", "cND"], ["cDM"], 128)
        TS(DF[:, 128:129], CB[:, 72:73], -127.0 / 128, OP.mult, ["cI"], ["cD0"], 64, CB[:, 8:9], OP.add)
        TS(DF[:, 129:130], CB[:, 71:72], 65.0 / 64, OP.mult, ["cI"], ["cD1"], 64, CB[:, 135:136], OP.subtract)
        TTo(DF[:, 0:64:63], DF[:, 0:64:63], DF[:, 128:130], OP.add, ["cDM", "cD0", "cD1"], ["cDM"], 64)
        S(DF[:, 64:128], DF[:, 0:64], FN.Copy, ["cDM"], ["cND"], 64, scale=-1.0)
        for z in range(6):
            eqs(T.RT, z * 480, [[-1, 3 if z < 5 else 1], [0, 32], [-16, 5]], -3 * z, RTK[z], 96, "ON")
        for z in range(16):
            iota(T.RT[96:97, z * 160:z * 160 + 160], [[64, 2], [-128, 16], [0, 5]], -128, 0, [RTK[6]], [RTK[6]], 160)
        for z in range(4):
            eqs(T.SELL, z * 512, [[-8, 4], [-1, 8], [0, 16]], -32 * z, SLK[z], 128, "C9")
        iota(T.IX[0:1, 0:400], [[0, 16], [8, 5], [1, 5]], 9, 0, [], ["IX"], 400)
        fill(T.IX[0:1, 0:400:25], 64.0, ["IX"], ["IX"], 64)
        fill(T.JD[:, :], 0.0, [], ["JD"], 200)
        fill(T.JD[:, 0::25], 64.0, ["JD"], ["JD"], 64)
        for x, f in ((I2, 2.0), (I592, 592.0), (I4K, 4096.0), (NI4K, -4096.0)):
            S(T.SI[:, x:x + 128], I16, FN.Copy, ["hI"], ["SI%d" % x], 128, scale=f)
        TS(T.THF[:, :], T.TH[:, :], -200.0, OP.mult, ["TH"], ["THF"], 64, 100.0, OP.add)
        fill(T.HT[64:96, :], 0.0, [], ["HTz"], 128)
        fill(T.HT[96:97, :], 1.0, ["HTz"], ["HTz"], 128)
        S(T.C3[:, 0:264], T.ON[:, 0:264], FN.Copy, ["ONb"], ["C30", "C31"], 264, scale=0.0)
        fill(CC[:, 4:5], -100.0, [], ["c100"], 64)
        fill(CC[:, 6:7], 0.5, [], ["c05"], 64)
        iota(CC[:, 16:32], [[0, 8], [127, 2]], 1, 0, [], ["cP"], 16)
        S(T.NE[:, :], CF[0:16, 128:384], FN.Copy, ["cEB"], ["NE"], 256, scale=-1.0)
        GC(lambda: g.iota(T.JI[:, 48:56], [[0, 8]], 0, 1), [], ["cm"], 8)
        TS(T.JI[:, 56:64], T.JI[:, 48:56], 15, OP.bitwise_and, ["cm"], ["cm2"], 64)
        TS(CC[:, 8:9], T.JI[:, 56:57], -200.0, OP.mult, ["cm2"], ["cM0"], 64, 100.0, OP.add)
        for j in range(1, 5):
            S(CC[:, 8 + j:9 + j], CC[:, 8:9], FN.Copy, ["cM0"], ["cM%d" % j], 64, bias=-200.0 * j)
        S(CC[:, 13:14], CC[:, 8:9], FN.Copy, ["cM0"], ["cM5"], 64, bias=-900.0, scale=8.0)

    n = len(T.cores)
    r = T.rank_of(core)
    its = items(r, T, topo)

    def send(k, after=()):
        buf, c0, c1, land, asem, dst, rel = its[k]

        def fn():
            if rel is None:
                remote(g, T, topo, core, dst, T[land][:, c0:c1], T[buf][:, c0:c1], asem, "lo%d" % k)
            else:
                remote(g, T, topo, core, rel, T[land][:, c0:c1], T[buf][:, c0:c1], "ri%d" % k, "lo%d" % k)
        op("g", fn, [buf + str(c0) if k < 4 else buf] + list(after), ["sent%d" % k], 0.5 if k else 2.5, "r", "lo%d" % k, len(topo.engines(core, dst if rel is None else rel)))

    def arrive(land, asem, giver, lat, after):
        tot = 0
        for it in items(giver, T, topo):
            if it[4] == asem:
                tot += len(topo.engines(T.cores[giver] if it[6] is None else it[6], core))
        op(None, None, after, [land], 0.0, "x", asem, tot, lat)
    for k in range(4):
        send(k)
    arrive("TP0", "aTP0", (r + 1) % n, PLAN["tp0"], ["sent%d" % k for k in range(4)])

    NB = T.NB[:, 0:1024]

    def nt(t, c, a):
        return t if a == 0 else (1 + a if c == 0 else 5 + a + 4 * t)

    def NTs(s, rows=17):
        return T.NT[0:rows, s * 128:s * 128 + 128]

    def offsets(C, out, ok, w):
        TS(T["B" + C][:, 0:w], T["T" + C][:, 0:w], 4, OP.arith_shift_right, ["T" + C], ["B" + C], w, 2047, OP.bitwise_and)
        CP(out, T["B" + C][:, 0:w], ["B" + C], [ok], w)

    def start(t, banks):
        P = "PT%d" % t
        X, XB = PS[banks[0]], "#" + banks[0]
        for z in range(8):
            MM(X[0:16, z:128:8], CH[:, PMV + z * 16:PMV + z * 16 + 16], T.STH[:, t * 16:t * 16 + 16], True, True, ["hPV", "STH"], [XB], 16, 16)
        CP(NTs(t, 16), X[0:16, 0:128], [XB], ["NT%d" % t], 128)
        MM(X[:, 128:144], NTs(t, 16), CH[0:16, 8:24], True, True, ["NT%d" % t, "hI"], [XB], 128, 16)
        CP(T[P][:, 80:96], X[:, 128:144], [XB], [P + "s5"], 64)
        TTo(T.DZ[:, 0::8], T[P][:, 80:96], T.RS[:, :], OP.add, [P + "s5", "RS", "DZ"], ["DZ"], 64)
        VG(lambda e: e.tensor_copy(T.NZ[:, :], NB.indirect(T.SU[:, t * 16:t * 16 + 16])), ["NB", "SU"], ["NZ"], 256)
        for c, bn in enumerate(banks):
            C, X = str(c), PS[bn]
            bon[0] = 1.0 - c
            for b in (0, 1):
                x = 400 + (2 * c + b) * 128
                MM(X[:, 0:128], CH[:, x:x + 128], T.NZ[:, b::2], b == 0, b == 1, ["hP4%d%d" % (c, b), "NZ"], ["#" + bn], 128, 128)
            for z in range(3):
                MM(X[:, 128 + z * 128:256 + z * 128], CW[:, z * 128:z * 128 + 128] if z < 2 else CF[:, 0:128], NTs(t), True, True, ["w0%d" % (z + 1), "NT%d" % t], ["#" + bn], 128, 128)
            np_ = T["NP" + C][:, :]
            CP(np_, X[:, 0:128], ["#" + bn], ["NP" + C], 128)
            TTo(T.MZ[:, :], np_, X[:, 128:256], OP.mult, ["NP" + C, "#" + bn], ["MZ"], 128)
            TTo(T.TZ[:, :], T.MZ[:, :], X[:, 256:384], OP.add, ["MZ", "#" + bn], ["TZ"], 128)
            TTo(T.BQZ[:, c * 128:c * 128 + 128], np_, X[:, 384:512], OP.is_equal, ["NP" + C, "#" + bn], ["BQZ" + C], 128)
            offsets("Z", T.OZ[:, c * 128:c * 128 + 128], "OZ" + C, 128)
        bon[0] = 0.0

    def step(t, c, a, tab, tkey):
        C = str(c)
        P = "PT%d" % t
        bon[0] = 1.0 - c
        kb, wb, xb, db = ("kA", "wA", "xA", "dA") if c == 0 else ("kB", "wB", "xB", "dB")
        K, W, X, D = PS[kb], PS[wb], PS[xb], PS[db]
        KB, WB, XB, DB = "#" + kb, "#" + wb, "#" + xb, "#" + db
        nn, nnk = T["NN" + C], "NN" + C
        nv = NV[a]
        tot, qr, QK = (2048, T.QZ, QZ) if a == 0 else (4096, T.QR, QA)

        def sl(i):
            return 5 + i if c == 0 else 5 - i
        if a:
            VG(lambda e: e.tensor_copy(nn[:, :], NB.indirect(T["VL" + C][:, 0:16])), ["NB", "VL" + C], [nnk], 256)
            s0, s1 = nt(t, c, a - 1), nt(t, c, a)
            for b in (0, 1):
                y = b * 128
                MM(W[:, y:y + 128], CW[:, 384 + y:512 + y], NTs(s0), True, True, ["wP", "NT%d" % s0], [WB], 128, 128)
            for b in (0, 1):
                y = b * 128
                MM(W[:, 256 + y:384 + y], CW[:, 640 + y:768 + y], NTs(s0), True, False, ["wQ", "NT%d" % s0], [WB], 128, 128)
                MM(W[:, 256 + y:384 + y], CW[0:16, 896 + y:1024 + y], NTs(s1, 16), False, True, ["wV", "NT%d" % s1], [WB], 128, 128)
            for b in (0, 1):
                y = b * 128
                TTo(T["M" + C][:, y:y + 128], nn[:, b::2], W[:, y:y + 128], OP.mult, [nnk, WB], ["M%s%d" % (C, b)], 128)
            TTo(T["T" + C][:, :], T["M" + C][:, :], W[:, 256:512], OP.add, ["M%s0" % C, "M%s1" % C, WB], ["T" + C], 256)
            offsets(C, T["OF" + C][:, :], "OF" + C, 256)
        of, o0, ofk = (T.OZ, c * 128, "OZ" + C) if a == 0 else (T["OF" + C], 0, "OF" + C)
        win = tab[:, 0:2048]
        dv, ab, xg = T["DV" + C], T["AB" + C], T["XG" + C]
        parts = [(z, min(p1, z + 512), e) for p0, p1, e in ((nv, tot, "s"), (0, nv, "v")) for z in range(p0, p1, 512)]

        def keys(nm, p0, p1):
            return ["%s%s.%d" % (nm, C, z) for z in range(p0 // 128, (p1 + 127) // 128)]
        for p0, p1, e in parts:
            off = of[:, o0 + p0 // 16:o0 + p1 // 16]
            if e == "v":
                VG(lambda en, p0=p0, p1=p1, off=off: en.tensor_tensor(dv[:, p0:p1], win.indirect(off), qr[:, p0:p1], OP.subtract),
                   [ofk, tkey] + QK, keys("dv", p0, p1), p1 - p0)
            else:
                SG(xg[:, p0 - nv:p1 - nv], win.indirect(off), [ofk, tkey], keys("XG", p0 - nv, p1 - nv), p1 - p0)
        kw = tot // 16
        BQ = T["BQ" + C]
        if a == 1:
            for b in (0, 1):
                MM(K[:, 256 + b:512:2], CF[0:16, 128 + b * 128:256 + b * 128], NTs(t, 16), True, True, ["wE", "NT%d" % t], [KB], 128, 128)
        if a:
            TTo(BQ[:, 0:256], nn[:, :], K[:, 256:512], OP.is_equal, [nnk, KB], ["BQ%s0" % C], 256)
        MM(K[:, 0:kw], T.ON[0:33, 0:128], T.CR[:, 0:kw], True, False, ["ON", "CR"], [KB], 128, kw)
        if a == 0:
            MM(K[:, 0:128], T["NP" + C][:, :], CH[:, PM0:PM0 + 128], False, False, ["NP" + C, "hP0"], [KB], 128, 128)
            MM(K[:, 0:128], T.BQZ[:, c * 128:c * 128 + 128], BIGP, False, False, ["BQZ" + C, "BIGP"], [KB], 128, 128)
        else:
            for b in (0, 1):
                MM(K[:, b * 128:b * 128 + 128], nn[:, b::2], I16, False, False, [nnk, "hI"], [KB], 128, 128)
        for p0, p1, e in parts:
            if e == "v":
                S(ab[:, p0:p1], dv[:, p0:p1], FN.Abs, keys("dv", p0, p1), keys("ab", p0, p1), p1 - p0)
            else:
                w = p1 - p0
                MM(D[:, 0:w], IB, xg[:, p0 - nv:p1 - nv], True, False, ["cI"] + keys("XG", p0 - nv, p1 - nv), [DB], 128, w)
                MM(D[:, 0:w], NEGI, qr[:, p0:p1], False, True, ["NEGI"] + QK, [DB], 128, w)
                S(ab[:, p0:p1], D[:, 0:w], FN.Abs, [DB], keys("ab", p0, p1), w)

        def score(b, last):
            for k in range(8 if a == 0 else 16):
                if a == 0:
                    o, l, kk = K[:, b * 64 + k:b * 64 + 64:8], ab[:, b * 8 + k:2048:16], keys("ab", 0, 2048)
                else:
                    o, l, kk = K[:, b * 128 + k:b * 128 + 128:16], ab[:, b * 2048 + k:b * 2048 + 2048:16], keys("ab", b * 2048, b * 2048 + 2048)
                MM(o, l, T.S8[:, :], False, last and k == (7 if a == 0 else 15), kk + ["S8"], [KB], 128, 8)
        score(0, False)
        for j in range(a + 1 if a else 0):
            s = nt(t, c, j)
            x0, j0 = (j % 2) * 256, j * 256
            bk = "BQ%s%d" % (C, j)
            if j:
                for b in (0, 1):
                    MM(X[:, x0 + b:x0 + 256:2], CF[0:16, 128 + b * 128:256 + b * 128], NTs(s, 16), True, True, ["wE", "NT%d" % s], [XB], 128, 128)
                TTo(BQ[:, j0:j0 + 256], nn[:, :], X[:, x0:x0 + 256], OP.is_equal, [nnk, XB], [bk], 256)
            for b in (0, 1):
                MM(K[:, b * 128:b * 128 + 128], BQ[:, j0 + b:j0 + 256:2], BIGI, False, False, [bk, "BIGI"], [KB], 128, 128)
        score(1, True)
        SC, Kt, Lt, Rt = T["SC" + C], T["K" + C], T["L" + C], T["R" + C]
        dd, dk = (T.DZ, "DZ") if a == 0 else (T["D" + C], "D" + C)
        if a:
            TTo(dd[:, 0::16], T[P][:, sl(a) * 16:sl(a) * 16 + 16], T.RS[:, :], OP.add, [P + "s%d" % sl(a), "RS", dk], [dk], 64)
        V(lambda e: e.tensor_tensor_scan(SC[:, 0:kw], dd[:, 0:kw], K[:, 0:kw], -BIG, OP.max, OP.min), [dk, KB], ["SC" + C], kw)
        ns = sl(a + 1)
        out, ok = T[P][:, ns * 16:ns * 16 + 16], P + "s%d" % ns
        if a == 0:
            TS(Rt[:, :], SC[:, 7:kw:8], 1023, OP.bitwise_and, ["SC" + C], ["R" + C], 64)
        else:
            TS(Kt[:, :], SC[:, 7:kw:8], ~7168, OP.bitwise_and, ["SC" + C], ["K" + C], 64)
            V(lambda e: e.tensor_tensor_scan(Lt[:, :], T.DH[:, :], Kt[:, :], 0.0, OP.add, OP.min), ["DH0", "DH1", "K" + C], ["L" + C], 64)
            TS(Rt[:, :], Lt[:, 1::2], 1023, OP.bitwise_and, ["L" + C], ["R" + C], 64)
        CP(out, Rt[:, :], ["R" + C], [ok], 64)
        if a < 4:
            s = nt(t, c, a + 1)
            MM(X[0:16, 0:128], out, I16, True, True, [ok, "hI"], [XB], 16, 128)
            CP(NTs(s, 16), X[0:16, 0:128], [XB], ["NT%d" % s], 128)
            for i in range(8):
                MM(X[:, 256:272], T.VH[:, i * 128:i * 128 + 128], T.NT[0:16, s * 128 + i:s * 128 + 128:8], i == 0, i == 7,
                   ["VH%d" % (i // 4), "NT%d" % s], [XB], 128, 16)
            CP(T["VL" + C][:, :], X[:, 256:272], [XB], ["VL" + C], 64)
        bon[0] = 0.0

    def lesser(el, tab, tk):
        for h in range(4):
            y = h * 512
            TS(T[el][:, y:y + 512], tab[:, y:y + 512], 0.75, OP.mult, [tk], ["%s.%d" % (el, h)], 256, 1024.375, OP.add)

    def lessen(tab, tk, mk, el, out, okey, banks):
        for qd in range(4):
            b = banks[qd % len(banks)]
            B, ek, x = PS[b], "%s.%d" % (el, qd), qd * 512
            MM(B[:, :], IB, T[el][:, x:x + 512], True, False, ["cI", ek], ["#" + b], 128, 512)
            for z in range(4):
                tt = (qd * 4 + z) * 128
                MM(B[:, z * 128:z * 128 + 128], T.SELL[:, tt:tt + 128], T[mk][:, :], False, z == 3, [SLK[qd], mk], ["#" + b], 128, 128)
            TTo(out[:, x:x + 512], B[:, :], tab[:, x:x + 512], OP.min, ["#" + b, tk], ["%s%d" % (okey, qd)], 512)

    def hot(m0, m1, hk):
        c0, c1, kz = m0 * 16, m1 * 16, str(m0)
        TS(T.WX[:, c0:c1], T.HH[:, c0:c1], 63, OP.bitwise_and, hk, ["WW" + kz], c1 - c0)
        if c1 - c0 > 16:
            TS(T.WS[:, c0:c1:2], T.WX[:, c0:c1:2], 1.0, OP.add, ["WW" + kz], ["WS" + kz], (c1 - c0) // 2)
            TS(T.WS[:, c0 + 1:c1:2], T.WX[:, c0 + 1:c1:2], 128.0, OP.add, ["WW" + kz], ["WT" + kz], (c1 - c0) // 2)
        else:
            TTo(T.WS[:, c0:c1], T.WX[:, c0:c1], CC[:, 16:32], OP.add, ["WW" + kz, "cP"], ["WS" + kz, "WT" + kz], 64)
        for col in range(c0, c1, 2):
            TS(T.OH[:, col * 64:col * 64 + 128], T.IO[:, :], T.WS[:, col:col + 1], OP.max, ["IO", "WS" + kz, "WT" + kz],
               ["OH%d" % col, "OH%d" % (col + 1)], 64, T.WS[:, col + 1:col + 2], OP.min)

    def rings(t, tab, tk):
        P = "PT%d" % t
        pt, JS, SI = T[P], T.JS, T.SI
        pk = [P + "s%d" % i for i in range(11)]
        uk, hw = ["U%d" % i for i in range(3)], ["HHe", "HHx", "HHy"]

        def slot(s):
            return pt[:, s * 16:s * 16 + 16]
        for z, (c0, c1, kk) in enumerate(((16, 160, pk[1:10]), (0, 16, pk[0:1]), (160, 176, pk[10:11]))):
            TS(T.U[:, c0:c1], pt[:, c0:c1], 2.0, OP.mult, kk, [uk[z]], c1 - c0, 1.0, OP.add)
        for z, (c0, c1, kk, ku) in enumerate(((16, 128, pk[1:10], uk[0:1]), (0, 16, pk[0:3], uk[0:2]), (128, 144, pk[8:11], [uk[0], uk[2]]))):
            TTo(T.PR[:, c0:c1], T.U[:, c0:c1], T.U[:, c0 + 32:c1 + 32], OP.mult, ku, ["PR%d" % z], 2 * (c1 - c0))
            if z == 0:
                S(T.V5[:, :], T.U[:, 16:160], FN.Copy, uk[0:1], ["V5"], 144, bias=-296.0, scale=296.0)
            TTo(T.TT[:, c0:c1], T.PR[:, c0:c1], T.V5[:, c0:c1], OP.add, ["PR%d" % z, "V5"], ["TT%d" % z], 2 * (c1 - c0))
            TS(T.HH[:, c0:c1], T.TT[:, c0:c1], 4, OP.arith_shift_right, ["TT%d" % z], [hw[z]], c1 - c0, 2047, OP.bitwise_and)
        S(T.PX[:, 16:160], T.U[:, 16:160], FN.Copy, uk[0:1], ["PXa"], 144, scale=1.0 / 4096)
        S(T.PX[:, 160:176], T.U[:, 160:176], FN.Copy, uk[2:3], ["PXb"], 64, scale=1.0 / 4096)
        TTo(T.DX[:, 16:80], T.PX[:, 32:96], T.PX[:, 16:80], OP.subtract, ["PXa"], ["DXa"], 128)
        TTo(T.DX[:, 80:144], T.PX[:, 80:144], T.PX[:, 96:160], OP.subtract, ["PXa"], ["DXb"], 128)
        TTo(T.DX[:, 144:160], T.PX[:, 144:160], T.PX[:, 160:176], OP.subtract, ["PXa", "PXb"], ["DXc"], 64)
        hot(1, 8, hw[0:1])
        hot(8, 9, hw[2:3])
        hot(0, 1, hw[1:2])
        J = PS["wA"]
        MM(J[:, 0:400], T.ON[0:1, 0:128], T.IX[0:1, 0:400], True, False, ["ON", "IX"], ["#wA"], 128, 400)
        terms = [(i, j, s) for i in range(1, 6) for j in range(1, 6) for s in (5 + i, 5 - j) if i + j > 2]
        terms.sort(key=lambda x: (x[2] == 0, x[2] == 10))
        for z, (i, j, s) in enumerate(terms):
            x = I4K if s > 5 else NI4K
            MM(J[:, (i - 1) * 5 + j - 1:400:25], SI[:, x:x + 128], slot(s), False, z == len(terms) - 1, ["SI%d" % x, pk[s]], ["#wA"], 128, 16)
        S(T.JA[:, :], J[:, 0:400], FN.Abs, ["#wA"], ["JA"], 400)
        V(lambda e: e.tensor_tensor_scan(T.JC[:, :], T.JD[:, :], T.JA[:, :], 0.0, OP.max, OP.min), ["JD", "JA"], ["JC"], 200)
        JU, J0, JJ = T.JI[:, 0:16], T.JI[:, 16:32], T.JI[:, 32:48]
        CP(JU, T.JC[:, 24::25], ["JC"], ["JU"], 64)
        TS(J0, JU, 63, OP.bitwise_and, ["JU"], ["J0"], 64)
        TS(JJ, JU, 7, OP.bitwise_and, ["JU"], ["JJ"], 64)
        NM = T.NM
        for m in range(1, 5):
            TS(NM[:, (4 + m) * 16:(5 + m) * 16], J0, 8.0 * (m + 1), OP.is_lt, ["J0"], ["NM%d" % (4 + m)], 64, 2048.0, OP.mult)
        for m in range(1, 5):
            TS(NM[:, (4 - m) * 16:(5 - m) * 16], JJ, m + 1.0, OP.is_lt, ["JJ"], ["NM%d" % (4 - m)], 64, 2048.0, OP.mult)
        TS(NM[:, 64:80], J0, 8.0, OP.is_lt, ["J0"], ["NM4"], 64, 2048.0, OP.mult)
        nk = ["NM%d" % i for i in range(9)]
        TTo(T.JP[:, 0:64], NM[:, 80:144], T.DX[:, 80:144], OP.mult, nk[5:9] + ["DXb"], ["JP0"], 128)
        TTo(T.JP[:, 128:192], NM[:, 0:64], T.DX[:, 16:80], OP.mult, nk[0:4] + ["DXa"], ["JP2"], 128)
        TTo(T.JP[:, 64:128], NM[:, 80:144], T.DX[:, 96:160], OP.mult, nk[5:9] + ["DXb", "DXc"], ["JP1"], 128)
        J = PS["kA"]
        for z, s, x in ((0, 9, I2), (2, 1, I2), (1, 10, I592)):
            o = J[:, z * 16:z * 16 + 16]
            MM(o, SI[:, x:x + 128], slot(s), True, False, ["SI%d" % x, pk[s]], ["#kA"], 128, 16)
            if x == I2:
                MM(o, T.ON[0:1, 0:128], T.ON[0:1, 0:16], False, False, ["ON"], ["#kA"], 128, 16)
            for k in range(4):
                MM(o, SI[:, x:x + 128], T.JP[:, z * 64 + k * 16:z * 64 + k * 16 + 16], False, k == 3, ["SI%d" % x, "JP%d" % z], ["#kA"], 128, 16)
        UA, PJ = JS[:, 0:16], JS[:, 16:32]
        CP(UA, J[:, 0:16], ["#kA"], ["UA"], 64)
        TTo(PJ, UA, J[:, 32:48], OP.mult, ["UA", "#kA"], ["PJ"], 64)
        TTo(T.TT[:, 144:160], PJ, J[:, 16:32], OP.add, ["PJ", "#kA"], ["TTb"], 64)
        TS(T.HH[:, 144:160], T.TT[:, 144:160], 4, OP.arith_shift_right, ["TTb"], ["HHb"], 64, 2047, OP.bitwise_and)
        TTo(T.HV[:, 0:80], T.HH[:, 0:80], NM[:, 0:80], OP.max, hw[0:2] + nk[0:5], ["HVa"], 160)
        TTo(T.HV[:, 80:144], T.HH[:, 80:144], NM[:, 80:144], OP.max, [hw[0], hw[2]] + nk[5:9], ["HVb"], 128)
        TTo(T.HV[:, 144:160], T.HH[:, 144:160], NM[:, 64:80], OP.max, ["HHb", "NM4"], ["HVc"], 64)
        X, X2 = PS["xA"], PS["xB"]
        MM(X[0:80, 0:128], T.HV[:, 0:80], I16, True, True, ["HVa", "hI"], ["#xA"], 80, 128)
        CP(T.HT[0:80, 0:128], X[0:80, 0:128], ["#xA", "HTz"], ["HT0"], 128)
        MM(X[0:80, 128:256], T.HV[:, 80:160], I16, True, True, ["HVb", "HVc", "hI"], ["#xA"], 80, 128)
        CP(T.HT[0:80, 128:256], X[0:80, 128:256], ["#xA", "HTz"], ["HT1"], 128)
        MM(X2[:, 0:128], CH[0:80, PR1:PR1 + 128], T.HT[0:80, 0:128], True, False, ["cR1", "HT0"], ["#xB"], 128, 128)
        MM(X2[:, 0:128], CH[0:80, PR2:PR2 + 128], T.HT[0:80, 128:256], False, True, ["cR2", "HT1"], ["#xB"], 128, 128)
        for z in range(4):
            MM(X2[:, 128:160], CH[0:80, PTZ + z * 128:PTZ + z * 128 + 128], T.HT[0:80, 128 + z:256:4], z == 0, z == 3, ["cZ%d" % z, "HT1"], ["#xB"], 128, 32)
        CP(T.OFR[:, :], X2[:, 0:160], ["#xB"], ["OFR"], 160)
        win = tab[:, 0:2064]
        for h in (0, 1):
            for e, x0, ln in (("v", h * 1024, XV), ("s", h * 1024 + XV, 1024 - XV), ("s", 2048 + h * 256, 256)):
                xo, fo = T.XR[:, x0:x0 + ln], T.OFR[:, x0 // 16:(x0 + ln) // 16]
                if e == "s":
                    SG(xo, win.indirect(fo), ["OFR", tk, tk + "z"], ["XR%d" % x0], ln)
                else:
                    VG(lambda e, xo=xo, fo=fo: e.tensor_copy(xo, win.indirect(fo)), ["OFR", tk, tk + "z"], ["XR%d" % x0], ln)
        hot(9, 10, ["HHb"])
        B, W = PS["kB"], PS["wB"]
        for z, u in enumerate((0, 1, 8, 9, 2, 3, 10, 11, 4, 5, 12, 13, 6, 7, 14, 15)):
            bn, tl = ("wA", "kA")[z % 2], T.TL[:, u * 320:u * 320 + 320]
            for h in (0, 1):
                MM(PS[bn][:, h:320:2], T.HT[:, h * 128:h * 128 + 128], T.RT[:, u * 160:u * 160 + 160], True, True,
                   ["HT%d" % h, "HTz", RTK[u // 3], RTK[6]], ["#" + bn], 128, 160)
            if u in HIV:
                TS(tl, PS[bn][:, 0:320], -0.5, OP.is_le, ["#" + bn], ["TL%d" % u], 320)
            else:
                S(tl, PS[bn][:, 0:320], FN.Sigmoid, ["#" + bn, "c100"], ["TL%d" % u], 320, bias=CC[:, 4:5], scale=-200.0)
        for h in (0, 1):
            for b in (0, 1):
                for m in range(10):
                    x0 = h * 1024 if m < 8 else 2048 + h * 256
                    xs = T.XR[:, x0 + 2 * m + b:x0 + 1024:16] if m < 8 else T.XR[:, x0 + 2 * m - 16 + b:x0 + 256:4]
                    y = b * 128 + h * 64
                    MM(B[:, y:y + 64], IB, xs, m == 0, m == 9, ["cI", "XR%d" % x0] + (["XR%d" % (x0 + XV)] if m < 8 else []), ["#kB"], 128, 64)
        S(T.CMP[:, :], B[:, 0:256], FN.Sigmoid, ["#kB", "THF"], ["CMP"], 256, bias=T.THF[:, 0:1], scale=200.0)
        for b in (0, 1):
            MM(W[:, b * 8:b * 8 + 8], T.CMP[:, b * 128:b * 128 + 128], T.S8[:, :], True, True, ["CMP", "S8"], ["#wB"], 128, 8)
        TS(T.HY[:, 0:16], W[:, 0:16], 8.5 * 8192, OP.is_ge, ["#wB"], ["HY"], 64)
        cn = "xB"
        C = PS[cn]
        for gp in range(4):
            for b in (0, 1):
                for u in (b * 8 + 2 * gp, b * 8 + 2 * gp + 1):
                    tl = T.TL[:, u * 320:u * 320 + 320]
                    TS(tl, tl, T.HY[:, u:u + 1], OP.mult, ["TL%d" % u, "HY"], ["TL%d" % u], 160)
                for m in range(10):
                    col, l0 = m * 16 + b * 8 + 2 * gp, (b * 8 + 2 * gp) * 320
                    MM(C[:, gp:256:4], T.OH[:, col * 64:col * 64 + 128], T.TL[:, l0 + (m % 5) * 2 + m // 5:l0 + 640:10], m + b == 0, m + b == 10,
                       ["OH%d" % col, "OH%d" % (col + 1), "TL%d" % (col % 16), "TL%d" % (col % 16 + 1)], ["#" + cn], 128, 64)
        for h in (0, 1):
            S(T.C3[h * 64:h * 64 + 64, 8 + h:264:2], C[h * 64:h * 64 + 64, h * 128:h * 128 + 128], FN.Copy, ["#" + cn], ["C3%d" % h], 128)
        for x, p0, p1 in ((64, 8, 136), (0, 136, 0)):
            MM(W[:, x:x + 64], T.C3[:, p0:p0 + 128], T.DF[:, 0:64], True, False, ["C30", "C31", "cDM"], ["#wB"], 128, 256)
            MM(W[:, x:x + 64], T.C3[:, p1:p1 + 128], T.DF[:, 64:128], False, True, ["C30", "C31", "cND"], ["#wB"], 128, 256)
        S(T.MKT[:, :], W[:, 0:128], FN.Sign, ["#wB", "c05"], ["MKT"], 128, bias=CC[:, 6:7], scale=-1.0)

    def show(t, bn):
        P = "PT%d" % t
        pt, JS = T[P], T.JS
        D = E = PS[bn]
        DB = "#" + bn
        J0, JJ = T.JI[:, 16:32], T.JI[:, 32:48]
        YI = T.JI[:, 64:80]
        TS(YI, J0, 3, OP.arith_shift_right, ["J0"], ["YI"], 64)
        CP(T.IL[:, 0:16], J0, ["J0"], ["ILi"], 64)
        TTo(T.IL[:, 16:32], YI, JJ, OP.add, ["YI", "JJ"], ["ILl"], 64)
        MM(E[0:96, 0:128], pt[:, 80:176], I16, True, True, [P + "s%d" % i for i in range(5, 11)] + ["hI"], [DB], 96, 128)
        for z, k in ((0, "ILi"), (1, "ILl")):
            MM(D[0:16, 128 + z * 128:256 + z * 128], T.IL[:, z * 16:z * 16 + 16], I16, True, True, [k, "hI"], [DB], 16, 128)
        CP(T.AT[:, :], E[0:96, 0:128], [DB], ["AT"], 128)
        S(T.LT[:, :], D[0:16, 128:384], FN.Copy, [DB], ["LT"], 256)
        for b in (0, 1):
            eb = CF[0:16, 128 + b * 128:256 + b * 128]
            for z in (0, 1):
                MM(D[:, z * 256 + b:z * 256 + 256:2], eb, T.LT[:, z * 128:z * 128 + 128], True, True, ["wE", "LT"], [DB], 128, 128)
        YK = [T.YK[:, j * 256:j * 256 + 256] for j in range(6)]
        S(YK[0], D[:, 0:256], FN.Sigmoid, [DB, "cM5"], ["YK0"], 256, bias=CC[:, 13:14], scale=200.0)
        S(YK[5], D[:, 256:512], FN.Sigmoid, [DB, "cM1"], ["YK5"], 256, bias=CC[:, 9:10], scale=200.0)
        for b in (0, 1):
            MM(D[:, b:256:2], CF[0:16, 128 + b * 128:256 + b * 128], T.LT[:, 128:256], True, False, ["wE", "LT"], [DB], 128, 128)
            MM(D[:, b:256:2], T.SI[:, NI4K:NI4K + 128], T.YK[:, b:256:2], False, True, ["SI%d" % NI4K, "YK0"], [DB], 128, 128)
        for j in range(1, 5):
            S(YK[j], D[:, 0:256], FN.Sigmoid, [DB, "cM%d" % j], ["YK%d" % j], 256, bias=CC[:, 8 + j:9 + j], scale=200.0)
        for j0, js in ((0, (0, 1)), (2, (2, 3)), (4, (4,))):
            for j in js:
                x, s = (j - j0) * 256, nt(t, 1, j)
                for b in (0, 1):
                    if j:
                        MM(E[:, x + b:x + 256:2], CF[0:16, 128 + b * 128:256 + b * 128], NTs(s, 16), True, j == 1, ["wE", "NT%d" % s], [DB], 128, 128)
                        if j > 1:
                            MM(E[:, x + b:x + 256:2], T.NE[:, b * 128:b * 128 + 128], NTs(s - 1, 16), False, True, ["NE", "NT%d" % (s - 1)], [DB], 128, 128)
                    else:
                        MM(E[:, b:256:2], CH[0:96, PAB + b * 128:PAB + b * 128 + 128], T.AT[:, :], True, True, ["hAB", "AT"], [DB], 128, 128)
            for j in js:
                x = (j - j0) * 256
                TTo(T.YB[:, j * 256:256 + j * 256], YK[j], E[:, x:x + 256], OP.mult, ["YK%d" % j, DB], ["YB%d" % j], 256)
        for z in range(6):
            MM(D[:, 0:256], I16, T.YB[:, z * 256:z * 256 + 256] if z < 5 else YK[5], z == 0, z == 5, ["hI", "YB%d" % z if z < 5 else "YK5"], [DB], 128, 256)
        S(T.YR[:, :], D[:, 0:256], FN.Copy, [DB], ["YR"], 256, bias=-1.0)
        DMA("y", T.yr[:, t * 256:t * 256 + 256], T.YR[:, :], ["YR"], [])

    start(0, ("dA", "dB"))
    ring_constants()
    own = "EL0"
    lesser(own, T.TO, "TO")
    for k in (4, 5):
        send(k, ["TP0"])
    arrive("TPn", "aTPn", (r + 2) % n, 50.0, ["sent4", "sent5"])
    for a in range(5):
        step(0, 0, a, T.TO, "TO")
        step(0, 1, a, T.TP0, "TP0")
        if a == 1:
            start(1, ("wA", "wB"))
    lesser("ELn", T.TPn, "TPn")
    rings(0, T.TO, "TO")
    send(6)
    show(0, "kB")
    arrive("MKP", "aMK", (r + 2) % n, PLAN["mk"], ["sent6"])
    lessen(T.TO, "TO", "MKT", own, T.TO1, "T1q", ("dB", "dA", "xA", "wA"))
    op(None, None, ["T1q%d" % q for q in range(4)], ["TO1"], 0.0, "n")
    lessen(T.TPn, "TPn", "MKP", "ELn", T.TP1, "P1q", ("wB", "xB", "dB"))
    op(None, None, ["P1q%d" % q for q in range(4)], ["TP1"], 0.0, "n")
    for a in range(5):
        step(1, 0, a, T.TO1, "TO1")
        step(1, 1, a, T.TP1, "TP1")
    lesser(own, T.TO1, "TO1")
    rings(1, T.TO1, "TO1")
    show(1, "kB")
    lessen(T.TO1, "TO1", "MKT", own, T.TO2, "T2q", ("dB", "dA", "xA", "wA"))
    for qd in range(4):
        DMA("y" if qd % 2 == 0 else "s", T.ye[:, qd * 512:qd * 512 + 512], T.TO2[:, qd * 512:qd * 512 + 512], ["T2q%d" % qd], [])
    for o in ops:
        more = set()
        for d in o["deps"]:
            if ops[d]["kind"] == "n":
                more |= ops[d]["deps"]
            else:
                more.add(d)
        o["deps"] = more
    return ops


def place(ops, pred, rank, way):
    n = len(ops)
    for i in way:
        for d, lag in pred[i]:
            if rank[d] >= rank[i]:
                rank[i] = rank[d] + 1e-7
    start, seq, busy = [0.0] * n, [0] * n, {q: [] for q in "vstgy"}
    for k, i in enumerate(sorted(way, key=lambda i: rank[i])):
        q, c = ops[i]
        s = 0.0
        for d, lag in pred[i]:
            if start[d] + lag > s:
                s = start[d] + lag
        if q is not None:
            b = busy[q]
            lo, hi = 0, len(b)
            while lo < hi:
                m = (lo + hi) // 2
                if b[m][1] <= s:
                    lo = m + 1
                else:
                    hi = m
            while lo < len(b) and b[lo][0] < s + c:
                s = max(s, b[lo][1])
                lo += 1
            if lo > 0 and b[lo - 1][1] >= s - 1e-9:
                b[lo - 1][1] = s + c
                if lo < len(b) and b[lo][0] <= s + c + 1e-9:
                    b[lo - 1][1] = b[lo][1]
                    del b[lo]
            elif lo < len(b) and b[lo][0] <= s + c + 1e-9:
                b[lo][0] = s
            else:
                b.insert(lo, [s, s + c])
        start[i], seq[i] = s, k
    return start, seq


def schedule(ops):
    n = len(ops)
    full = [o["cost"] + o["lat"] for o in ops]
    fwd, back = [[] for _ in range(n)], [[] for _ in range(n)]
    for i, o in enumerate(ops):
        for d in o["deps"]:
            w = PLAN["wake"] if ops[d]["q"] != o["q"] else PLAN["same"]
            fwd[i].append((d, full[d] + w))
            back[d].append((i, o["cost"] + w + ops[d]["lat"]))
        for d in o["order"]:
            fwd[i].append((d, ops[d]["cost"]))
            back[d].append((i, o["cost"]))
    way = [0.0] * n
    for i in range(n - 1, -1, -1):
        way[i] = max([way[j] + lag - ops[j]["cost"] for j, lag in back[i]] + [ops[i]["lat"]]) + ops[i]["cost"]
    qc, up, down = [(o["q"], o["cost"]) for o in ops], list(range(n)), list(range(n - 1, -1, -1))
    waits = [[(d, ops[d]["lat"] + (PLAN["wake"] if ops[d]["q"] != o["q"] else PLAN["same"])) for d in o["deps"]] for o in ops]
    costs = [[o["lat"] * f["far"] if o["kind"] == "x" else o["cost"] * f.get(o["q"], 1.0) * (f["gat"] if o["gat"] else 1.0) for o in ops] for f in OTHERS]

    def lasts(order, cost):
        fin, free = [0.0] * n, {q: 0.0 for q in "vstgy"}
        free[None] = 0.0
        for i in order:
            q = qc[i][0]
            s = free[q]
            for d, w in waits[i]:
                if fin[d] + w > s:
                    s = fin[d] + w
            fin[i] = s + cost[i]
            if q:
                free[q] = fin[i]
        return max(fin[i] + ops[i]["lat"] for i in order[-200:])

    def rnd():
        seed[0] = (seed[0] * 1103515245 + 12345) % 2147483648
        return seed[0] / 2147483648.0

    def turn(start, shake, z):
        t0, w = rnd() * max(start), PLAN["wide"] * (0.3 + rnd())
        e = [shake * rnd() if abs(start[i] - t0) < w else 0.0 for i in range(n)]
        if z % 3 == 2:
            rank = [start[i] + e[i] for i in range(n)]
        else:
            rs, _ = place(qc, back, [-(start[i] + full[i]) + e[i] * (1 - z % 3) for i in range(n)], down)
            rank = [-(rs[i] + ops[i]["cost"]) + e[i] * (z % 3) for i in range(n)]
        start, seq = place(qc, fwd, rank, up)
        order = sorted(range(n), key=lambda i: (start[i], seq[i]))
        end = sum(lasts(order, f) for f in costs) / len(costs)
        ORDERS.setdefault("ends", []).append(end)
        return end, start, seq
    seed = [1]
    best = min(turn(place(qc, fwd, [-way[i] - lead * ops[i]["bon"] for i in range(n)], up)[0], 0.0, 0) for lead in LEADS)
    for z in range(PLAN["turns"]):
        best = min(best, turn(best[1], PLAN["shake"] * (0.5, 1.0, 2.0, 4.0)[z % 4], z))
    return sorted(range(n), key=lambda i: (best[1][i], best[2][i]))


def emit(g, T, ops, order):
    eng = {"v": g.vector, "s": g.scalar, "t": g.tensor, "g": g, "y": g.sync}
    csem = {"v": "v", "s": "s", "t": "t", "g": "gc"}
    count, final = {}, {}
    know = {q: {} for q in eng}
    mark = [None] * len(ops)
    after = [None] * len(ops)
    for i in order:
        o = ops[i]
        q = o["q"]
        if o["kind"] == "n":
            continue
        if o["kind"] == "x":
            mark[i] = (o["sem"], o["val"])
            after[i] = {o["sem"]: o["val"]}
            final[o["sem"]] = o["val"]
            continue
        K = know[q]
        for d in sorted(o["deps"], key=lambda d: -sum(after[d].values())):
            s, v = mark[d]
            if K.get(s, 0) >= v:
                continue
            eng[q].wait_ge(T.sem[s], v)
            for s2, v2 in after[d].items():
                if K.get(s2, 0) < v2:
                    K[s2] = v2
        if q == "g" and o["kind"] == "c" and K.get("gc", 0) < count.get("gc", 0):
            g.wait_ge(T.sem["gc"], count["gc"])
            K["gc"] = count["gc"]
        ins = o["fn"]()
        if o["kind"] == "c":
            s = csem[q]
            count[s] = count.get(s, 0) + 1
            ins.then_inc(T.sem[s], 1)
            mark[i] = (s, count[s])
        elif o["kind"] == "d":
            ins.then_inc(T.sem[o["sem"]], 16)
            count[o["sem"]] = count.get(o["sem"], 0) + 16
            mark[i] = (o["sem"], count[o["sem"]])
        else:
            mark[i] = (o["sem"], o["val"])
        final[mark[i][0]] = mark[i][1]
        after[i] = dict(K)
        after[i][mark[i][0]] = mark[i][1]
    for s in final:
        if know["g"].get(s, 0) < final[s]:
            g.wait_ge(T.sem[s], final[s])


def rank_program(g, core, T, topo):
    if T.rank_of(core) is None:
        hand_on(g, core, T, topo)
        return
    ops = build(g, core, T, topo)
    if "order" not in ORDERS:
        ORDERS["order"] = schedule(ops)
    emit(g, T, ops, ORDERS["order"])
